import numpy as np, ml_dtypes
CORES = [10,34,74,98]
N = 4
BF = ml_dtypes.bfloat16
def gentries(a):
    return np.ascontiguousarray(a.reshape(8, 16, -1).transpose(0, 2, 1)).reshape(8, -1)
def gtable(e):
    e = np.asarray(e); return np.ascontiguousarray(e.reshape(8, -1, 16).transpose(0, 2, 1)).reshape(128, -1).astype(np.int32)
M, MB, Q, BASE, L, LA, T, C = 4096, 12, 2048, 1792, 256, 128, 4, 12
def boxes(rng):
    c = rng.integers(-255, 256, (2, N, 8, 8, M))
    return np.concatenate([np.minimum(c[0], c[1]), -np.maximum(c[0], c[1])], axis=2)
def tags(rng):
    u = rng.integers(0, 20, (N, 8, 16, BASE))
    return (u >= 8).astype(np.int64) + (u >= 15)
def grow(rng, fill):
    tag = tags(rng); name = np.where(tag == 0, rng.integers(1, M, tag.shape), rng.integers(1, BASE, tag.shape))
    return np.where(rng.random(tag.shape) < fill, name + M * tag, 0)
def starts(rng):
    v = rng.integers(1, BASE, (N, 8, T, L)); few = rng.integers(1, BASE, (N, 8, T, 12))
    return np.where(rng.random(v.shape) < 0.3, np.take_along_axis(few, rng.integers(0, 12, v.shape), 3), v)
def pack(R, e, x, v):
    return {"rg": R.reshape(N, 128, M).astype(np.float32).astype(BF), "nd": np.ascontiguousarray(e.reshape(N, 128, BASE)).astype(np.int32),
            "z": np.concatenate([x, -x], axis=2).reshape(N, 128, L).astype(np.float32).astype(BF), "vs": np.stack([gtable(a.reshape(8, -1)) for a in v])}
def setup_inputs(rng):
    fill = rng.choice(np.array([0.0, 0.3, 0.5, 0.7, 0.85, 0.85, 0.95, 1.0]), (N, 8, 1, BASE))
    return pack(boxes(rng), grow(rng, fill), rng.integers(-255, 256, (N, 8, 8, L)), starts(rng))
def setup_inputs_spread(rng):
    R = np.floor(511 * rng.random((N, 8, 16, M)) ** rng.choice(np.array([0.5, 1.0, 2.0, 4.0, 4.0]), (N, 8, 1, M))).astype(np.int64) - 255
    x = np.floor(511 * rng.random((N, 8, 8, L)) ** rng.choice(np.array([0.5, 1.0, 2.0]), (N, 8, 1, L))).astype(np.int64) - 255
    tag = tags(rng); u = rng.random(tag.shape)
    name = 1 + np.where(tag == 0, np.floor((M - 1) * u ** 3), np.floor((BASE - 1) * u ** 2)).astype(np.int64)
    e = np.where(rng.random(tag.shape) < rng.choice(np.array([0.2, 0.5, 0.8, 0.95, 1.0]), (N, 8, 1, BASE)), name + M * tag, 0)
    return pack(R, e, x, 1 + np.floor((BASE - 1) * rng.random((N, 8, T, L)) ** 2).astype(np.int64))
def setup_inputs_ties(rng):
    c = rng.integers(-200, 201, (2, 8, 8, 5)); lo = np.minimum(c[0], c[1]); hi = np.maximum(c[0], c[1])
    tm = np.broadcast_to(np.concatenate([lo, -hi], axis=1), (N, 8, 16, 5))
    R = np.take_along_axis(tm, rng.integers(0, 5, (N, 8, 1, M)), 3)
    R = R + rng.integers(-1, 2, R.shape) * (rng.random(R.shape) < 0.02)
    k = rng.integers(0, 5, (N, 8, 1, L))
    x = np.where(rng.random((N, 8, 8, L)) < 0.5, np.take_along_axis(np.broadcast_to(lo, (N, 8, 8, 5)), k, 3), np.take_along_axis(np.broadcast_to(hi, (N, 8, 8, 5)), k, 3))
    x = x + rng.integers(-1, 2, x.shape)
    return pack(R, grow(rng, rng.choice(np.array([0.3, 0.6, 0.85, 1.0]), (N, 8, 1, BASE))), x, starts(rng))
def setup_inputs_ends(rng):
    F = np.array([1, 2, M - 2, M - 1]); B = np.array([3, 6, M - 5, M - 10]); B3 = (B[:, None] + np.arange(3)).reshape(-1)
    kind = rng.choice(np.array([0, 0, 1, 1, 2, 2, 3, 4, 4]), (N, 8, M)); u = rng.integers(15 - C, 18 - C, (N, 8, M))
    off = rng.random((N, 8, M)) < 0.25; off[:, :, F] = False; u[:, :, F] = 16 - C
    kind[:, :, B3] = 0; off[:, :, B3] = False
    for g in range(8):
        kind[:, g, F] = 1 + (g & 1)
        if (g >> 1) & 1 == 0: off[:, g, 1:3] = True
    few = np.where((np.arange(8)[:, None] + rng.integers(0, 8, (N, 8, 1, M))) % 8 < u[:, :, None, :], 255, -255); k = kind[:, :, None, :]
    any_ = np.where(rng.random((N, 8, 16, M)) < 0.6, -255, 255)
    low = np.where(k == 0, -255, np.where(k == 2, few, np.where(k == 4, any_[:, :, :8], 255)))
    neg = np.where(k == 0, -255, np.where(k == 1, few, np.where(k == 4, any_[:, :, 8:], 255)))
    R = np.concatenate([low, neg], axis=2)
    at = np.where(kind == 2, 8, 0) + rng.integers(0, 8, (N, 8, M))
    off[:, :, B3] = False
    R = np.where((np.arange(16)[:, None] == at[:, :, None, :]) & off[:, :, None, :], R - np.sign(R), R)
    w = rng.choice(np.array([0, 0, 0, 1, 1, 1, 2, 3]), (N, 8, 1, L)); w[..., 0] = 1; w[..., 1] = 0; w[..., L - 2] = 1; w[..., L - 1] = 0
    r = np.where(rng.random((N, 8, 8, L)) < 0.5, -255, 255); one = np.where(np.arange(8)[:, None] == rng.integers(0, 8, (N, 8, 1, L)), -255, 255)
    x = np.where(w == 0, 255, np.where(w == 1, -255, np.where(w == 2, r, one)))
    tag = tags(rng); e1 = rng.choice(F, tag.shape); e2 = rng.choice(np.array([1, 2, BASE - 2, BASE - 1]), tag.shape); h = rng.random(tag.shape) < 0.5
    name = np.where(tag == 0, np.where(h, e1, rng.integers(1, M, tag.shape)), np.where(h, e2, rng.integers(1, BASE, tag.shape)))
    p = rng.random(tag.shape); e = np.where(p < 0.42, 0, np.where(p < 0.66, 2 * M + BASE - 1, name + M * tag))
    for c in (1, BASE - 1):
        for i, n in ((0, M - 1), (1, M - 2), (2, M + BASE - 2), (13, M + 2), (14, 2), (15, 1)): e[:, :, i, c] = n
    few_nodes = np.array([3, 4, BASE - 4, BASE - 3])
    for j in range(4):
        e[:, :, :, few_nodes[j]] = 0
        for i, n in ((0, B[j] + 2), (7, B[j] + 1), (15, B[j])): e[:, :, i, few_nodes[j]] = n
    p = rng.random((N, 8, T, L)); v = np.where(p < 0.33, 1, np.where(p < 0.66, BASE - 1, rng.integers(1, BASE, p.shape)))
    v[..., 0] = 1; v[..., 1] = BASE - 1; v[..., L - 2] = 1; v[..., L - 1] = BASE - 1
    v[..., L - 10:L - 2] = np.tile(few_nodes, 2)
    return pack(R, e, x, v)
def pairs(rng, mode, P):
    if mode in (0, 1):
        a = np.full(LA, P[0]); b = np.full(LA, P[1])
        if mode == 1: j = int(rng.choice(np.array([0, LA - 1, rng.integers(0, LA)]))); a[j] = P[2]; b[j] = P[3]
        return a, b
    a = P[:LA].copy(); b = P[LA:].copy()
    if mode == 3: b[:] = P[LA]
    if mode == 4: b = P[1:LA + 1].copy()
    if mode == 5: a[LA - 1] = a[0]; b[LA - 1] = b[0]
    return a, b
def staged(rng, mode, tight, fill):
    R = boxes(rng); e = grow(rng, fill); x = rng.integers(-255, 256, (N, 8, 8, L)); v = starts(rng); P0 = BASE - 2 * T * LA
    for g in range(8):
        if mode[0, g] < 0: continue
        x[:, g] = rng.integers(-100, 101, (N, 8, L))
        for t in range(T):
            R[:, g, :, P0 + 2 * t * LA:P0 + 2 * (t + 1) * LA] = 40 * t - 255; R[:, g, :, M - (t + 1) * LA:M - t * LA] = 40 * t - 255
        R[:, g, :, Q:Q + 16] = 255; R[:, g, :8, Q + 8:Q + 16] = -255
        for q in range(N):
            for t in range(T):
                P = P0 + 2 * t * LA + rng.permutation(2 * LA); a, b = pairs(rng, int(mode[q, g]), P); sh = (16, LA); pad = Q + rng.integers(0, 16, sh)
                vals = np.zeros(sh, np.int64); nf = rng.choice(np.array([0, 1, 2, 5, 13]), LA) if tight and t % 2 == 0 else np.full(LA, 13)
                vals[0] = M + b
                if t % 2 == 0:
                    vals[2] = np.where(rng.random(LA) < 0.5, M + P0 + 2 * (t + 1) * LA - 1, 0); ty = rng.integers(0, 6, (1, LA))
                    if mode[q, g] == 2: vals[2, 0] = 0; nf[0] = 13; ty[0, 0] = 2
                    row = np.where(ty == 5, rng.integers(0, 5, sh), ty)
                    bf = np.where(row == 0, 0, np.where(row == 1, rng.integers(1, BASE, sh) + M * rng.integers(1, 3, sh), np.where(row == 2, M + P[rng.integers(0, 2 * LA, sh)],
                         np.where(row == 3, Q + rng.integers(0, 8, sh), Q + 8 + rng.integers(0, 8, sh)))))
                else:
                    c = M - 1 - np.arange(LA) - t * LA; vals[1] = c; vals[2] = np.where(rng.random(LA) < 0.5, c, 0)
                    room = rng.choice(np.array([0, 1, 2, 16]) if tight else np.array([1, 2, 9, 16]), (1, LA))
                    bf = np.where(np.argsort(rng.random(sh), axis=0) < room, 0, pad)
                vals[3:] = np.where(np.arange(3, 16)[:, None] < 16 - nf, pad[3:], 0)
                if t % 2 == 1: vals[3:5] = np.where(rng.random(LA) < 0.3, c, 0)
                ac = np.take_along_axis(vals, np.argsort(rng.random(sh), axis=0), 0)
                ev = e[q, g]; ev[:, b] = bf; ev[:, a] = ac
                v[(q - t) % N, g, t, :LA] = a
    return pack(R, e, x, v)
def setup_inputs_crowd(rng):
    mode = rng.integers(0, 6, (N, 8)); mode[0] = rng.permutation(np.array([0, 0, 1, 1, 2, 3, 4, 5])); mode[1] = 2; mode[1, rng.integers(0, 8)] = 5; mode[N - 1] = 2
    return staged(rng, mode, False, 0.6)
def setup_inputs_corners(rng):
    mode = rng.integers(0, 6, (N, 8)); mode[0] = rng.permutation(np.array([0, 1, 2, 2, 3, 4, 4, 5])); mode[:, rng.permutation(8)[:2]] = -1
    return staged(rng, mode, True, rng.choice(np.array([0.0, 0.06, 0.5, 0.94, 0.94, 1.0]), (N, 8, 1, BASE)))
def check_inputs(d):
    bad = []
    for k, lo, hi in (("rg", -255, 255), ("z", -255, 255), ("nd", 0, 2 * M + BASE - 1), ("vs", 1, BASE - 1)):
        a = np.asarray(d[k]).astype(np.float64)
        if not np.all((a >= lo) & (a <= hi)): bad.append("range of " + k)
        elif np.any(a != np.floor(a)): bad.append("whole numbers of " + k)
    a = np.asarray(d["nd"]).astype(np.int64); n = a & (M - 1)
    if np.any((a >= M) & ((n < 1) | (n >= BASE))): bad.append("names of nd")
    a = np.asarray(d["z"]).astype(np.float32).reshape(-1, 2, 8, L)
    if np.any(a[:, 0] != -a[:, 1]): bad.append("halves of z")
    return bad
def take(a, i):
    return np.take_along_axis(a, i[:, :, None, :], 3)
def pick(a, i):
    return np.take_along_axis(a, i.reshape(N, 8, -1), 2).reshape(i.shape)
def reference(rg, nd, z, vs):
    R = rg.astype(np.float32).astype(np.int16).reshape(N, 8, 16, M); X = z.astype(np.float32).astype(np.int16).reshape(N, 8, 16, L)
    W = np.stack([gentries(a) for a in vs]).astype(np.int64).reshape(N, 8, T, L)
    D = np.zeros((N, 8, 16, Q), np.int64); D[..., :BASE] = nd.reshape(N, 8, 16, BASE)
    G = np.zeros((N, 8, 3, L), np.int64); A = np.zeros(N, np.int64); LOW = -2 ** 40
    for t in range(T):
        home = (np.arange(N) - t) % N
        x = X[home]; g = G[home]; need = (C - (A[home] & 1)).reshape(N, 1, 1, 1); S = np.add.reduce(R, axis=2, dtype=np.int64)
        n = np.stack([np.add.reduce(x >= take(R, g[:, :, k]), axis=2, dtype=np.int64) for k in range(3)], axis=2)
        keep = (g > 0) & (n >= need); g = np.where(keep, g, 0); gs = np.where(keep, pick(S, g), -2 ** 20)
        h = np.zeros_like(g); v = W[home][:, :, t]
        for s in (2, 1, 0):
            e = take(D, v); nm = e & (M - 1); tg = e >> MB
            n = np.add.reduce(x[:, :, :, None, :] >= take(R, nm.reshape(N, 8, 16 * L)).reshape(N, 8, 16, 16, L), axis=2, dtype=np.int64)
            ok = (e > 0) & (n >= need); score = pick(S, nm)
            for k in range(s + 1):
                best = np.max(np.where(ok & (tg == k), score * M + (M - 1 - nm), LOW), axis=2)
                new = (best > LOW) & ((best >> MB) > gs[:, :, k])
                g[:, :, k] = np.where(new, M - 1 - (best & (M - 1)), g[:, :, k]); gs[:, :, k] = np.where(new, best >> MB, gs[:, :, k]); h[:, :, k] = np.where(new, v, h[:, :, k])
            if s > 0: v = np.where(g[:, :, s] > 0, g[:, :, s], v)
        even = t % 2 == 0
        a = h[:, :, 1 if even else 0, :LA]; b = g[:, :, 1, :LA] if even else v[:, :, :LA]
        ea = take(D, a); eb = take(D, b)
        ask = (a > 0) & (a != b) & np.any((ea if even else eb) == 0, axis=2)
        a1 = a[:, :, :, None]; b1 = b[:, :, :, None]; a2 = a[:, :, None, :]; b2 = b[:, :, None, :]
        meet = ((a1 == a2) | (a1 == b2) | (b1 == a2) | (b1 == b2)) & ask[:, :, None, :] & np.tri(LA, LA, -1, dtype=bool)
        act = ask & ~np.any(meet, axis=3); A[home] = np.add.reduce(act, axis=(1, 2), dtype=np.int64)
        q, p, l = np.nonzero(act); al = a[q, p, l]; bl = b[q, p, l]
        if even:
            nb = eb & (M - 1); full = eb > 0
            go = full & (pick(R[:, :, t], nb) >= x[:, :, t, None, :LA]); stay = full & ~go & (pick(R[:, :, 8 + t], nb) >= x[:, :, 8 + t, None, :LA])
            strad = full & ~go & ~stay; number = np.add.accumulate(strad, axis=2, dtype=np.int64)
            free = ea == 0; place = np.add.accumulate(free, axis=2, dtype=np.int64) - free
            put = strad & (number < np.add.reduce(free, axis=2, dtype=np.int64)[:, :, None, :])
            new = BASE + LA * (t >> 1) + np.arange(LA)
            ya = np.where(free & (place == 0), M + new, ea)
            for j in range(16):
                ya = np.where(free & put[:, :, j:j + 1] & (place == number[:, :, j:j + 1]), eb[:, :, j:j + 1], ya)
            yb = np.where(go | put, 0, eb); yw = np.where(go, eb, 0)
            D[q, p, :, new[l]] = yw[q, p, :, l]
            cut = R[q, p, :, bl]; half = cut.copy(); half[:, t] = x[q, p, t, l]; cut[:, 8 + t] = x[q, p, 8 + t, l]
            R[q, p, :, new[l]] = half; R[q, p, :, bl] = cut
        else:
            e0 = g[:, :, 0, None, :LA]; free = eb == 0; place = np.add.accumulate(free, axis=2, dtype=np.int64) - free
            ya = np.where(ea == e0, 0, ea); yb = np.where(free & (place == 0), e0, eb)
        D[q, p, :, al] = ya[q, p, :, l]; D[q, p, :, bl] = yb[q, p, :, l]
        G[home] = g
    return {"yn": D.reshape(N, 128, Q).astype(np.float32), "yr": R[..., :Q].reshape(N, 128, Q).astype(np.float32).astype(BF), "yg": g.reshape(N, 8, 3 * L).astype(np.float32)}

@@ -1,0 +1,736 @@
+import numpy as np
+from concourse.bass import DstId, RemoteDMATransfer
+from concourse.mybir import AluOpType as A, ActivationFunctionType as F
+
+N, NV = 4, 4
+BIG = float(2 ** 27)
+NOG = float(2 ** 26)
+CC = 16384.0
+f32, bf, i32, u16, f16 = "float32", "bfloat16", "int32", "uint16", "float16"
+
+SB = {
+    "RW": (10496, bf), "RSV": (256, bf), "D": (2304, f32), "NDI": (1792, i32),
+    "XZ": (1024, bf), "VSO": (64, i32), "VSR": (64, i32), "XT": (1024, bf), "L2": (64, u16),
+    "GF": (960, f32), "GR": (960, f32), "KS": (16, f32), "KR": (16, f32), "K0": (4, f32),
+    "KA": (4, f32), "KT": (8, f32), "NIB": (128, bf), "HB": (256, bf), "IB": (128, bf), "IF": (128, f32), "ONE": (128, bf), "RBIG": (512, bf),
+    "BK3": (24, bf), "BKF": (8, f32), "SC": (24, bf), "SCT": (64, bf), "SX": (512, bf),
+    "TRX": (128, bf), "TRC": (128, bf), "PBC": (2048, bf), "TRL": (512, bf), "SELG": (1024, bf),
+    "CK": (768, bf), "RS": (384, f32), "MKI": (384, i32), "MKJ": (384, i32), "MK": (384, f32), "NMK": (16, f32),
+    "PM": (4, f32), "DU0": (24, f32), "DUM": (24, f32), "NC": (256, f32),
+    "OCI": (128, i32), "OC": (128, u16), "O5I": (48, i32), "O5": (48, u16),
+    "EU": (256, u16), "FA": (256, bf), "FB": (256, bf), "FW": (768, f16),
+    "R": (4096, bf), "CMP": (4096, bf), "PEN": (256, bf), "SCN": (768, f32),
+    "MI": (48, i32), "LO": (48, i32), "THR": (48, i32), "D0": (240, f32), "D1": (240, f32),
+    "VS": (160, f32), "AX": (256, f16), "LV": (32, u16), "AV": (256, f16), "AL": (128, f16),
+    "AG": (768, f32), "LG": (48, u16), "RG": (768, bf), "CG": (768, bf), "T1": (48, f32), "T2": (48, f32),
+    "DH": (40, f32), "HS": (40, f32), "AA": (128, f32), "LA": (8, u16), "PRE": (24, f32),
+    "EA": (128, f32), "EB": (128, f32), "FR": (128, bf), "S8": (8, f32), "DD": (8, f32), "HH": (8, f32),
+    "NQ": (8, f32), "Q8": (8, f32), "ASK": (16, bf), "ACT": (16, bf), "ABT": (256, f16),
+    "AB": (2048, f32), "EQ": (2048, bf), "AC": (128, bf), "LT": (24, f32), "LU": (24, f32), "LS": (24, u16),
+    "AI": (4, i32), "AJ": (4, i32), "YS": (512, f32), "GE": (256, bf), "ST": (128, bf),
+    "W1": (128, f32), "W2": (128, f32), "W3": (128, f32), "W4": (128, f32), "W5": (128, bf), "W6": (128, bf),
+    "U": (512, f32), "MM": (2048, f32), "GI": (136, i32), "GD": (128, i32), "GA": (128, i32), "VAL": (128, f32),
+    "RB": (256, bf), "XS": (256, bf), "YG": (768, f32),
+}
+PS = ["X0", "X1", "Y0", "Y1", "C", "K", "M", "M2"]
+SCRATCH = {k: ("sbuf", [128, n], d) for k, (n, d) in SB.items()}
+SCRATCH.update({k: ("psum", [128, 512], f32) for k in PS})
+DMAS = ["ld%d" % i for i in range(8)] + ["st%d" % i for i in range(6)]
+SEMAPHORES = ["qv", "qs", "qp", "qg", "sent"] + DMAS + ["%s%d" % (a, t) for a in ("in", "ga", "gb", "ks") for t in (1, 2, 3)]
+SQS = ((), (0, 1, 2), (0, 1, 2, 3))
+PAT = ((0, 2), (0, 2), (0, 2))
+CHUNKS = ((0, 512), (512, 1024), (1024, 1536), (1536, 2048))
+VG = (((), ()), ((), ()), ((), ()))
+LEADS = [1000.0 * i for i in range(-2, 14)]
+EVEN = 3
+ROUNDS, PASSES, SHAKE = 300, 2, 100.0
+PLAN = {}
+PEN_S = False
+
+GATH, SCAT = 1.56, 3.8
+PE0, PE1 = 5.0, 0.5
+LAT = 100.0
+
+
+def ap(name, c0, c1, st=1, p0=0, p1=128):
+    return (name, c0, c1, st, p0, p1)
+
+
+def ind(win, off):
+    return ("ind", win, off)
+
+
+def width(a):
+    if a[0] == "ind":
+        return 16 * (a[2][2] - a[2][1])
+    return (a[2] - a[1] + a[3] - 1) // a[3]
+
+
+def two(a):
+    return a[0] != "ind" and a[0] in SB and SB[a[0]][1] in (bf, u16, f16)
+
+
+def rank_program(g, core, T, topo):
+    rank = T.rank_of(core)
+    if rank is None:
+        return
+    ops = []
+    stage = [0, 0]
+    last_w = {}
+    last_r = {}
+    last_p = {}
+
+    def real(a):
+        if not isinstance(a, tuple):
+            return a
+        if a[0] == "ind":
+            return real(a[1]).indirect(real(a[2]))
+        t = T[a[0]]
+        if a[3] == 1:
+            return t[a[4]:a[5], a[1]:a[2]]
+        return t[a[4]:a[5], a[1]:a[2]:a[3]]
+
+    def op(eng, fn, outs, ins, cost, waits=(), after=(), sem=None, lat=0.0):
+        k = len(ops)
+        rd, wr = [], []
+        for a in ins:
+            if isinstance(a, tuple):
+                rd += [a[1], a[2]] if a[0] == "ind" else [a]
+        for a in outs:
+            if a[0] == "ind":
+                wr.append(a[1])
+                rd.append(a[2])
+            else:
+                wr.append(a)
+        dep = {}
+        for a in rd + wr:
+            if a[0] in PS:
+                j = last_p.get(a[0])
+                if j is not None and j != k:
+                    dep[j] = dep.get(j, False) or ops[j]["eng"] != eng
+                last_p[a[0]] = k
+        for a in rd:
+            if a[0] not in PS:
+                for c0, c1, j in last_w.get(a[0], []):
+                    if c0 < a[2] and a[1] < c1:
+                        dep[j] = True
+        for a in wr:
+            if a[0] not in PS:
+                for c0, c1, j in last_w.get(a[0], []):
+                    if c0 < a[2] and a[1] < c1:
+                        dep[j] = True
+                for c0, c1, j in last_r.get(a[0], []):
+                    if c0 < a[2] and a[1] < c1:
+                        dep[j] = True
+        for a in wr:
+            if a[0] not in PS:
+                if a[3] == 1 and a[4] == 0 and a[5] == 128:
+                    last_w[a[0]] = [e for e in last_w.get(a[0], []) if not (a[1] <= e[0] and e[1] <= a[2])]
+                    last_r[a[0]] = [e for e in last_r.get(a[0], []) if not (a[1] <= e[0] and e[1] <= a[2])]
+                last_w.setdefault(a[0], []).append((a[1], a[2], k))
+        for a in rd:
+            if a[0] not in PS:
+                last_r.setdefault(a[0], []).append((a[1], a[2], k))
+        soft = dict(after)
+        ops.append({"eng": eng, "fn": fn, "dep": dep, "cost": cost, "waits": list(waits), "soft": soft, "sem": sem, "lat": lat, "out": wr[:1],
+                    "half": stage[1], "stage": stage[0]})
+        return k
+
+    def vcost(out, ins, rate):
+        n = width(out)
+        if out[0] == "ind":
+            rate = SCAT
+        elif ins[0][0] == "ind":
+            rate = GATH
+        return 60.0 + n * rate
+
+    def tt(out, a, b, alu, **kw):
+        rate = 1.0 if (a[0] in PS or b[0] in PS) else 2.0
+        return op("v", lambda: g.vector.tensor_tensor(real(out), real(a), real(b), alu), [out], [a, b], vcost(out, [a], rate), **kw)
+
+    def ts(out, a, s1, o1, s2=None, o2=None, **kw):
+        rate = 0.5 if two(out) and two(a) else 1.0
+        if o2 is None:
+            fn = lambda: g.vector.tensor_scalar(real(out), real(a), real(s1), None, o1)
+        else:
+            fn = lambda: g.vector.tensor_scalar(real(out), real(a), real(s1), real(s2), o1, o2)
+        return op("v", fn, [out], [a, s1, s2], vcost(out, [a], rate), **kw)
+
+    def cp(out, a, **kw):
+        rate = 0.5 if two(out) and two(a) else 1.0
+        return op("v", lambda: g.vector.tensor_copy(real(out), real(a)), [out], [a], vcost(out, [a], rate), **kw)
+
+    def ms(out, c):
+        return op("v", lambda: g.vector.memset(real(out), c), [out], [], 60.0 + width(out) * (0.5 if two(out) else 1.0))
+
+    def scan(out, d0, d1, o0, o1):
+        return op("v", lambda: g.vector.tensor_tensor_scan(real(out), real(d0), real(d1), 0.0, o0, o1), [out], [d0, d1], 60.0 + width(out))
+
+    def act(out, a, fn=F.Identity, bias=None, scale=None, **kw):
+        ar = {}
+        def call():
+            if bias is not None:
+                ar["bias"] = real(bias)
+            if scale is not None:
+                ar["scale"] = real(scale)
+            return g.scalar.activation(real(out), real(a), fn, **ar)
+        return op("s", call, [out], [a, bias, scale], 70.0 + width(out) * (GATH if a[0] == "ind" else 1.0), **kw)
+
+    def mm(out, l, r, start=True, stop=True, **kw):
+        c = max(min(64, width(l)), width(r)) * (4 if SB[l[0]][1] == f32 else 1)
+        return op("p", lambda: g.tensor.matmul(real(out), real(l), real(r), start, stop), [out], [l, r], PE0 + PE1 * c, **kw)
+
+    def iota(out, pat, base, cm):
+        if SB[out[0]][1] == i32:
+            fn = lambda: g.iota(real(out), pat, base, cm)
+        else:
+            fn = lambda: g.iota(real(out), pat, base, cm, allow_small_or_imprecise_dtypes=True)
+        return op("g", fn, [out], [], 150.0 + 2 * width(out))
+
+    def sel(out, a, pat, cmp, base, cm):
+        return op("g", lambda: g.affine_select(real(out), real(a), pat, cmp, 0.0, base, cm), [out], [a], 200.0 + 2 * width(out))
+
+    nd_ = [0, 0]
+    outs_ = []
+
+    def load(q, out, src, ns, prev=None):
+        s = "ld%d" % nd_[0]
+        nd_[0] += 1
+        e = g.sync if q == "y" else g.scalar
+        return op(q, lambda: e.dma_start(real(out), src), [out], [], 60.0, sem=s, lat=ns, after={} if prev is None else {prev: 0.0})
+
+    def store(q, dst, a, ns):
+        s = "st%d" % nd_[1]
+        nd_[1] += 1
+        outs_.append(s)
+        e = g.sync if q == "y" else g.scalar
+        return op(q, lambda: e.dma_start(dst, real(a)), [], [a], 60.0, sem=s, lat=ns)
+
+    sent = [0]
+
+    def emask(dst, a, b):
+        m = 0
+        for e in topo.engines(core, dst)[a:b]:
+            m |= 1 << e
+        return m
+
+    def send(pairs, ins):
+        trs = []
+        for dt_, o, s, sem, e0 in pairs:
+            dst = T.cores[(rank + dt_) % N]
+            rid, pid, _ = topo.addr(dst)
+            trs.append((dst, rid, pid, o, s, sem, e0))
+        sent[0] += 2 * len(pairs)
+        def call():
+            if len(trs) == 1:
+                dst, rid, pid, o, s, sem, e0 = trs[0]
+                g.remote_dma(real(o), real(s), T.sem[sem], T.sem["sent"], pid, rid, emask(dst, e0, e0 + 2))
+            else:
+                g.remote_dma_fused([RemoteDMATransfer(dst_ids=[DstId(rid=rid, pnc=pid)], dma_engine_mask=emask(dst, e0, e0 + 2),
+                                                      remote_sem=T.sem[sem], src=real(s), dst=real(o))
+                                    for dst, rid, pid, o, s, sem, e0 in trs], local_sem=T.sem["sent"])
+            return None
+        return op("g", call, [], ins, 1000.0)
+
+    l0 = load("y", ap("RW", 0, 2048), T.rg[:, 0:2048], 3500.0)
+    load("s", ap("VSO", 0, 64), T.vs[:, :], 2000.0)
+    load("s", ap("XZ", 0, 256), T.z[:, :], 2200.0)
+    l1 = load("y", ap("NDI", 0, 896), T.nd[:, 0:896], 4800.0, l0)
+    l2 = load("y", ap("NDI", 896, 1792), T.nd[:, 896:1792], 6000.0, l1)
+    load("y", ap("RW", 2048, 4096), T.rg[:, 2048:4096], 7500.0, l2)
+
+    ms(ap("ONE", 0, 128), 1.0)
+    iota(ap("OCI", 0, 128), [[1, 128]], 0, 0)
+    cp(ap("OC", 0, 128), ap("OCI", 0, 128))
+    sel(ap("IB", 0, 128), ap("ONE", 0, 128), [[-1, 128]], A.is_equal, 0, 1)
+    act(ap("RW", 6144, 8192), ind(ap("IB", 0, 128), ap("OC", 0, 128)))
+    cp(ap("IF", 0, 128), ap("IB", 0, 128))
+    ms(ap("RBIG", 0, 128), 0.0)
+    ms(ap("RBIG", 384, 512), 0.0)
+    ts(ap("RBIG", 128, 256), ap("IB", 0, 128), BIG, A.mult)
+    ts(ap("RBIG", 256, 384), ap("IB", 0, 128), -BIG, A.mult)
+    sel(ap("BK3", 0, 24), ap("ONE", 0, 24), [[0, 3], [-16, 8]], A.is_ge, 0, 1)
+    sel(ap("BK3", 0, 24), ap("BK3", 0, 24), [[0, 3], [16, 8]], A.is_ge, 15, -1)
+    cp(ap("BKF", 0, 8), ap("BK3", 0, 8))
+    ts(ap("SC", 0, 24), ap("BK3", 0, 24), -4096.0, A.mult)
+    iota(ap("O5I", 0, 48), [[5, 48]], 4, 0)
+    cp(ap("O5", 0, 48), ap("O5I", 0, 48))
+    iota(ap("MKI", 0, 384), [[0, 24], [-1, 16]], 16, 1)
+    ts(ap("MKJ", 0, 384), ap("MKI", 0, 384), 15, A.bitwise_and)
+    ts(ap("MK", 0, 384), ap("MKJ", 0, 384), 0.0, A.is_equal)
+    ts(ap("NMK", 0, 16), ap("MK", 0, 16), -1.0, A.mult, 1.0, A.add)
+    cp(ap("PM", 0, 1), ap("MKJ", 0, 1))
+    iota(ap("DU0", 0, 16), [[16, 16]], 2048, 0)
+    iota(ap("DU0", 16, 24), [[16, 8]], 128, 0)
+    ts(ap("DUM", 0, 24), ap("DU0", 0, 24), ap("PM", 0, 1), A.add)
+    ms(ap("CK", 0, 768, 1, 0, 64), 0.0)
+    ms(ap("CK", 128, 384, 1, 0, 32), BIG / 32)
+    ms(ap("CK", 0, 512, 1, 32, 64), 64.0)
+    ms(ap("RS", 0, 384), 0.0)
+    ms(ap("RS", 0, 384, 16), float(2 ** 30))
+    ms(ap("D0", 0, 240), 1.0)
+    ms(ap("D0", 0, 240, 5), 0.0)
+    ms(ap("D1", 0, 240), 0.0)
+    ms(ap("DH", 0, 40), 0.0)
+    ms(ap("THR", 0, 48), 2 ** 25)
+    ms(ap("K0", 0, 4), 12.0)
+    ms(ap("GI", 0, 8), 0)
+    iota(ap("RW", 10240, 10496), [[0, 256]], 0, 0)
+    iota(ap("D", 1792, 2304), [[0, 512]], 0, 0)
+    iota(ap("YS", 384, 512), [[0, 128]], 0, 0)
+    ms(ap("PRE", 16, 24), -128.0)
+    ms(ap("KA", 0, 4), 1.0)
+    for j, sq in enumerate(SQS):
+        for q in sq:
+            ms(ap("KA", j + 1, j + 2, 1, 32 * q, 32 * q + 32), 2.0)
+            ms(ap("K0", j + 1, j + 2, 1, 32 * q, 32 * q + 32), 8.0)
+    ts(ap("NIB", 0, 128), ap("IB", 0, 128), -1.0, A.mult)
+    cp(ap("D", 0, 896), ap("NDI", 0, 896))
+    cp(ap("D", 896, 1792), ap("NDI", 896, 1792))
+    act(ap("RW", 4096, 6144), ap("RW", 0, 2048))
+    cp(ap("RW", 8192, 10240), ap("RW", 0, 2048))
+    ms(ap("RW", 0, 1), 300.0)
+    act(ap("RSV", 0, 128), ap("RW", 2176, 2304))
+    act(ap("RSV", 128, 256), ap("RW", 6272, 6400))
+    sz = send([(t, ap("XZ", 256 * t, 256 * t + 256), ap("XZ", 0, 256), "in%d" % t, 2 * t - 2) for t in (1, 2, 3)], [ap("XZ", 0, 256)])
+    sv = send([(t, ap("VSR", 16 * t, 16 * t + 16), ap("VSO", 16 * t, 16 * t + 16), "in%d" % t, 2 * t - 2) for t in (1, 2, 3)], [ap("VSO", 0, 64)])
+    for j, t in enumerate((0, 2)):
+        cp(ap("SCT", 32 * j, 32 * j + 8), ap("SC", 0, 8))
+        sel(ap("SCT", 32 * j + 8, 32 * j + 24), ap("ONE", 0, 16), [[-8, 2], [-16, 8]], A.is_equal, -t, 1)
+        iota(ap("SX", 256 * j, 256 * j + 256), [[0, 256]], -1, 0)
+        sel(ap("SX", 256 * j, 256 * j + 256), ap("SX", 256 * j, 256 * j + 256), [[-8, 2], [-16, 8], [0, 16]], A.is_equal, -t, 1)
+    sel(ap("TRX", 0, 128), ap("ONE", 0, 128), [[-16, 8], [0, 16]], A.is_ge, 0, 1)
+    sel(ap("TRX", 0, 128), ap("TRX", 0, 128), [[16, 8], [1, 16]], A.is_gt, 0, -1)
+    iota(ap("TRC", 0, 128), [[0, 128]], int(CC), 0)
+    sel(ap("TRC", 0, 128), ap("TRC", 0, 128), [[-16, 8], [0, 16]], A.is_ge, 0, 1)
+    sel(ap("TRC", 0, 128), ap("TRC", 0, 128), [[16, 8], [1, 16]], A.is_ge, 0, -1)
+    iota(ap("TRL", 0, 512), [[0, 512]], 4096, 0)
+    sel(ap("TRL", 0, 512), ap("TRL", 0, 512), [[0, 4], [-1, 128]], A.is_ge, 0, 1)
+    sg = ap("SELG", 0, 1024, 1, 0, 8)
+    iota(sg, [[0, 1024]], 1, 0)
+    sel(sg, sg, [[-1, 8], [0, 128]], A.is_equal, 0, 1)
+    iota(ap("NC", 0, 256), [[1, 256]], 4096 + 1792, 0)
+    iota(ap("PBC", 0, 2048), [[0, 2048]], int(CC), 0)
+    sel(ap("PBC", 0, 2048), ap("PBC", 0, 2048), [[0, 16], [-16, 8], [0, 16]], A.is_ge, 0, 1)
+    sel(ap("PBC", 0, 2048), ap("PBC", 0, 2048), [[1, 16], [16, 8], [0, 16]], A.is_gt, 1, -1)
+
+    xb = [0, 0]
+    KB, CB = ("M2", "K"), ("M", "C")
+
+    def xbank(h):
+        xb[h] += 1
+        return "YX"[h] + "01"[xb[h] % 2]
+
+    sends = {}
+
+    def arrived(kind, t):
+        if t == 0:
+            return {}
+        if kind == "in":
+            return {"waits": [("in%d" % t, 4)], "after": {sz: 4000.0, sv: 4000.0}}
+        return {"waits": [("%s%d" % (kind, t), 2)], "after": {sends[kind, t]: 3500.0}}
+
+    def xs(t, h):
+        return ap("XZ", 256 * t + 128 * h, 256 * t + 128 * h + 128)
+
+    def kcol(t, j=0):
+        return ap("K0", j, j + 1) if t == 0 else ap("KR", 4 * t + j, 4 * t + j + 1)
+
+    def prep(t):
+        for h in range(2):
+            mm(ap("C", 256 + 128 * h, 384 + 128 * h), xs(t, h), ap("IB", 0, 128), **arrived("in", t))
+        act(ap("XT", 256 * t, 256 * t + 256), ap("C", 256, 512))
+        cp(ap("L2", 16 * t, 16 * t + 16), ap("VSR" if t else "VSO", 16 * t, 16 * t + 16), **arrived("in", t))
+
+    def prep_next(t):
+        if t + 1 < NV:
+            prep(t + 1)
+
+    def start_nodes(t, h):
+        if True:
+            c = 16 * t + 8 * h
+            tt(ap("AV", 128 * h, 128 * h + 128), ind(ap("VSR" if t else "VSO", c, c + 8), ap("OC", 0, 8)), ap("MK", 0, 128), A.mult, **arrived("in", t))
+            mm(ap(CB[h], 200, 208), ap("AV", 128 * h, 128 * h + 128), ap("BK3", 0, 8))
+            cp(ap("D1", 120 * h + 80, 120 * h + 120, 5), ap(CB[h], 200, 208))
+
+    def guards(t, h):
+        o, w = 384 * h, 24 * h
+        gr = 240 * t + 120 * h
+        tt(ap("AG", o, o + 384), ind(ap("GR", gr, gr + 120), ap("O5", 0, 24)), ap("MK", 0, 384), A.mult, **arrived("ga" if h == 0 else "gb", t))
+        for k in range(3):
+            mm(ap(KB[h], 8 * k, 8 + 8 * k), ap("AG", o + 128 * k, o + 128 * k + 128), ap("BKF", 0, 8))
+        cp(ap("LG", w, w + 24), ap(KB[h], 0, 24))
+        act(ap("RG", o, o + 384), ind(ap("RW", 0, 4096), ap("LG", w, w + 24)))
+        x = xbank(h)
+        for k in range(3):
+            mm(ap(x, 128 * k, 128 * k + 128), ap("IB", 0, 128), xs(t, h), **arrived("in", t))
+        tt(ap("CG", o, o + 384), ap("RG", o, o + 384), ap(x, 0, 384), A.is_le)
+        for k in range(3):
+            mm(ap(CB[h], 160 + 8 * k, 168 + 8 * k), ap("RG", o + 128 * k, o + 128 * k + 128), ap("SC", 0, 8))
+        for k in range(3):
+            mm(ap(CB[h], 128 + 8 * k, 136 + 8 * k), ap("CG", o + 128 * k, o + 128 * k + 128), ap("BK3", 0, 8))
+        cnt = ap(CB[h], 128, 152)
+        ts(ap("D0", 120 * h + 1, 120 * h + 120, 5), cnt, kcol(t), A.is_lt, **arrived("ks", t))
+        ts(ap("T1", w, w + 24), cnt, kcol(t), A.is_lt, NOG, A.mult, **arrived("ks", t))
+        ts(ap("T2", w, w + 24), cnt, kcol(t), A.is_ge, **arrived("ks", t))
+        tt(ap("THR", w, w + 24), ap("T1", w, w + 24), ap(CB[h], 160, 184), A.add)
+        tt(ap("D1", 120 * h + 1, 120 * h + 120, 5), ap("T2", w, w + 24), ap("GR", gr + 4, gr + 120, 5), A.mult, **arrived("ga" if h == 0 else "gb", t))
+
+    def vlist(t, s, h):
+        return ap("L2", 16 * t + 8 * h, 16 * t + 8 * h + 8) if s == 2 else ap("LV", 16 * s + 8 * h, 16 * s + 8 * h + 8)
+
+    def gather(t, s, h):
+        o = 128 * h
+        e = ap("EU", o, o + 128)
+        cp(e, ind(ap("D", 0, 2048), vlist(t, s, h)))
+        sq = SQS[PAT[s][h]]
+        for c0, c1 in CHUNKS:
+            (cp if c0 // 512 in VG[s][h] else act)(ap("R", 2048 * h + c0, 2048 * h + c1), ind(ap("RW", 0, 10240), ap("EU", o + c0 // 16, o + c1 // 16)))
+        ts(ap("FA", o, o + 128), e, 4096.0, A.is_ge)
+        if s:
+            ts(ap("FB", o, o + 128), e, 8192.0, A.is_ge)
+        for k in range(s + 1):
+            ts(ap("FW", 384 * h + 128 * k, 384 * h + 128 * k + 128), e, -4096.0 * k - 2048.0, A.add)
+        for q in range(4):
+            x = xbank(h)
+            c = 2048 * h + 512 * q
+            mm(ap(x, 0, 512), ap("XT", 256 * t + o, 256 * t + o + 128), ap("RW", 6144 + 512 * q, 6656 + 512 * q), True, q not in sq)
+            if q in sq:
+                mm(ap(x, 0, 512), ap("NIB", 0, 128), ap("R", c, c + 512), False, True)
+                act(ap("CMP", c, c + 512), ap(x, 0, 512), F.Sign, bias=0.5)
+            else:
+                tt(ap("CMP", c, c + 512), ap("R", c, c + 512), ap(x, 0, 512), A.is_le)
+
+    def tail(t, s, h):
+        o, n, w, W = 128 * h, 128 * (s + 1), 24 * h, 8 * (s + 1)
+        cut = s == 0 and h == 0 and t % 2 == 0
+        K, C, kc = KB[h], CB[h], kcol(t, 1 + PAT[s][h])
+        if cut:
+            mm(ap(K, 0, 384), ap("ONE", 0, 128, 1, 0, 64), ap("CK", 384, 768, 1, 0, 64), True, False)
+            mm(ap(K, 128, 384), xs(t, 0), ap("SX", 128 * t, 128 * t + 256), False, False, **arrived("in", t))
+        else:
+            mm(ap(K, 0, n), ap("ONE", 0, 128, 1, 0, 64), ap("CK", 0, n, 1, 0, 64), True, False)
+        mm(ap(K, 0, n), ap("FA", o, o + 128), ap("RBIG", 128, 128 + n), False, False)
+        if s:
+            mm(ap(K, 128, n), ap("FB", o, o + 128), ap("RBIG", 128, n), False, False)
+        for k in range(s + 1):
+            mm(ap(K, 128 * k, 128 * k + 128), ap("FW", 384 * h + 128 * k, 384 * h + 128 * k + 128), ap("IB", 0, 128), False, False)
+        for i in range(16):
+            r = ap("R", 2048 * h + i, 2048 * h + 2048, 16)
+            if cut:
+                mm(ap(K, i, 384, 16), r, ap("SCT", 16 * t, 16 * t + 24), False, False)
+            else:
+                mm(ap(K, i, n, 16), r, ap("SC", 0, W), False, False)
+        for i in range(16):
+            mm(ap(C, i, 128, 16), ap("CMP", 2048 * h + i, 2048 * h + 2048, 16), ap("BK3", 0, 8))
+        if PEN_S:
+            act(ap("PEN", o, o + 128), ap(C, 0, 128), F.Relu, bias=kc, scale=-1.0, **arrived("ks", t))
+        else:
+            ts(ap("PEN", o, o + 128), ap(C, 0, 128), kc, A.is_lt, **arrived("ks", t))
+        for k in range(s + 1):
+            mm(ap(K, 128 * k, 128 * k + 128), ap("RBIG", 128, 256), ap("PEN", o, o + 128), False, k == s)
+        scan(ap("SCN", 384 * h, 384 * h + n), ap("RS", 0, n), ap(K, 0, n), A.add, A.min)
+        if cut:
+            ts(ap("GE", 0, 256), ap(K, 128, 384), 0.0, A.is_ge)
+        mi, lo = ap("MI", w, w + W), ap("LO", w, w + W)
+        tt(mi, ap("SCN", 384 * h + 15, 384 * h + n, 16), ap("THR", w, w + W), A.min)
+        ts(lo, mi, 4095, A.bitwise_and)
+        c = 120 * h + 4 - s
+        cp(ap("D1", c, 120 * h + 40 * (s + 1), 5), lo)
+        ts(ap("D0", c, 120 * h + 40 * (s + 1), 5), lo, 0.0, A.is_equal)
+        if s:
+            v = 80 * h + 40 * (2 - s)
+            scan(ap("VS", v, v + 40), ap("D0", 120 * h + 40 * s, 120 * h + 40 * s + 40), ap("D1", 120 * h + 40 * s, 120 * h + 40 * s + 40), A.mult, A.add)
+            tt(ap("AX", o, o + 128), ind(ap("VS", v, v + 40), ap("O5", 0, 8)), ap("MK", 0, 128), A.mult)
+            mm(ap(C, 192, 200), ap("AX", o, o + 128), ap("BK3", 0, 8))
+            cp(vlist(t, s - 1, h), ap(C, 192, 200))
+            if s == 1 and h == 0:
+                tt(ap("PRE", 8, 16), ap(C, 192, 200), ap("DUM", 8, 16), A.subtract)
+            tt(ap("THR", w, w + W - 8), ap("MI", w, w + W - 8), ap("LO", w, w + W - 8), A.subtract)
+            if s == 2:
+                cp(ap("D1", 120 * h + 40, 120 * h + 80, 5), ap("VS", v + 4, v + 40, 5))
+
+    def final_guards(t, h):
+        ms(ap("D1", 120 * h + 40, 120 * h + 120, 5), 0.0)
+        scan(ap("GF", 240 * t + 120 * h, 240 * t + 120 * h + 120), ap("D0", 120 * h, 120 * h + 120), ap("D1", 120 * h, 120 * h + 120), A.mult, A.add)
+        if t + 1 < NV:
+            c, kind = 240 * t + 120 * h, "ga" if h == 0 else "gb"
+            gf = ap("GF", c, c + 120)
+            sends[kind, t + 1] = send([(1, ap("GR", c + 240, c + 360), gf, "%s%d" % (kind, t + 1), 0)], [gf])
+
+    v2, v1, v0 = ap("D1", 80, 120, 5), ap("D1", 40, 80, 5), ap("VS", 44, 80, 5)
+    av = ap("HS", 4, 40, 5)
+
+    def early3(t):
+        ts(ap("DH", 1, 40, 5), v2, -1.0, A.mult)
+        tt(ap("DH", 2, 40, 5), v2, v1, A.subtract)
+        tt(ap("DH", 3, 40, 5), v1, v0, A.subtract)
+        cp(ap("DH", 4, 40, 5), v0)
+        act(ap("EB", 0, 128), ind(ap("D", 0, 2048), vlist(t, 0, 0)))
+        if t % 2 == 0:
+            lb = ind(ap("RW", 0, 2048), vlist(t, 0, 0))
+            act(ap("RB", 0, 128), lb, scale=ap("NMK", 8 + t, 9 + t))
+            act(ap("RB", 128, 256), lb, scale=ap("NMK", t, t + 1))
+            act(ap("XS", 0, 128), xs(t, 0), scale=ap("MK", 8 + t, 9 + t), **arrived("in", t))
+            act(ap("XS", 128, 256), xs(t, 0), scale=ap("MK", t, t + 1), **arrived("in", t))
+            tt(ap("HB", 0, 128), ap("RB", 128, 256), ap("XS", 128, 256), A.add)
+            act(ap("HB", 128, 256), ap("RW", 1792 + 64 * t, 1920 + 64 * t))
+
+    def source(t):
+        k = 1 - t % 2
+        scan(ap("HS", 0, 40), ap("D0", 40 * k, 40 * k + 40), ap("DH", 0, 40), A.mult, A.add)
+        tt(ap("AL", 0, 128), ind(ap("HS", 0, 40), ap("O5", 0, 8)), ap("MK", 0, 128), A.mult)
+        mm(ap("M", 128, 256, 1, 0, 8), av, ap("IF", 0, 128))
+        mm(ap("M", 256, 384, 1, 0, 8), v0, ap("IF", 0, 128))
+        cp(ap("ABT", 0, 256, 1, 0, 8), ap("M", 128, 384, 1, 0, 8))
+        mm(ap("M", 80, 88), ap("AL", 0, 128), ap("BK3", 0, 8))
+        cp(ap("LA", 0, 8), ap("M", 80, 88))
+        tt(ap("PRE", 0, 8), ap("M", 80, 88), ap("DUM", 0, 8), A.subtract)
+        act(ap("EA", 0, 128), ind(ap("D", 0, 2048), ap("LA", 0, 8)))
+        tt(ap("S8", 0, 8), av, v0, A.add)
+        tt(ap("DD", 0, 8), av, v0, A.subtract)
+        act(ap("HH", 0, 8), ap("DD", 0, 8), F.Abs)
+        ts(ap("NQ", 0, 8), ap("DD", 0, 8), 0.0, A.not_equal)
+        tt(ap("Q8", 0, 8), ap("NQ", 0, 8), av, A.min)
+        ts(ap("FR", 0, 128), ap("EA" if k else "EB", 0, 128), 0.0, A.is_equal)
+        mm(ap("M", 32, 40), ap("FR", 0, 128), ap("BK3", 0, 8))
+        mm(ap("M", 384, 512), ap("TRX", 0, 128), ap("FR", 0, 128))
+        tt(ap("ASK", 0, 8), ap("Q8", 0, 8), ap("M", 32, 40), A.min)
+        tt(ap("W5", 0, 128), ap("FR", 0, 128), ap("M", 384, 512), A.is_gt)
+
+    def meet(t):
+        for b in range(4):
+            y = "Y%d" % (b % 2)
+            mm(ap(y, 0, 512), ap("IB", 0, 128), ap("TRL", 0, 512), True, False)
+            for j in range(2):
+                gg = 2 * b + j
+                mm(ap(y, 256 * j, 256 * j + 256), ap("SELG", 128 * gg, 128 * gg + 128, 1, 0, 8), ap("ABT", 0, 256, 1, 0, 8), False, j == 1)
+            for j in range(2):
+                gg = 2 * b + j
+                act(ap("AB", 256 * gg, 256 * gg + 256), ap(y, 256 * j, 256 * j + 256), F.Abs, bias=ap("S8", gg, gg + 1), scale=-2.0)
+                ts(ap("EQ", 256 * gg, 256 * gg + 256), ap("AB", 256 * gg, 256 * gg + 256), ap("HH", gg, gg + 1), A.is_equal)
+
+    def acts(t):
+        for gg in range(8):
+            for x in range(2):
+                c = 256 * gg + 128 * x
+                mm(ap("M", 40 + gg, 41 + gg), ap("EQ", c, c + 128), ap("ASK", gg, gg + 1), x == 0, x == 1)
+        tt(ap("ACT", 0, 8), ap("ASK", 0, 8), ap("M", 40, 48), A.is_gt)
+        nl = 24 if t % 2 == 0 else 16
+        tt(ap("AC", 0, 128), ind(ap("ACT", 0, 8), ap("OC", 0, 8)), ap("MK", 0, 128), A.mult)
+        mm(ap("M", 48, 48 + nl), ap("AC", 0, 128), ap("BK3", 0, nl))
+        if t < NV - 1:
+            for gg in range(8):
+                mm(ap("M", 72, 73), ap("ONE", 0, 128), ap("ACT", gg, gg + 1), gg == 0, gg == 7)
+        tt(ap("LT", 0, nl), ap("PRE", 0, nl), ap("M", 48, 48 + nl), A.mult)
+        if t < NV - 1:
+            cp(ap("AI", 0, 1), ap("M", 72, 73))
+            ts(ap("AJ", 0, 1), ap("AI", 0, 1), 1, A.bitwise_and)
+            ks = ap("KS", 4 * t, 4 * t + 4)
+            cp(ap("KT", 0, 1), ap("AJ", 0, 1))
+            ts(ap("KT", 4, 8), ap("KA", 0, 4), ap("KT", 0, 1), A.mult)
+            tt(ks, ap("K0", 0, 4), ap("KT", 4, 8), A.subtract)
+            sends["ks", t + 1] = send([(1, ap("KR", 4 * t + 4, 4 * t + 8), ks, "ks%d" % (t + 1), 0)], [ks])
+        tt(ap("LU", 0, nl), ap("LT", 0, nl), ap("DUM", 0, nl), A.add)
+        cp(ap("LS", 0, nl), ap("LU", 0, nl))
+
+    def split_rows(t):
+        eb = ap("EB", 0, 128)
+        mm(ap("M2", 136, 264), ap("GE", 0, 128), ap("IB", 0, 128))
+        mm(ap("M2", 264, 392), ap("GE", 0, 128), ap("IB", 0, 128), True, False)
+        mm(ap("M2", 264, 392), ap("GE", 128, 256), ap("IB", 0, 128), False, True)
+        ts(ap("ST", 0, 128), ap("M2", 264, 392), 0.0, A.is_equal)
+        tt(ap("YS", 256, 384), eb, ap("M2", 136, 264), A.mult)
+        mm(ap("M2", 264, 392), ap("TRC", 0, 128), ap("ST", 0, 128))
+        tt(ap("W1", 0, 128), eb, ap("M2", 264, 392), A.add)
+        tt(ap("U", 0, 128), ap("W1", 0, 128), ap("ST", 0, 128), A.mult)
+        act(ap("U", 128, 256), ap("U", 0, 128))
+        act(ap("U", 256, 512), ap("U", 0, 256))
+        tt(ap("W2", 0, 128), eb, ap("YS", 256, 384), A.subtract)
+
+    def place_rows(t):
+        for b in range(4):
+            y = "Y%d" % (b % 2)
+            for j in range(4):
+                c = 512 * b + 128 * j
+                mm(ap(y, 128 * j, 128 * j + 128), ap("PBC", c, c + 128), ap("FR", 0, 128))
+            tt(ap("MM", 512 * b, 512 * b + 512), ap("U", 0, 512), ap(y, 0, 512), A.max)
+            for j in range(4):
+                c, i = 512 * b + 128 * j, 4 * b + j + 1
+                mm(ap("M2", i, i + 113, 16), ap("MM", c, c + 128), ap("BKF", 0, 8))
+        cp(ap("GI", 1, 129), ap("M2", 1, 129))
+        tt(ap("GD", 0, 128), ap("GI", 0, 128), ap("GI", 1, 129), A.subtract)
+        ts(ap("GA", 0, 128), ap("GD", 0, 128), int(CC) - 1, A.bitwise_and)
+        cp(ap("VAL", 0, 128), ap("GA", 0, 128))
+        ms(ap("VAL", 0, 128, 16), 0.0)
+        mm(ap("M2", 264, 392), ap("VAL", 0, 128), ap("IF", 0, 128))
+        tt(ap("W6", 0, 128), ap("MM", 1920, 2048), ap("U", 0, 128), A.is_le)
+        tt(ap("W6", 0, 128), ap("ST", 0, 128), ap("W6", 0, 128), A.is_le)
+        tt(ap("W3", 0, 128), ap("W5", 0, 128), ap("NC", 64 * t, 64 * t + 128), A.mult)
+        tt(ap("W4", 0, 128), ap("W3", 0, 128), ap("EA", 0, 128), A.add)
+        tt(ap("YS", 0, 128), ap("W4", 0, 128), ap("M2", 264, 392), A.add)
+        tt(ap("YS", 128, 256), ap("W2", 0, 128), ap("W6", 0, 128), A.mult)
+
+    def move_down(t):
+        act(ap("AA", 0, 128), ind(ap("GF", 240 * t, 240 * t + 40), ap("O5", 0, 8)))
+        mm(ap("M2", 136, 264), ap("AA", 0, 128), ap("IF", 0, 128))
+        tt(ap("W1", 0, 128), ap("EA", 0, 128), ap("M2", 136, 264), A.not_equal)
+        tt(ap("W2", 0, 128), ap("W5", 0, 128), ap("M2", 136, 264), A.mult)
+        tt(ap("YS", 0, 128), ap("W1", 0, 128), ap("EA", 0, 128), A.mult)
+        tt(ap("YS", 128, 256), ap("W2", 0, 128), ap("EB", 0, 128), A.add)
+
+    def write_back(t):
+        cp(ind(ap("D", 0, 2304), ap("LS", 0, 16)), ap("YS", 0, 256))
+        if t % 2 == 0:
+            n0, ln = 1792 + 64 * t, ap("LS", 16, 24)
+            act(ap("D", n0, n0 + 128), ind(ap("YS", 256, 512), ln))
+            for c in (0, 4096, 8192):
+                tt(ind(ap("RW", c, c + 2304), ap("LS", 8, 16)), ap("RB", 0, 128), ap("XS", 0, 128), A.add)
+                if c < 8192:
+                    act(ap("RW", c + n0, c + n0 + 128), ind(ap("HB", 0, 256), ln))
+                    r = 128 * (c // 4096)
+                    act(ap("RW", c + 2176, c + 2304), ap("RSV", r, r + 128))
+
+    prep(0)
+    for t in range(NV):
+        steps = [(start_nodes, 0), (start_nodes, 1), (guards, 0), (gather, 2, 0), (gather, 2, 1), (tail, 2, 0), (guards, 1),
+                 (gather, 1, 0), (tail, 2, 1), (gather, 1, 1), (prep_next,), (tail, 1, 0), (tail, 1, 1), (gather, 0, 1)]
+        if t % 2:
+            steps += [(gather, 0, 0), (early3,), (tail, 0, 0), (source,), (final_guards, 0), (move_down,), (meet,), (acts,)]
+        else:
+            steps += [[(early3,), (source,), (meet,), (acts,), (gather, 0, 0), (tail, 0, 0)],
+                      [(gather, 0, 0), (early3,), (source,), (meet,), (tail, 0, 0), (acts,)],
+                      [(gather, 0, 0), (early3,), (source,), (meet,), (acts,), (tail, 0, 0)],
+                      [(early3,), (source,), (meet,), (gather, 0, 0), (tail, 0, 0), (acts,)]][EVEN]
+            steps += [(final_guards, 0), (split_rows,), (place_rows,)]
+        steps += [(tail, 0, 1), (final_guards, 1), (write_back,)]
+        for s_ in steps:
+            stage[0] += 1
+            stage[1] = s_[-1] if len(s_) > 1 else 0
+            if t or s_[0] is not guards:
+                s_[0](t, *s_[1:])
+        if t == 2:
+            store("y", T.yr[:, :], ap("RW", 4096, 6144), 4000.0)
+    store("y", T.yn[:, 0:1024], ap("D", 0, 1024), 4000.0)
+    store("s", T.yn[:, 1024:2048], ap("D", 1024, 2048), 4000.0)
+    for k in range(3):
+        for h in range(2):
+            c, b = 256 * k + 128 * h, 720 + 120 * h + 40 * k
+            mm(ap("Y%d" % (c // 512), c % 512, c % 512 + 128, 1, 0, 8), ap("GF", b + 4, b + 40, 5), ap("IF", 0, 128))
+    act(ap("YG", 0, 512, 1, 0, 8), ap("Y0", 0, 512, 1, 0, 8))
+    act(ap("YG", 512, 768, 1, 0, 8), ap("Y1", 0, 256, 1, 0, 8))
+    store("y", T.yg[:, :], ap("YG", 0, 768, 1, 0, 8), 2000.0)
+
+    n = len(ops)
+    succ = [[] for _ in range(n)]
+    edge = [{} for _ in range(n)]
+    for k, o in enumerate(ops):
+        for j, wt in o["dep"].items():
+            edge[k][j] = ops[j]["lat"] + (LAT if wt else 0.0)
+        for j, l in o["soft"].items():
+            edge[k][j] = max(edge[k].get(j, 0.0), l)
+        for j in edge[k]:
+            succ[j].append(k)
+    level = [0.0] * n
+    for k in range(n - 1, -1, -1):
+        level[k] = ops[k]["cost"] + max([ops[k]["lat"]] + [edge[j][k] + level[j] for j in succ[k]])
+    cost = [o["cost"] for o in ops]
+    engs = [o["eng"] for o in ops]
+    tails = [o["lat"] for o in ops]
+    fwd = [list(edge[k].items()) for k in range(n)]
+    bwd = [[(j, edge[j][k]) for j in succ[k]] for k in range(n)]
+
+    def place(seq, pre, first):
+        busy = {e: ([], []) for e in "vspgy"}
+        at = [0.0] * n
+        for k in seq:
+            t0 = first[k]
+            for j, l in pre[k]:
+                t0 = max(t0, at[j] + cost[j] + l)
+            st, en = busy[engs[k]]
+            lo, hi = 0, len(en)
+            while lo < hi:
+                mid = (lo + hi) // 2
+                if en[mid] <= t0:
+                    lo = mid + 1
+                else:
+                    hi = mid
+            while lo < len(st) and st[lo] < t0 + cost[k]:
+                t0 = max(t0, en[lo])
+                lo += 1
+            st.insert(lo, t0)
+            en.insert(lo, t0 + cost[k])
+            at[k] = t0
+        return at
+
+    if "order" not in PLAN:
+        rng = np.random.default_rng(1)
+        zero = [0.0] * n
+        best = None
+        for rnd in range(ROUNDS):
+            if rnd < len(LEADS):
+                key = [-level[k] - LEADS[rnd] * ops[k]["half"] for k in range(n)]
+            else:
+                st_ = rng.normal(0.0, SHAKE * 3 * (rnd % 2), stage[0] + 1)
+                key = [best[1][k] + float(x) + float(st_[ops[k]["stage"]]) for k, x in enumerate(rng.normal(0.0, SHAKE, n))]
+            for k in range(n):
+                for j, l in fwd[k]:
+                    key[k] = max(key[k], key[j] + 0.001)
+            seq = sorted(range(n), key=lambda k: key[k])
+            for it in range(PASSES):
+                at = place(seq, fwd, zero)
+                end = max(at[k] + cost[k] + tails[k] for k in range(n))
+                if best is None or end < best[0]:
+                    best = (end, at)
+                back = place(sorted(range(n), key=lambda k: (-at[k] - cost[k], -k)), bwd, tails)
+                seq = sorted(range(n), key=lambda k: (-back[k] - cost[k], k))
+        PLAN["order"] = sorted(range(n), key=lambda k: (best[1][k], k))
+        PLAN["at"], PLAN["fin"] = best[1], best[0]
+    order, fin = PLAN["order"], PLAN["fin"]
+    for k in range(n):
+        ops[k]["at"] = PLAN["at"][k]
+
+    pos = {k: i for i, k in enumerate(order)}
+    seen = {}
+    need = [[] for _ in range(n)]
+    marked = set()
+    for k in order:
+        e = ops[k]["eng"]
+        best = {}
+        for j, wt in ops[k]["dep"].items():
+            if not wt:
+                continue
+            key = ops[j]["sem"] or "q" + ops[j]["eng"]
+            marked.add(j)
+            if key not in best or pos[j] > pos[best[key]]:
+                best[key] = j
+        for key, j in best.items():
+            if seen.get((e, key), -1) < pos[j]:
+                seen[(e, key)] = pos[j]
+                need[k].append((key, j))
+                marked.add(j)
+    count = {"qv": 0, "qs": 0, "qp": 0, "qg": 0}
+    val = {}
+    queue = {"v": g.vector, "s": g.scalar, "p": g.tensor, "g": g, "y": g.sync}
+    got = set()
+    for k in order:
+        o = ops[k]
+        q = queue[o["eng"]]
+        for key, j in need[k]:
+            q.wait_ge(T.sem[key], val[j])
+        for key, c in o["waits"]:
+            if (o["eng"], key) not in got:
+                got.add((o["eng"], key))
+                q.wait_ge(T.sem[key], c)
+        ins = o["fn"]()
+        if o["sem"]:
+            ins.then_inc(T.sem[o["sem"]], 16)
+            val[k] = 16
+        elif k in marked:
+            count["q" + o["eng"]] += 1
+            val[k] = count["q" + o["eng"]]
+            ins.then_inc(T.sem["q" + o["eng"]], 1)
+    g.wait_ge(T.sem["sent"], sent[0])
+    for s in outs_:
+        g.wait_ge(T.sem[s], 16)
+    return {"ops": ops, "order": order, "fin": fin, "level": level, "edge": edge, "succ": succ}

@@ -11,8 +11,8 @@ f32, bf, i32, u16, f16 = "float32", "bfloat16", "int32", "uint16", "float16"
 SB = {
     "RW": (10496, bf), "RSV": (256, bf), "D": (2304, f32), "NDI": (1792, i32),
     "XZ": (1024, bf), "VSO": (64, i32), "VSR": (64, i32), "XT": (1024, bf), "L2": (64, u16),
-    "GF": (960, f32), "GR": (960, f32), "KS": (16, f32), "KR": (16, f32), "K0": (4, f32),
-    "KA": (4, f32), "KT": (8, f32), "NIB": (128, bf), "HB": (256, bf), "IB": (128, bf), "IF": (128, f32), "ONE": (128, bf), "RBIG": (512, bf),
+    "GF": (960, f32), "GR": (960, f32), "KS": (32, f32), "KR": (32, f32), "K0": (8, f32),
+    "KA": (8, f32), "KT": (16, f32), "NIB": (128, bf), "R0": (16, bf), "HB": (256, bf), "IB": (128, bf), "IF": (128, f32), "ONE": (128, bf), "RBIG": (512, bf),
     "BK3": (24, bf), "BKF": (8, f32), "SC": (24, bf), "SCT": (64, bf), "SX": (512, bf),
     "TRX": (128, bf), "TRC": (128, bf), "PBC": (2048, bf), "TRL": (512, bf), "SELG": (1024, bf),
     "CK": (768, bf), "RS": (384, f32), "MKI": (384, i32), "MKJ": (384, i32), "MK": (384, f32), "NMK": (16, f32),
@@ -28,7 +28,7 @@ SB = {
     "NQ": (8, f32), "Q8": (8, f32), "ASK": (16, bf), "ACT": (16, bf), "ABT": (256, f16),
     "AB": (2048, f32), "EQ": (2048, bf), "AC": (128, bf), "LT": (24, f32), "LU": (24, f32), "LS": (24, u16),
     "AI": (4, i32), "AJ": (4, i32), "YS": (512, f32), "GE": (256, bf), "ST": (128, bf),
-    "W1": (128, f32), "W2": (128, f32), "W3": (128, f32), "W4": (128, f32), "W5": (128, bf), "W6": (128, bf),
+    "W1": (128, f32), "W2": (128, f32), "W3": (128, f32), "W4": (128, f32), "W5": (128, bf), "W6": (128, f32),
     "U": (512, f32), "MM": (2048, f32), "GI": (136, i32), "GD": (128, i32), "GA": (128, i32), "VAL": (128, f32),
     "RB": (256, bf), "XS": (256, bf), "YG": (768, f32),
 }
@@ -37,19 +37,19 @@ SCRATCH = {k: ("sbuf", [128, n], d) for k, (n, d) in SB.items()}
 SCRATCH.update({k: ("psum", [128, 512], f32) for k in PS})
 DMAS = ["ld%d" % i for i in range(8)] + ["st%d" % i for i in range(6)]
 SEMAPHORES = ["qv", "qs", "qp", "qg", "sent"] + DMAS + ["%s%d" % (a, t) for a in ("in", "ga", "gb", "ks") for t in (1, 2, 3)]
-SQS = ((), (0, 1, 2), (0, 1, 2, 3))
-PAT = ((0, 2), (0, 2), (0, 2))
-CHUNKS = ((0, 512), (512, 1024), (1024, 1536), (1536, 2048))
-VG = (((), ()), ((), ()), ((), ()))
+CHUNKS = (((0, 512), (512, 1024), (1024, 1536), (1536, 2048)), ((0, 1024), (1024, 1536), (1536, 2048)), ((0, 1024), (1024, 2048)))
+CFG = [(1, 1, 0, 0, 0), (4, 0, 0, 0, 0)] * 9 + [(2, 1, 0, 0, 0), (3, 1, 0, 0, 0)] * 3
 LEADS = [1000.0 * i for i in range(-2, 14)]
+SHARE = {1: (0, 4), 2: (4, 6), 3: (6, 8)}
+OTHERS = [(1.1, 2.2, 0.87, 200.0, 1.6), (1.3, 3.0, 0.9, 120.0, 2.0), (2.0, 5.0, 1.0, 150.0, 1.0)]
+WINDOW = 8000.0
 EVEN = 3
-ROUNDS, PASSES, SHAKE = 300, 2, 100.0
+ROUNDS, PASSES, SHAKE = 2600, 2, 200.0
 PLAN = {}
-PEN_S = False
 
-GATH, SCAT = 1.56, 3.8
+GATH, SCAT = 1.35, 3.4
 PE0, PE1 = 5.0, 0.5
-LAT = 100.0
+LAT = 150.0
 
 
 def ap(name, c0, c1, st=1, p0=0, p1=128):
@@ -133,7 +133,9 @@ def rank_program(g, core, T, topo):
                 last_r.setdefault(a[0], []).append((a[1], a[2], k))
         soft = dict(after)
         ops.append({"eng": eng, "fn": fn, "dep": dep, "cost": cost, "waits": list(waits), "soft": soft, "sem": sem, "lat": lat, "out": wr[:1],
-                    "half": stage[1], "stage": stage[0]})
+                    "half": stage[1], "stage": stage[0],
+                    "ns": width(outs[0]) if outs and outs[0][0] == "ind" else 0,
+                    "ng": width(outs[0]) if outs and ins and isinstance(ins[0], tuple) and ins[0][0] == "ind" else 0})
         return k
 
     def vcost(out, ins, rate):
@@ -187,8 +189,8 @@ def rank_program(g, core, T, topo):
             fn = lambda: g.iota(real(out), pat, base, cm, allow_small_or_imprecise_dtypes=True)
         return op("g", fn, [out], [], 150.0 + 2 * width(out))
 
-    def sel(out, a, pat, cmp, base, cm):
-        return op("g", lambda: g.affine_select(real(out), real(a), pat, cmp, 0.0, base, cm), [out], [a], 200.0 + 2 * width(out))
+    def sel(out, a, pat, cmp, base, cm, fill=0.0):
+        return op("g", lambda: g.affine_select(real(out), real(a), pat, cmp, fill, base, cm), [out], [a], 200.0 + 2 * width(out))
 
     nd_ = [0, 0]
     outs_ = []
@@ -220,13 +222,13 @@ def rank_program(g, core, T, topo):
             dst = T.cores[(rank + dt_) % N]
             rid, pid, _ = topo.addr(dst)
             trs.append((dst, rid, pid, o, s, sem, e0))
-        sent[0] += 2 * len(pairs)
+        sent[0] += 8
         def call():
             if len(trs) == 1:
                 dst, rid, pid, o, s, sem, e0 = trs[0]
-                g.remote_dma(real(o), real(s), T.sem[sem], T.sem["sent"], pid, rid, emask(dst, e0, e0 + 2))
+                g.remote_dma(real(o), real(s), T.sem[sem], T.sem["sent"], pid, rid, emask(dst, 0, 8))
             else:
-                g.remote_dma_fused([RemoteDMATransfer(dst_ids=[DstId(rid=rid, pnc=pid)], dma_engine_mask=emask(dst, e0, e0 + 2),
+                g.remote_dma_fused([RemoteDMATransfer(dst_ids=[DstId(rid=rid, pnc=pid)], dma_engine_mask=emask(dst, *e0),
                                                       remote_sem=T.sem[sem], src=real(s), dst=real(o))
                                     for dst, rid, pid, o, s, sem, e0 in trs], local_sem=T.sem["sent"])
             return None
@@ -263,37 +265,36 @@ def rank_program(g, core, T, topo):
     iota(ap("DU0", 0, 16), [[16, 16]], 2048, 0)
     iota(ap("DU0", 16, 24), [[16, 8]], 128, 0)
     ts(ap("DUM", 0, 24), ap("DU0", 0, 24), ap("PM", 0, 1), A.add)
-    ms(ap("CK", 0, 768, 1, 0, 64), 0.0)
+    iota(ap("CK", 0, 768), [[0, 768]], 0, 0)
     ms(ap("CK", 128, 384, 1, 0, 32), BIG / 32)
     ms(ap("CK", 0, 512, 1, 32, 64), 64.0)
-    ms(ap("RS", 0, 384), 0.0)
+    iota(ap("RS", 0, 384), [[0, 384]], 0, 0)
     ms(ap("RS", 0, 384, 16), float(2 ** 30))
     ms(ap("D0", 0, 240), 1.0)
     ms(ap("D0", 0, 240, 5), 0.0)
     ms(ap("D1", 0, 240), 0.0)
     ms(ap("DH", 0, 40), 0.0)
     ms(ap("THR", 0, 48), 2 ** 25)
-    ms(ap("K0", 0, 4), 12.0)
     ms(ap("GI", 0, 8), 0)
     iota(ap("RW", 10240, 10496), [[0, 256]], 0, 0)
     iota(ap("D", 1792, 2304), [[0, 512]], 0, 0)
     iota(ap("YS", 384, 512), [[0, 128]], 0, 0)
     ms(ap("PRE", 16, 24), -128.0)
-    ms(ap("KA", 0, 4), 1.0)
-    for j, sq in enumerate(SQS):
-        for q in sq:
-            ms(ap("KA", j + 1, j + 2, 1, 32 * q, 32 * q + 32), 2.0)
-            ms(ap("K0", j + 1, j + 2, 1, 32 * q, 32 * q + 32), 8.0)
+    for name, plain, sums in (("K0", 12, 8.0), ("KA", 1, 2.0)):
+        iota(ap(name, 0, 8), [[0, 8]], plain, 0)
+        sel(ap(name, 0, 8), ap(name, 0, 8), [[-32, 8]], A.is_ge, 0, 1, sums)
     ts(ap("NIB", 0, 128), ap("IB", 0, 128), -1.0, A.mult)
     cp(ap("D", 0, 896), ap("NDI", 0, 896))
     cp(ap("D", 896, 1792), ap("NDI", 896, 1792))
     act(ap("RW", 4096, 6144), ap("RW", 0, 2048))
     cp(ap("RW", 8192, 10240), ap("RW", 0, 2048))
-    ms(ap("RW", 0, 1), 300.0)
+    cp(ap("R0", 0, 1), ap("RW", 0, 1))
+    for c in (0, 4096, 8192):
+        ms(ap("RW", c, c + 1), 300.0)
     act(ap("RSV", 0, 128), ap("RW", 2176, 2304))
     act(ap("RSV", 128, 256), ap("RW", 6272, 6400))
-    sz = send([(t, ap("XZ", 256 * t, 256 * t + 256), ap("XZ", 0, 256), "in%d" % t, 2 * t - 2) for t in (1, 2, 3)], [ap("XZ", 0, 256)])
-    sv = send([(t, ap("VSR", 16 * t, 16 * t + 16), ap("VSO", 16 * t, 16 * t + 16), "in%d" % t, 2 * t - 2) for t in (1, 2, 3)], [ap("VSO", 0, 64)])
+    sz = send([(t, ap("XZ", 256 * t, 256 * t + 256), ap("XZ", 0, 256), "in%d" % t, SHARE[t]) for t in (1, 2, 3)], [ap("XZ", 0, 256)])
+    sv = send([(t, ap("VSR", 16 * t, 16 * t + 16), ap("VSO", 16 * t, 16 * t + 16), "in%d" % t, SHARE[t]) for t in (1, 2, 3)], [ap("VSO", 0, 64)])
     for j, t in enumerate((0, 2)):
         cp(ap("SCT", 32 * j, 32 * j + 8), ap("SC", 0, 8))
         sel(ap("SCT", 32 * j + 8, 32 * j + 24), ap("ONE", 0, 16), [[-8, 2], [-16, 8]], A.is_equal, -t, 1)
@@ -327,14 +328,14 @@ def rank_program(g, core, T, topo):
         if t == 0:
             return {}
         if kind == "in":
-            return {"waits": [("in%d" % t, 4)], "after": {sz: 4000.0, sv: 4000.0}}
-        return {"waits": [("%s%d" % (kind, t), 2)], "after": {sends[kind, t]: 3500.0}}
+            return {"waits": [("in%d" % t, 2 * (SHARE[t][1] - SHARE[t][0]))], "after": {sz: 4000.0, sv: 4000.0}}
+        return {"waits": [("%s%d" % (kind, t), 8)], "after": {sends[kind, t]: 3000.0}}
 
     def xs(t, h):
         return ap("XZ", 256 * t + 128 * h, 256 * t + 128 * h + 128)
 
     def kcol(t, j=0):
-        return ap("K0", j, j + 1) if t == 0 else ap("KR", 4 * t + j, 4 * t + j + 1)
+        return ap("K0", j, j + 1) if t == 0 else ap("KR", 8 * t + j, 8 * t + j + 1)
 
     def prep(t):
         for h in range(2):
@@ -382,12 +383,18 @@ def rank_program(g, core, T, topo):
     def gather(t, s, h):
         o = 128 * h
         e = ap("EU", o, o + 128)
-        cp(e, ind(ap("D", 0, 2048), vlist(t, s, h)))
-        sq = SQS[PAT[s][h]]
-        for c0, c1 in CHUNKS:
-            (cp if c0 // 512 in VG[s][h] else act)(ap("R", 2048 * h + c0, 2048 * h + c1), ind(ap("RW", 0, 10240), ap("EU", o + c0 // 16, o + c1 // 16)))
-        ts(ap("FA", o, o + 128), e, 4096.0, A.is_ge)
-        if s:
+        whole = s == 2 or (s == 0 and h == 0 and t % 2 == 0)
+        if whole:
+            cp(e, ind(ap("D", 0, 2048), vlist(t, s, h)))
+        else:
+            ts(e, ind(ap("D", 0, 2048), vlist(t, s, h)), 4096.0 * (s + 1), A.min)
+        ns, vg, ch = CFG[6 * t + 2 * s + h][:3]
+        sq = range(ns)
+        for c0, c1 in CHUNKS[ch]:
+            (cp if c0 >= 2048 - 512 * vg else act)(ap("R", 2048 * h + c0, 2048 * h + c1), ind(ap("RW", 0, 10240), ap("EU", o + c0 // 16, o + c1 // 16)))
+        if s or whole:
+            ts(ap("FA", o, o + 128), e, 4096.0, A.is_ge)
+        if s == 2:
             ts(ap("FB", o, o + 128), e, 8192.0, A.is_ge)
         for k in range(s + 1):
             ts(ap("FW", 384 * h + 128 * k, 384 * h + 128 * k + 128), e, -4096.0 * k - 2048.0, A.add)
@@ -404,14 +411,15 @@ def rank_program(g, core, T, topo):
     def tail(t, s, h):
         o, n, w, W = 128 * h, 128 * (s + 1), 24 * h, 8 * (s + 1)
         cut = s == 0 and h == 0 and t % 2 == 0
-        K, C, kc = KB[h], CB[h], kcol(t, 1 + PAT[s][h])
+        K, C, kc = KB[h], CB[h], kcol(t, CFG[6 * t + 2 * s + h][0])
         if cut:
             mm(ap(K, 0, 384), ap("ONE", 0, 128, 1, 0, 64), ap("CK", 384, 768, 1, 0, 64), True, False)
             mm(ap(K, 128, 384), xs(t, 0), ap("SX", 128 * t, 128 * t + 256), False, False, **arrived("in", t))
         else:
             mm(ap(K, 0, n), ap("ONE", 0, 128, 1, 0, 64), ap("CK", 0, n, 1, 0, 64), True, False)
-        mm(ap(K, 0, n), ap("FA", o, o + 128), ap("RBIG", 128, 128 + n), False, False)
-        if s:
+        if s or cut:
+            mm(ap(K, 0, n), ap("FA", o, o + 128), ap("RBIG", 128, 128 + n), False, False)
+        if s == 2:
             mm(ap(K, 128, n), ap("FB", o, o + 128), ap("RBIG", 128, n), False, False)
         for k in range(s + 1):
             mm(ap(K, 128 * k, 128 * k + 128), ap("FW", 384 * h + 128 * k, 384 * h + 128 * k + 128), ap("IB", 0, 128), False, False)
@@ -421,9 +429,10 @@ def rank_program(g, core, T, topo):
                 mm(ap(K, i, 384, 16), r, ap("SCT", 16 * t, 16 * t + 24), False, False)
             else:
                 mm(ap(K, i, n, 16), r, ap("SC", 0, W), False, False)
-        for i in range(16):
-            mm(ap(C, i, 128, 16), ap("CMP", 2048 * h + i, 2048 * h + 2048, 16), ap("BK3", 0, 8))
-        if PEN_S:
+        for p0, p1 in ((0, 96), (96, 128)) if CFG[6 * t + 2 * s + h][4] else ((0, 128),):
+            for i in range(16):
+                mm(ap(C, i, 128, 16, p0, p1), ap("CMP", 2048 * h + 16 * p0 + i, 2048 * h + 16 * p1, 16), ap("BK3", 0, 8))
+        if CFG[6 * t + 2 * s + h][3]:
             act(ap("PEN", o, o + 128), ap(C, 0, 128), F.Relu, bias=kc, scale=-1.0, **arrived("ks", t))
         else:
             ts(ap("PEN", o, o + 128), ap(C, 0, 128), kc, A.is_lt, **arrived("ks", t))
@@ -431,7 +440,7 @@ def rank_program(g, core, T, topo):
             mm(ap(K, 128 * k, 128 * k + 128), ap("RBIG", 128, 256), ap("PEN", o, o + 128), False, k == s)
         scan(ap("SCN", 384 * h, 384 * h + n), ap("RS", 0, n), ap(K, 0, n), A.add, A.min)
         if cut:
-            ts(ap("GE", 0, 256), ap(K, 128, 384), 0.0, A.is_ge)
+            act(ap("GE", 0, 256), ap(K, 128, 384), F.Sign, bias=0.5)
         mi, lo = ap("MI", w, w + W), ap("LO", w, w + W)
         tt(mi, ap("SCN", 384 * h + 15, 384 * h + n, 16), ap("THR", w, w + W), A.min)
         ts(lo, mi, 4095, A.bitwise_and)
@@ -466,6 +475,8 @@ def rank_program(g, core, T, topo):
         tt(ap("DH", 2, 40, 5), v2, v1, A.subtract)
         tt(ap("DH", 3, 40, 5), v1, v0, A.subtract)
         cp(ap("DH", 4, 40, 5), v0)
+        if t % 2:
+            mm(ap("M", 256, 384, 1, 0, 8), v0, ap("IF", 0, 128))
         act(ap("EB", 0, 128), ind(ap("D", 0, 2048), vlist(t, 0, 0)))
         if t % 2 == 0:
             lb = ind(ap("RW", 0, 2048), vlist(t, 0, 0))
@@ -481,7 +492,8 @@ def rank_program(g, core, T, topo):
         scan(ap("HS", 0, 40), ap("D0", 40 * k, 40 * k + 40), ap("DH", 0, 40), A.mult, A.add)
         tt(ap("AL", 0, 128), ind(ap("HS", 0, 40), ap("O5", 0, 8)), ap("MK", 0, 128), A.mult)
         mm(ap("M", 128, 256, 1, 0, 8), av, ap("IF", 0, 128))
-        mm(ap("M", 256, 384, 1, 0, 8), v0, ap("IF", 0, 128))
+        if k:
+            mm(ap("M", 256, 384, 1, 0, 8), v0, ap("IF", 0, 128))
         cp(ap("ABT", 0, 256, 1, 0, 8), ap("M", 128, 384, 1, 0, 8))
         mm(ap("M", 80, 88), ap("AL", 0, 128), ap("BK3", 0, 8))
         cp(ap("LA", 0, 8), ap("M", 80, 88))
@@ -526,11 +538,11 @@ def rank_program(g, core, T, topo):
         if t < NV - 1:
             cp(ap("AI", 0, 1), ap("M", 72, 73))
             ts(ap("AJ", 0, 1), ap("AI", 0, 1), 1, A.bitwise_and)
-            ks = ap("KS", 4 * t, 4 * t + 4)
+            ks = ap("KS", 8 * t, 8 * t + 8)
             cp(ap("KT", 0, 1), ap("AJ", 0, 1))
-            ts(ap("KT", 4, 8), ap("KA", 0, 4), ap("KT", 0, 1), A.mult)
-            tt(ks, ap("K0", 0, 4), ap("KT", 4, 8), A.subtract)
-            sends["ks", t + 1] = send([(1, ap("KR", 4 * t + 4, 4 * t + 8), ks, "ks%d" % (t + 1), 0)], [ks])
+            ts(ap("KT", 8, 16), ap("KA", 0, 8), ap("KT", 0, 1), A.mult)
+            tt(ks, ap("K0", 0, 8), ap("KT", 8, 16), A.subtract)
+            sends["ks", t + 1] = send([(1, ap("KR", 8 * t + 8, 8 * t + 16), ks, "ks%d" % (t + 1), 0)], [ks])
         tt(ap("LU", 0, nl), ap("LT", 0, nl), ap("DUM", 0, nl), A.add)
         cp(ap("LS", 0, nl), ap("LU", 0, nl))
 
@@ -539,14 +551,14 @@ def rank_program(g, core, T, topo):
         mm(ap("M2", 136, 264), ap("GE", 0, 128), ap("IB", 0, 128))
         mm(ap("M2", 264, 392), ap("GE", 0, 128), ap("IB", 0, 128), True, False)
         mm(ap("M2", 264, 392), ap("GE", 128, 256), ap("IB", 0, 128), False, True)
-        ts(ap("ST", 0, 128), ap("M2", 264, 392), 0.0, A.is_equal)
+        ts(ap("ST", 0, 128), ap("M2", 264, 392), -2.0, A.is_equal)
         tt(ap("YS", 256, 384), eb, ap("M2", 136, 264), A.mult)
         mm(ap("M2", 264, 392), ap("TRC", 0, 128), ap("ST", 0, 128))
         tt(ap("W1", 0, 128), eb, ap("M2", 264, 392), A.add)
         tt(ap("U", 0, 128), ap("W1", 0, 128), ap("ST", 0, 128), A.mult)
         act(ap("U", 128, 256), ap("U", 0, 128))
         act(ap("U", 256, 512), ap("U", 0, 256))
-        tt(ap("W2", 0, 128), eb, ap("YS", 256, 384), A.subtract)
+        ts(ap("W2", 0, 128), ap("YS", 256, 384), 0.0, A.min, -1.0, A.mult)
 
     def place_rows(t):
         for b in range(4):
@@ -554,7 +566,8 @@ def rank_program(g, core, T, topo):
             for j in range(4):
                 c = 512 * b + 128 * j
                 mm(ap(y, 128 * j, 128 * j + 128), ap("PBC", c, c + 128), ap("FR", 0, 128))
-            tt(ap("MM", 512 * b, 512 * b + 512), ap("U", 0, 512), ap(y, 0, 512), A.max)
+            for c0, c1, u in ((0, 128, 0), (128, 256, 0), (256, 512, 0)) if b == 0 else ((0, 512, 0),):
+                tt(ap("MM", 512 * b + c0, 512 * b + c1), ap("U", u, u + c1 - c0), ap(y, c0, c1), A.max)
             for j in range(4):
                 c, i = 512 * b + 128 * j, 4 * b + j + 1
                 mm(ap("M2", i, i + 113, 16), ap("MM", c, c + 128), ap("BKF", 0, 8))
@@ -567,23 +580,21 @@ def rank_program(g, core, T, topo):
         tt(ap("W6", 0, 128), ap("MM", 1920, 2048), ap("U", 0, 128), A.is_le)
         tt(ap("W6", 0, 128), ap("ST", 0, 128), ap("W6", 0, 128), A.is_le)
         tt(ap("W3", 0, 128), ap("W5", 0, 128), ap("NC", 64 * t, 64 * t + 128), A.mult)
-        tt(ap("W4", 0, 128), ap("W3", 0, 128), ap("EA", 0, 128), A.add)
-        tt(ap("YS", 0, 128), ap("W4", 0, 128), ap("M2", 264, 392), A.add)
-        tt(ap("YS", 128, 256), ap("W2", 0, 128), ap("W6", 0, 128), A.mult)
+        tt(ap("W1", 0, 128), ap("W3", 0, 128), ap("M2", 264, 392), A.add)
 
     def move_down(t):
         act(ap("AA", 0, 128), ind(ap("GF", 240 * t, 240 * t + 40), ap("O5", 0, 8)))
         mm(ap("M2", 136, 264), ap("AA", 0, 128), ap("IF", 0, 128))
         tt(ap("W1", 0, 128), ap("EA", 0, 128), ap("M2", 136, 264), A.not_equal)
         tt(ap("W2", 0, 128), ap("W5", 0, 128), ap("M2", 136, 264), A.mult)
-        tt(ap("YS", 0, 128), ap("W1", 0, 128), ap("EA", 0, 128), A.mult)
-        tt(ap("YS", 128, 256), ap("W2", 0, 128), ap("EB", 0, 128), A.add)
 
     def write_back(t):
-        cp(ind(ap("D", 0, 2304), ap("LS", 0, 16)), ap("YS", 0, 256))
+        even = t % 2 == 0
+        tt(ind(ap("D", 0, 2304), ap("LS", 8, 16)), ap("W2", 0, 128), ap("W6" if even else "EB", 0, 128), A.mult if even else A.add)
+        tt(ind(ap("D", 0, 2304), ap("LS", 0, 8)), ap("W1", 0, 128), ap("EA", 0, 128), A.add if even else A.mult)
         if t % 2 == 0:
             n0, ln = 1792 + 64 * t, ap("LS", 16, 24)
-            act(ap("D", n0, n0 + 128), ind(ap("YS", 256, 512), ln))
+            act(ap("D", n0, n0 + 128), ind(ap("YS", 256, 512), ln), F.Relu)
             for c in (0, 4096, 8192):
                 tt(ind(ap("RW", c, c + 2304), ap("LS", 8, 16)), ap("RB", 0, 128), ap("XS", 0, 128), A.add)
                 if c < 8192:
@@ -610,7 +621,9 @@ def rank_program(g, core, T, topo):
             if t or s_[0] is not guards:
                 s_[0](t, *s_[1:])
         if t == 2:
-            store("y", T.yr[:, :], ap("RW", 4096, 6144), 4000.0)
+            act(ap("R0", 1, 16), ap("RW", 4097, 4112))
+            store("y", T.yr[:, 0:16], ap("R0", 0, 16), 2000.0)
+            store("y", T.yr[:, 16:2048], ap("RW", 4112, 6144), 4000.0)
     store("y", T.yn[:, 0:1024], ap("D", 0, 1024), 4000.0)
     store("s", T.yn[:, 1024:2048], ap("D", 1024, 2048), 4000.0)
     for k in range(3):
@@ -663,16 +676,36 @@ def rank_program(g, core, T, topo):
             at[k] = t0
         return at
 
+    def replay(seq, cs, pre):
+        free = {e: 0.0 for e in "vspgy"}
+        done = [0.0] * n
+        for k in seq:
+            t0 = free[engs[k]]
+            for j, l in pre[k]:
+                if done[j] + l > t0:
+                    t0 = done[j] + l
+            done[k] = free[engs[k]] = t0 + cs[k]
+        return max(done[k] + tails[k] for k in range(n))
+
     if "order" not in PLAN:
+        others = []
+        for ga, sc, f, lat, far in OTHERS:
+            cs = [(o["cost"] + o["ng"] * (ga - GATH) + o["ns"] * (sc - SCAT)) * (f if o["eng"] in "vsp" else 1.0) for o in ops]
+            pre = [[(j, l * far if j in ops[k]["soft"] else l + (lat - LAT if ops[k]["dep"].get(j) else 0.0)) for j, l in fwd[k]] for k in range(n)]
+            others.append((cs, pre))
         rng = np.random.default_rng(1)
         zero = [0.0] * n
         best = None
+        stages = np.array([o["stage"] for o in ops])
         for rnd in range(ROUNDS):
             if rnd < len(LEADS):
                 key = [-level[k] - LEADS[rnd] * ops[k]["half"] for k in range(n)]
             else:
-                st_ = rng.normal(0.0, SHAKE * 3 * (rnd % 2), stage[0] + 1)
-                key = [best[1][k] + float(x) + float(st_[ops[k]["stage"]]) for k, x in enumerate(rng.normal(0.0, SHAKE, n))]
+                base = np.array(best[1])
+                mid = rng.uniform(0.0, best[0])
+                near = np.abs(base - mid) < rng.uniform(1000.0, WINDOW)
+                st_ = rng.normal(0.0, SHAKE * rng.choice([0.0, 3.0, 10.0]), stage[0] + 1)
+                key = (base + near * (rng.normal(0.0, SHAKE, n) + st_[stages])).tolist()
             for k in range(n):
                 for j, l in fwd[k]:
                     key[k] = max(key[k], key[j] + 0.001)
@@ -680,12 +713,18 @@ def rank_program(g, core, T, topo):
             for it in range(PASSES):
                 at = place(seq, fwd, zero)
                 end = max(at[k] + cost[k] + tails[k] for k in range(n))
-                if best is None or end < best[0]:
-                    best = (end, at)
+                if best is None or end <= best[0] + 1500.0:
+                    sq_ = sorted(range(n), key=lambda k: (at[k], k))
+                    each = [replay(sq_, c_, p_) for c_, p_ in others]
+                    worth = end + sum(each)
+                    if best is None or worth <= best[2]:
+                        best = (end, at, worth, each)
+                if it == PASSES - 1:
+                    break
                 back = place(sorted(range(n), key=lambda k: (-at[k] - cost[k], -k)), bwd, tails)
                 seq = sorted(range(n), key=lambda k: (-back[k] - cost[k], k))
         PLAN["order"] = sorted(range(n), key=lambda k: (best[1][k], k))
-        PLAN["at"], PLAN["fin"] = best[1], best[0]
+        PLAN["at"], PLAN["fin"], PLAN["each"] = best[1], best[0], best[3]
     order, fin = PLAN["order"], PLAN["fin"]
     for k in range(n):
         ops[k]["at"] = PLAN["at"][k]

@@ -5,7 +5,13 @@ from concourse.mybir import AluOpType as A, ActivationFunctionType as F
 N, NV = 4, 4
 BIG = float(2 ** 27)
 NOG = float(2 ** 26)
-CC = 16384.0
+HUGE = float(2 ** 40)
+MEET = ("X", "Y")
+ACTS = ("X0", "M")
+ORDER = (0, 0)
+FAR = 16384.0
+CC = 32768.0
+RND, RN2 = 1.5 * 2 ** 38, 1.5 * 2 ** 24
 f32, bf, i32, u16, f16 = "float32", "bfloat16", "int32", "uint16", "float16"
 
 SB = {
@@ -14,9 +20,10 @@ SB = {
     "GF": (960, f32), "GR": (960, f32), "KS": (32, f32), "KR": (32, f32), "K0": (8, f32),
     "KA": (8, f32), "KT": (16, f32), "NIB": (128, bf), "R0": (16, bf), "HB": (256, bf), "IB": (128, bf), "IF": (128, f32), "ONE": (128, bf), "RBIG": (512, bf),
     "BK3": (24, bf), "BKF": (8, f32), "SC": (24, bf), "SCT": (64, bf), "SX": (512, bf),
-    "TRX": (128, bf), "TRC": (128, bf), "PBC": (2048, bf), "TRL": (512, bf), "SELG": (1024, bf),
+    "TRC": (128, bf), "PBC": (2048, bf), "BLK": (128, bf), "TRL": (512, bf), "SELG": (1024, bf),
     "CK": (768, bf), "RS": (384, f32), "MKI": (384, i32), "MKJ": (384, i32), "MK": (384, f32), "NMK": (16, f32),
-    "PM": (4, f32), "DU0": (24, f32), "DUM": (24, f32), "NC": (256, f32),
+    "PM": (4, f32), "DU0": (24, f32), "DUM": (24, f32), "NCB": (512, bf), "NIF": (128, f32), "TRZ": (128, bf),
+    "XR": (8192, bf), "RF": (2048, f16), "GP": (48, f32), "THA": (16, f32), "SS": (136, f32), "GT": (128, f32),
     "OCI": (128, i32), "OC": (128, u16), "O5I": (48, i32), "O5": (48, u16),
     "EU": (256, u16), "FA": (256, bf), "FB": (256, bf), "FW": (768, f16),
     "R": (4096, bf), "CMP": (4096, bf), "PEN": (256, bf), "SCN": (768, f32),
@@ -24,27 +31,32 @@ SB = {
     "VS": (160, f32), "AX": (256, f16), "LV": (32, u16), "AV": (256, f16), "AL": (128, f16),
     "AG": (768, f32), "LG": (48, u16), "RG": (768, bf), "CG": (768, bf), "T1": (48, f32), "T2": (48, f32),
     "DH": (40, f32), "HS": (40, f32), "AA": (128, f32), "LA": (8, u16), "PRE": (24, f32),
-    "EA": (128, f32), "EB": (128, f32), "FR": (128, bf), "S8": (8, f32), "DD": (8, f32), "HH": (8, f32),
+    "EB": (128, f32), "FR": (128, bf), "S8": (8, f32), "DD": (8, f32), "HH": (8, f32),
     "NQ": (8, f32), "Q8": (8, f32), "ASK": (16, bf), "ACT": (16, bf), "ABT": (256, f16),
     "AB": (2048, f32), "EQ": (2048, bf), "AC": (128, bf), "LT": (24, f32), "LU": (24, f32), "LS": (24, u16),
-    "AI": (4, i32), "AJ": (4, i32), "YS": (512, f32), "GE": (256, bf), "ST": (128, bf),
-    "W1": (128, f32), "W2": (128, f32), "W3": (128, f32), "W4": (128, f32), "W5": (128, bf), "W6": (128, f32),
-    "U": (512, f32), "MM": (2048, f32), "GI": (136, i32), "GD": (128, i32), "GA": (128, i32), "VAL": (128, f32),
+    "YS": (512, f32), "GE": (256, bf), "ST": (128, bf),
+    "W1": (256, f32), "W2": (128, f32), "W6": (128, f32), "E2": (256, f32),
+    "U": (512, f32), "MM": (2048, f32), "GD": (128, f32),
     "RB": (256, bf), "XS": (256, bf), "YG": (768, f32),
 }
 PS = ["X0", "X1", "Y0", "Y1", "C", "K", "M", "M2"]
-SCRATCH = {k: ("sbuf", [128, n], d) for k, (n, d) in SB.items()}
+SCRATCH, AT = {}, {}
+for k_, (n_, d_) in SB.items():
+    pool_ = k_ if n_ > 256 else "pool" + d_
+    used_ = SCRATCH[pool_][1][1] if pool_ in SCRATCH else 0
+    AT[k_] = (pool_, used_)
+    SCRATCH[pool_] = ("sbuf", [128, used_ + (n_ + 31) // 32 * 32], d_)
 SCRATCH.update({k: ("psum", [128, 512], f32) for k in PS})
 DMAS = ["ld%d" % i for i in range(8)] + ["st%d" % i for i in range(6)]
 SEMAPHORES = ["qv", "qs", "qp", "qg", "sent"] + DMAS + ["%s%d" % (a, t) for a in ("in", "ga", "gb", "ks") for t in (1, 2, 3)]
 CHUNKS = (((0, 512), (512, 1024), (1024, 1536), (1536, 2048)), ((0, 1024), (1024, 1536), (1536, 2048)), ((0, 1024), (1024, 2048)))
-CFG = [(1, 1, 0, 0, 0), (4, 0, 0, 0, 0)] * 9 + [(2, 1, 0, 0, 0), (3, 1, 0, 0, 0)] * 3
+BOTH = [("DDAA", 0, 1, 0), ("DDDA", 0, 1, 0)]
+CFG = BOTH * 2 + [("DCCE", 0, 0, 0), ("DDDD", 0, 0, 0)] + BOTH * 9
 LEADS = [1000.0 * i for i in range(-2, 14)]
 SHARE = {1: (0, 4), 2: (4, 6), 3: (6, 8)}
 OTHERS = [(1.1, 2.2, 0.87, 200.0, 1.6), (1.3, 3.0, 0.9, 120.0, 2.0), (2.0, 5.0, 1.0, 150.0, 1.0)]
 WINDOW = 8000.0
-EVEN = 3
-ROUNDS, PASSES, SHAKE = 2600, 2, 200.0
+ROUNDS, PASSES, SHAKE = 1900, 2, 200.0
 PLAN = {}
 
 GATH, SCAT = 1.35, 3.4
@@ -85,10 +97,16 @@ def rank_program(g, core, T, topo):
             return a
         if a[0] == "ind":
             return real(a[1]).indirect(real(a[2]))
-        t = T[a[0]]
+        pool, c = AT.get(a[0], (a[0], 0))
+        t = T[pool]
         if a[3] == 1:
-            return t[a[4]:a[5], a[1]:a[2]]
-        return t[a[4]:a[5], a[1]:a[2]:a[3]]
+            return t[a[4]:a[5], c + a[1]:c + a[2]]
+        return t[a[4]:a[5], c + a[1]:c + a[2]:a[3]]
+
+    def meets(a, e):
+        if not (e[0] < a[2] and a[1] < e[1]):
+            return False
+        return a[3] != e[2] or a[3] == 1 or (a[1] - e[0]) % a[3] == 0
 
     def op(eng, fn, outs, ins, cost, waits=(), after=(), sem=None, lat=0.0):
         k = len(ops)
@@ -111,26 +129,23 @@ def rank_program(g, core, T, topo):
                 last_p[a[0]] = k
         for a in rd:
             if a[0] not in PS:
-                for c0, c1, j in last_w.get(a[0], []):
-                    if c0 < a[2] and a[1] < c1:
-                        dep[j] = True
+                for e in last_w.get(a[0], []):
+                    if meets(a, e):
+                        dep[e[3]] = True
         for a in wr:
             if a[0] not in PS:
-                for c0, c1, j in last_w.get(a[0], []):
-                    if c0 < a[2] and a[1] < c1:
-                        dep[j] = True
-                for c0, c1, j in last_r.get(a[0], []):
-                    if c0 < a[2] and a[1] < c1:
-                        dep[j] = True
+                for e in last_w.get(a[0], []) + last_r.get(a[0], []):
+                    if meets(a, e):
+                        dep[e[3]] = True
         for a in wr:
             if a[0] not in PS:
-                if a[3] == 1 and a[4] == 0 and a[5] == 128:
-                    last_w[a[0]] = [e for e in last_w.get(a[0], []) if not (a[1] <= e[0] and e[1] <= a[2])]
-                    last_r[a[0]] = [e for e in last_r.get(a[0], []) if not (a[1] <= e[0] and e[1] <= a[2])]
-                last_w.setdefault(a[0], []).append((a[1], a[2], k))
+                if a[4] == 0 and a[5] == 128:
+                    for d in (last_w, last_r):
+                        d[a[0]] = [e for e in d.get(a[0], []) if not (a[1] <= e[0] and e[1] <= a[2] and (a[3] == 1 or a[3] == e[2] and (a[1] - e[0]) % a[3] == 0))]
+                last_w.setdefault(a[0], []).append((a[1], a[2], a[3], k))
         for a in rd:
             if a[0] not in PS:
-                last_r.setdefault(a[0], []).append((a[1], a[2], k))
+                last_r.setdefault(a[0], []).append((a[1], a[2], a[3], k))
         soft = dict(after)
         ops.append({"eng": eng, "fn": fn, "dep": dep, "cost": cost, "waits": list(waits), "soft": soft, "sem": sem, "lat": lat, "out": wr[:1],
                     "half": stage[1], "stage": stage[0],
@@ -189,8 +204,8 @@ def rank_program(g, core, T, topo):
             fn = lambda: g.iota(real(out), pat, base, cm, allow_small_or_imprecise_dtypes=True)
         return op("g", fn, [out], [], 150.0 + 2 * width(out))
 
-    def sel(out, a, pat, cmp, base, cm, fill=0.0):
-        return op("g", lambda: g.affine_select(real(out), real(a), pat, cmp, fill, base, cm), [out], [a], 200.0 + 2 * width(out))
+    def sel(out, a, pat, cmp, base, cm, fill=0.0, **kw):
+        return op("g", lambda: g.affine_select(real(out), real(a), pat, cmp, fill, base, cm), [out], [a], 200.0 + 2 * width(out), **kw)
 
     nd_ = [0, 0]
     outs_ = []
@@ -265,19 +280,22 @@ def rank_program(g, core, T, topo):
     iota(ap("DU0", 0, 16), [[16, 16]], 2048, 0)
     iota(ap("DU0", 16, 24), [[16, 8]], 128, 0)
     ts(ap("DUM", 0, 24), ap("DU0", 0, 24), ap("PM", 0, 1), A.add)
-    iota(ap("CK", 0, 768), [[0, 768]], 0, 0)
+    ms(ap("CK", 0, 768), 0.0)
     ms(ap("CK", 128, 384, 1, 0, 32), BIG / 32)
     ms(ap("CK", 0, 512, 1, 32, 64), 64.0)
-    iota(ap("RS", 0, 384), [[0, 384]], 0, 0)
-    ms(ap("RS", 0, 384, 16), float(2 ** 30))
+    ms(ap("RS", 0, 384), 0.0)
+    ms(ap("RS", 0, 384, 16), HUGE)
     ms(ap("D0", 0, 240), 1.0)
     ms(ap("D0", 0, 240, 5), 0.0)
     ms(ap("D1", 0, 240), 0.0)
     ms(ap("DH", 0, 40), 0.0)
     ms(ap("THR", 0, 48), 2 ** 25)
-    ms(ap("GI", 0, 8), 0)
-    iota(ap("RW", 10240, 10496), [[0, 256]], 0, 0)
-    iota(ap("D", 1792, 2304), [[0, 512]], 0, 0)
+    ms(ap("SS", 0, 1), 0.0)
+    ms(ap("GP", 0, 1), 0.0)
+    ms(ap("ACT", 8, 9), -1.0 / 256)
+    ms(ap("W1", 128, 256), 1.0)
+    ms(ap("RW", 10240, 10496), 0.0)
+    ms(ap("D", 1792, 2304), 0.0)
     iota(ap("YS", 384, 512), [[0, 128]], 0, 0)
     ms(ap("PRE", 16, 24), -128.0)
     for name, plain, sums in (("K0", 12, 8.0), ("KA", 1, 2.0)):
@@ -295,25 +313,32 @@ def rank_program(g, core, T, topo):
     act(ap("RSV", 128, 256), ap("RW", 6272, 6400))
     sz = send([(t, ap("XZ", 256 * t, 256 * t + 256), ap("XZ", 0, 256), "in%d" % t, SHARE[t]) for t in (1, 2, 3)], [ap("XZ", 0, 256)])
     sv = send([(t, ap("VSR", 16 * t, 16 * t + 16), ap("VSO", 16 * t, 16 * t + 16), "in%d" % t, SHARE[t]) for t in (1, 2, 3)], [ap("VSO", 0, 64)])
+    ms(ap("SX", 0, 512), -1.0)
     for j, t in enumerate((0, 2)):
-        cp(ap("SCT", 32 * j, 32 * j + 8), ap("SC", 0, 8))
         sel(ap("SCT", 32 * j + 8, 32 * j + 24), ap("ONE", 0, 16), [[-8, 2], [-16, 8]], A.is_equal, -t, 1)
-        iota(ap("SX", 256 * j, 256 * j + 256), [[0, 256]], -1, 0)
         sel(ap("SX", 256 * j, 256 * j + 256), ap("SX", 256 * j, 256 * j + 256), [[-8, 2], [-16, 8], [0, 16]], A.is_equal, -t, 1)
-    sel(ap("TRX", 0, 128), ap("ONE", 0, 128), [[-16, 8], [0, 16]], A.is_ge, 0, 1)
-    sel(ap("TRX", 0, 128), ap("TRX", 0, 128), [[16, 8], [1, 16]], A.is_gt, 0, -1)
-    iota(ap("TRC", 0, 128), [[0, 128]], int(CC), 0)
-    sel(ap("TRC", 0, 128), ap("TRC", 0, 128), [[-16, 8], [0, 16]], A.is_ge, 0, 1)
-    sel(ap("TRC", 0, 128), ap("TRC", 0, 128), [[16, 8], [1, 16]], A.is_ge, 0, -1)
-    iota(ap("TRL", 0, 512), [[0, 512]], 4096, 0)
+    for name, above, on in (("TRZ", -FAR, FAR), ("TRC", CC, -15 * CC)):
+        iota(ap(name, 0, 128), [[0, 128]], int(above), 0)
+        sel(ap(name, 0, 128), ap(name, 0, 128), [[-16, 8], [0, 16]], A.is_ge, 0, 1)
+        sel(ap(name, 0, 128), ap(name, 0, 128), [[16, 8], [1, 16]], A.is_ge, 0, -1)
+        sel(ap(name, 0, 128), ap(name, 0, 128), [[-1, 128]], A.not_equal, 0, 1, on)
+    act(ap("NIF", 0, 128), ap("IB", 0, 128), scale=-1.0)
+    ms(ap("TRL", 0, 512), 4096.0)
     sel(ap("TRL", 0, 512), ap("TRL", 0, 512), [[0, 4], [-1, 128]], A.is_ge, 0, 1)
     sg = ap("SELG", 0, 1024, 1, 0, 8)
-    iota(sg, [[0, 1024]], 1, 0)
+    ms(sg, 1.0)
     sel(sg, sg, [[-1, 8], [0, 128]], A.is_equal, 0, 1)
-    iota(ap("NC", 0, 256), [[1, 256]], 4096 + 1792, 0)
-    iota(ap("PBC", 0, 2048), [[0, 2048]], int(CC), 0)
-    sel(ap("PBC", 0, 2048), ap("PBC", 0, 2048), [[0, 16], [-16, 8], [0, 16]], A.is_ge, 0, 1)
-    sel(ap("PBC", 0, 2048), ap("PBC", 0, 2048), [[1, 16], [16, 8], [0, 16]], A.is_gt, 1, -1)
+    nc = ap("NCB", 0, 256, 1, 0, 32)
+    iota(nc, [[0, 2], [1, 128]], 0, 0)
+    sel(nc, nc, [[0, 256]], A.is_equal, 0, 1)
+    for j in range(2):
+        ms(ap("NCB", 128 * j, 128 * j + 128, 1, 32, 64), (4096 + 1792 + 128 * j - FAR) / 32)
+    ms(ap("NCB", 256, 384), CC / 8)
+    ms(ap("NCB", 384, 512), -FAR / 128)
+    iota(ap("BLK", 0, 128), [[0, 128]], int(CC), 0)
+    sel(ap("BLK", 0, 128), ap("BLK", 0, 128), [[-16, 8], [0, 16]], A.is_ge, 0, 1)
+    for i in range(16):
+        sel(ap("PBC", 128 * i, 128 * i + 128), ap("BLK", 0, 128), [[16, 8], [0, 16]], A.is_ge, i, -1)
 
     xb = [0, 0]
     KB, CB = ("M2", "K"), ("M", "C")
@@ -348,37 +373,48 @@ def rank_program(g, core, T, topo):
             prep(t + 1)
 
     def start_nodes(t, h):
-        if True:
-            c = 16 * t + 8 * h
-            tt(ap("AV", 128 * h, 128 * h + 128), ind(ap("VSR" if t else "VSO", c, c + 8), ap("OC", 0, 8)), ap("MK", 0, 128), A.mult, **arrived("in", t))
-            mm(ap(CB[h], 200, 208), ap("AV", 128 * h, 128 * h + 128), ap("BK3", 0, 8))
-            cp(ap("D1", 120 * h + 80, 120 * h + 120, 5), ap(CB[h], 200, 208))
+        c = 16 * t + 8 * h
+        tt(ap("AV", 128 * h, 128 * h + 128), ind(ap("VSR" if t else "VSO", c, c + 8), ap("OC", 0, 8)), ap("MK", 0, 128), A.mult, **arrived("in", t))
+        mm(ap(CB[h], 200, 208), ap("AV", 128 * h, 128 * h + 128), ap("BK3", 0, 8))
+        cp(ap("D1", 120 * h + 80, 120 * h + 120, 5), ap(CB[h], 200, 208))
 
     def guards(t, h):
         o, w = 384 * h, 24 * h
         gr = 240 * t + 120 * h
         tt(ap("AG", o, o + 384), ind(ap("GR", gr, gr + 120), ap("O5", 0, 24)), ap("MK", 0, 384), A.mult, **arrived("ga" if h == 0 else "gb", t))
+        x = b = "Y0" if h == 0 else xbank(h)
         for k in range(3):
-            mm(ap(KB[h], 8 * k, 8 + 8 * k), ap("AG", o + 128 * k, o + 128 * k + 128), ap("BKF", 0, 8))
-        cp(ap("LG", w, w + 24), ap(KB[h], 0, 24))
+            mm(ap(b, 448 + 8 * k, 456 + 8 * k), ap("AG", o + 128 * k, o + 128 * k + 128), ap("BKF", 0, 8))
+        cp(ap("LG", w, w + 24), ap(b, 448, 472))
         act(ap("RG", o, o + 384), ind(ap("RW", 0, 4096), ap("LG", w, w + 24)))
-        x = xbank(h)
         for k in range(3):
             mm(ap(x, 128 * k, 128 * k + 128), ap("IB", 0, 128), xs(t, h), **arrived("in", t))
         tt(ap("CG", o, o + 384), ap("RG", o, o + 384), ap(x, 0, 384), A.is_le)
         for k in range(3):
-            mm(ap(CB[h], 160 + 8 * k, 168 + 8 * k), ap("RG", o + 128 * k, o + 128 * k + 128), ap("SC", 0, 8))
+            mm(ap(b, 416 + 8 * k, 424 + 8 * k), ap("RG", o + 128 * k, o + 128 * k + 128), ap("SC", 0, 8))
         for k in range(3):
-            mm(ap(CB[h], 128 + 8 * k, 136 + 8 * k), ap("CG", o + 128 * k, o + 128 * k + 128), ap("BK3", 0, 8))
-        cnt = ap(CB[h], 128, 152)
-        ts(ap("D0", 120 * h + 1, 120 * h + 120, 5), cnt, kcol(t), A.is_lt, **arrived("ks", t))
+            mm(ap(b, 384 + 8 * k, 392 + 8 * k), ap("CG", o + 128 * k, o + 128 * k + 128), ap("BK3", 0, 8))
+        cnt = ap(b, 384, 408)
         ts(ap("T1", w, w + 24), cnt, kcol(t), A.is_lt, NOG, A.mult, **arrived("ks", t))
-        ts(ap("T2", w, w + 24), cnt, kcol(t), A.is_ge, **arrived("ks", t))
-        tt(ap("THR", w, w + 24), ap("T1", w, w + 24), ap(CB[h], 160, 184), A.add)
-        tt(ap("D1", 120 * h + 1, 120 * h + 120, 5), ap("T2", w, w + 24), ap("GR", gr + 4, gr + 120, 5), A.mult, **arrived("ga" if h == 0 else "gb", t))
+        tt(ap("THR", w, w + 24), ap("T1", w, w + 24), ap(b, 416, 440), A.add)
+        ts(ap("D0", 120 * h + 1, 120 * h + 120, 5), ap("T1", w, w + 24), 0.0, A.is_gt)
+        tt(ap("D1", 120 * h + 1, 120 * h + 120, 5), ap("GR", gr + 4, gr + 120, 5), ap("T1", w, w + 24), A.subtract, **arrived("ga" if h == 0 else "gb", t))
 
     def vlist(t, s, h):
         return ap("L2", 16 * t + 8 * h, 16 * t + 8 * h + 8) if s == 2 else ap("LV", 16 * s + 8 * h, 16 * s + 8 * h + 8)
+
+    def cfg(t, s, h):
+        return CFG[6 * t + 2 * s + h]
+
+    def spans(t, s, h):
+        n = 128 - 32 * cfg(t, s, h)[0].count("A")
+        return [(0, n, "R", 2048 * h)] + [(n, 128, "RF", 1024 * h - 1024)] * (n < 128)
+
+    def spread(t):
+        for h in range(2):
+            n, e = 32 * max(cfg(t, s, h)[0].count("A") for s in range(3)), 2048 * t + 1024 * h + 1024
+            for i in range(16 if n else 0):
+                sel(ap("XR", e - 16 * n + i, e, 16), ap("XZ", 256 * t + 128 * h + 128 - n, 256 * t + 128 * h + 128), [[0, n]], A.is_equal, 0, 0, **arrived("in", t))
 
     def gather(t, s, h):
         o = 128 * h
@@ -388,59 +424,67 @@ def rank_program(g, core, T, topo):
             cp(e, ind(ap("D", 0, 2048), vlist(t, s, h)))
         else:
             ts(e, ind(ap("D", 0, 2048), vlist(t, s, h)), 4096.0 * (s + 1), A.min)
-        ns, vg, ch = CFG[6 * t + 2 * s + h][:3]
-        sq = range(ns)
+        kinds, ch = cfg(t, s, h)[:2]
         for c0, c1 in CHUNKS[ch]:
-            (cp if c0 >= 2048 - 512 * vg else act)(ap("R", 2048 * h + c0, 2048 * h + c1), ind(ap("RW", 0, 10240), ap("EU", o + c0 // 16, o + c1 // 16)))
+            src, kind = ind(ap("RW", 0, 10240), ap("EU", o + c0 // 16, o + c1 // 16)), kinds[c0 // 512]
+            if kind == "A":
+                c = 1024 * h - 1024
+                tt(ap("RF", c + c0, c + c1), src, ap("XR", 2048 * t + c + c0, 2048 * t + c + c1), A.subtract)
+            else:
+                (cp if kind == "E" else act)(ap("R", 2048 * h + c0, 2048 * h + c1), src)
         if s or whole:
             ts(ap("FA", o, o + 128), e, 4096.0, A.is_ge)
         if s == 2:
             ts(ap("FB", o, o + 128), e, 8192.0, A.is_ge)
         for k in range(s + 1):
             ts(ap("FW", 384 * h + 128 * k, 384 * h + 128 * k + 128), e, -4096.0 * k - 2048.0, A.add)
+
+    def compare(t, s, h):
+        o = 128 * h
+        kinds = cfg(t, s, h)[0]
         for q in range(4):
-            x = xbank(h)
             c = 2048 * h + 512 * q
-            mm(ap(x, 0, 512), ap("XT", 256 * t + o, 256 * t + o + 128), ap("RW", 6144 + 512 * q, 6656 + 512 * q), True, q not in sq)
-            if q in sq:
+            if kinds[q] == "A":
+                ts(ap("CMP", c, c + 512), ap("RF", c - 1024 * (h + 1), c - 1024 * (h + 1) + 512), 0.0, A.is_le)
+                continue
+            x = "Y1" if t and s == 2 and h == 0 else xbank(h)
+            mm(ap(x, 0, 512), ap("XT", 256 * t + o, 256 * t + o + 128), ap("RW", 6144 + 512 * q, 6656 + 512 * q), True, kinds[q] != "D")
+            if kinds[q] == "D":
                 mm(ap(x, 0, 512), ap("NIB", 0, 128), ap("R", c, c + 512), False, True)
                 act(ap("CMP", c, c + 512), ap(x, 0, 512), F.Sign, bias=0.5)
             else:
                 tt(ap("CMP", c, c + 512), ap("R", c, c + 512), ap(x, 0, 512), A.is_le)
 
+    def by_entry(t, s, h, bank, c0, c1, w):
+        for p0, p1, name, base in spans(t, s, h):
+            for i in range(16):
+                mm(ap(bank, c0 + i, c1, 16, p0, p1), ap(name, base + 16 * p0 + i, base + 16 * p1, 16), w, False, False)
+
     def tail(t, s, h):
         o, n, w, W = 128 * h, 128 * (s + 1), 24 * h, 8 * (s + 1)
         cut = s == 0 and h == 0 and t % 2 == 0
-        K, C, kc = KB[h], CB[h], kcol(t, CFG[6 * t + 2 * s + h][0])
-        if cut:
-            mm(ap(K, 0, 384), ap("ONE", 0, 128, 1, 0, 64), ap("CK", 384, 768, 1, 0, 64), True, False)
-            mm(ap(K, 128, 384), xs(t, 0), ap("SX", 128 * t, 128 * t + 256), False, False, **arrived("in", t))
-        else:
-            mm(ap(K, 0, n), ap("ONE", 0, 128, 1, 0, 64), ap("CK", 0, n, 1, 0, 64), True, False)
+        K, kc = KB[h], kcol(t, cfg(t, s, h)[0].count("D"))
+        C, c0 = ("Y0" if cut else CB[h]), 0
+        mm(ap(K, 0, n), ap("ONE", 0, 128, 1, 0, 64), ap("CK", 0, n, 1, 0, 64), True, False)
         if s or cut:
             mm(ap(K, 0, n), ap("FA", o, o + 128), ap("RBIG", 128, 128 + n), False, False)
         if s == 2:
             mm(ap(K, 128, n), ap("FB", o, o + 128), ap("RBIG", 128, n), False, False)
         for k in range(s + 1):
             mm(ap(K, 128 * k, 128 * k + 128), ap("FW", 384 * h + 128 * k, 384 * h + 128 * k + 128), ap("IB", 0, 128), False, False)
-        for i in range(16):
-            r = ap("R", 2048 * h + i, 2048 * h + 2048, 16)
-            if cut:
-                mm(ap(K, i, 384, 16), r, ap("SCT", 16 * t, 16 * t + 24), False, False)
-            else:
-                mm(ap(K, i, n, 16), r, ap("SC", 0, W), False, False)
-        for p0, p1 in ((0, 96), (96, 128)) if CFG[6 * t + 2 * s + h][4] else ((0, 128),):
+        by_entry(t, s, h, K, 0, n, ap("SC", 0, W))
+        for p0, p1 in ((0, 64), (64, 128)) if cfg(t, s, h)[3] else ((0, 128),):
             for i in range(16):
-                mm(ap(C, i, 128, 16, p0, p1), ap("CMP", 2048 * h + 16 * p0 + i, 2048 * h + 16 * p1, 16), ap("BK3", 0, 8))
-        if CFG[6 * t + 2 * s + h][3]:
-            act(ap("PEN", o, o + 128), ap(C, 0, 128), F.Relu, bias=kc, scale=-1.0, **arrived("ks", t))
+                mm(ap(C, c0 + i, c0 + 128, 16, p0, p1), ap("CMP", 2048 * h + 16 * p0 + i, 2048 * h + 16 * p1, 16), ap("BK3", 0, 8))
+        if cfg(t, s, h)[2]:
+            act(ap("PEN", o, o + 128), ap(C, c0, c0 + 128), F.Relu, bias=kc, scale=-1.0, **arrived("ks", t))
         else:
-            ts(ap("PEN", o, o + 128), ap(C, 0, 128), kc, A.is_lt, **arrived("ks", t))
+            ts(ap("PEN", o, o + 128), ap(C, c0, c0 + 128), kc, A.is_lt, **arrived("ks", t))
         for k in range(s + 1):
             mm(ap(K, 128 * k, 128 * k + 128), ap("RBIG", 128, 256), ap("PEN", o, o + 128), False, k == s)
         scan(ap("SCN", 384 * h, 384 * h + n), ap("RS", 0, n), ap(K, 0, n), A.add, A.min)
-        if cut:
-            act(ap("GE", 0, 256), ap(K, 128, 384), F.Sign, bias=0.5)
+        if s == 0 and h == 0 and t % 2:
+            tt(ap("ASK", 0, 8), ap("SCN", 15, 128, 16), ap("THA", 8, 16), A.is_ge)
         mi, lo = ap("MI", w, w + W), ap("LO", w, w + W)
         tt(mi, ap("SCN", 384 * h + 15, 384 * h + n, 16), ap("THR", w, w + W), A.min)
         ts(lo, mi, 4095, A.bitwise_and)
@@ -449,7 +493,7 @@ def rank_program(g, core, T, topo):
         ts(ap("D0", c, 120 * h + 40 * (s + 1), 5), lo, 0.0, A.is_equal)
         if s:
             v = 80 * h + 40 * (2 - s)
-            scan(ap("VS", v, v + 40), ap("D0", 120 * h + 40 * s, 120 * h + 40 * s + 40), ap("D1", 120 * h + 40 * s, 120 * h + 40 * s + 40), A.mult, A.add)
+            scan(ap("VS", v, v + 40), ap("D0", 120 * h + 40 * s, 120 * h + 40 * s + 40), ap("D1", 120 * h + 40 * s, 120 * h + 40 * s + 40), A.mult, A.max)
             tt(ap("AX", o, o + 128), ind(ap("VS", v, v + 40), ap("O5", 0, 8)), ap("MK", 0, 128), A.mult)
             mm(ap(C, 192, 200), ap("AX", o, o + 128), ap("BK3", 0, 8))
             cp(vlist(t, s - 1, h), ap(C, 192, 200))
@@ -461,7 +505,7 @@ def rank_program(g, core, T, topo):
 
     def final_guards(t, h):
         ms(ap("D1", 120 * h + 40, 120 * h + 120, 5), 0.0)
-        scan(ap("GF", 240 * t + 120 * h, 240 * t + 120 * h + 120), ap("D0", 120 * h, 120 * h + 120), ap("D1", 120 * h, 120 * h + 120), A.mult, A.add)
+        scan(ap("GF", 240 * t + 120 * h, 240 * t + 120 * h + 120), ap("D0", 120 * h, 120 * h + 120), ap("D1", 120 * h, 120 * h + 120), A.mult, A.max)
         if t + 1 < NV:
             c, kind = 240 * t + 120 * h, "ga" if h == 0 else "gb"
             gf = ap("GF", c, c + 120)
@@ -469,15 +513,14 @@ def rank_program(g, core, T, topo):
 
     v2, v1, v0 = ap("D1", 80, 120, 5), ap("D1", 40, 80, 5), ap("VS", 44, 80, 5)
     av = ap("HS", 4, 40, 5)
+    ea, eb, fr = ap("E2", 0, 128), ap("EB", 0, 128), ap("FR", 0, 128)
 
     def early3(t):
         ts(ap("DH", 1, 40, 5), v2, -1.0, A.mult)
         tt(ap("DH", 2, 40, 5), v2, v1, A.subtract)
         tt(ap("DH", 3, 40, 5), v1, v0, A.subtract)
         cp(ap("DH", 4, 40, 5), v0)
-        if t % 2:
-            mm(ap("M", 256, 384, 1, 0, 8), v0, ap("IF", 0, 128))
-        act(ap("EB", 0, 128), ind(ap("D", 0, 2048), vlist(t, 0, 0)))
+        act(eb, ind(ap("D", 0, 2048), vlist(t, 0, 0)))
         if t % 2 == 0:
             lb = ind(ap("RW", 0, 2048), vlist(t, 0, 0))
             act(ap("RB", 0, 128), lb, scale=ap("NMK", 8 + t, 9 + t))
@@ -492,27 +535,31 @@ def rank_program(g, core, T, topo):
         scan(ap("HS", 0, 40), ap("D0", 40 * k, 40 * k + 40), ap("DH", 0, 40), A.mult, A.add)
         tt(ap("AL", 0, 128), ind(ap("HS", 0, 40), ap("O5", 0, 8)), ap("MK", 0, 128), A.mult)
         mm(ap("M", 128, 256, 1, 0, 8), av, ap("IF", 0, 128))
-        if k:
-            mm(ap("M", 256, 384, 1, 0, 8), v0, ap("IF", 0, 128))
+        mm(ap("M", 256, 384, 1, 0, 8), v0, ap("IF", 0, 128))
         cp(ap("ABT", 0, 256, 1, 0, 8), ap("M", 128, 384, 1, 0, 8))
         mm(ap("M", 80, 88), ap("AL", 0, 128), ap("BK3", 0, 8))
         cp(ap("LA", 0, 8), ap("M", 80, 88))
         tt(ap("PRE", 0, 8), ap("M", 80, 88), ap("DUM", 0, 8), A.subtract)
-        act(ap("EA", 0, 128), ind(ap("D", 0, 2048), ap("LA", 0, 8)))
+        act(ea, ind(ap("D", 0, 2048), ap("LA", 0, 8)))
         tt(ap("S8", 0, 8), av, v0, A.add)
         tt(ap("DD", 0, 8), av, v0, A.subtract)
         act(ap("HH", 0, 8), ap("DD", 0, 8), F.Abs)
         ts(ap("NQ", 0, 8), ap("DD", 0, 8), 0.0, A.not_equal)
         tt(ap("Q8", 0, 8), ap("NQ", 0, 8), av, A.min)
-        ts(ap("FR", 0, 128), ap("EA" if k else "EB", 0, 128), 0.0, A.is_equal)
-        mm(ap("M", 32, 40), ap("FR", 0, 128), ap("BK3", 0, 8))
-        mm(ap("M", 384, 512), ap("TRX", 0, 128), ap("FR", 0, 128))
-        tt(ap("ASK", 0, 8), ap("Q8", 0, 8), ap("M", 32, 40), A.min)
-        tt(ap("W5", 0, 128), ap("FR", 0, 128), ap("M", 384, 512), A.is_gt)
+        ts(fr, ea if k else eb, 0.0, A.is_equal)
+        mm(ap("M", 32, 40), fr, ap("BK3", 0, 8))
+        tt(ap("ASK", 8 - 8 * k, 16 - 8 * k), ap("Q8", 0, 8), ap("M", 32, 40), A.min)
+        if k:
+            mm(ap("M", 384, 512), ap("ONE", 0, 128, 1, 0, 64), ap("NCB", 64 * t, 64 * t + 128, 1, 0, 64), True, False)
+            mm(ap("M", 384, 512), ap("TRZ", 0, 128), fr, False, True)
+            tt(ap("E2", 128, 256), ea, ap("M", 384, 512), A.max)
+        else:
+            ts(ap("THA", 0, 8), ap("ASK", 8, 16), -HUGE, A.mult, HUGE, A.add)
+            tt(ap("THA", 8, 16), ap("THA", 0, 8), ap("THR", 0, 8), A.add)
 
     def meet(t):
         for b in range(4):
-            y = "Y%d" % (b % 2)
+            y = MEET[t % 2] + "%d" % (b % 2)
             mm(ap(y, 0, 512), ap("IB", 0, 128), ap("TRL", 0, 512), True, False)
             for j in range(2):
                 gg = 2 * b + j
@@ -523,97 +570,106 @@ def rank_program(g, core, T, topo):
                 ts(ap("EQ", 256 * gg, 256 * gg + 256), ap("AB", 256 * gg, 256 * gg + 256), ap("HH", gg, gg + 1), A.is_equal)
 
     def acts(t):
+        b = ACTS[t % 2]
         for gg in range(8):
             for x in range(2):
                 c = 256 * gg + 128 * x
-                mm(ap("M", 40 + gg, 41 + gg), ap("EQ", c, c + 128), ap("ASK", gg, gg + 1), x == 0, x == 1)
-        tt(ap("ACT", 0, 8), ap("ASK", 0, 8), ap("M", 40, 48), A.is_gt)
+                mm(ap(b, 40 + gg, 41 + gg), ap("EQ", c, c + 128), ap("ASK", gg, gg + 1), x == 0, x == 1)
+        tt(ap("ACT", 0, 8), ap("ASK", 0, 8), ap(b, 40, 48), A.is_gt)
         nl = 24 if t % 2 == 0 else 16
         tt(ap("AC", 0, 128), ind(ap("ACT", 0, 8), ap("OC", 0, 8)), ap("MK", 0, 128), A.mult)
-        mm(ap("M", 48, 48 + nl), ap("AC", 0, 128), ap("BK3", 0, nl))
         if t < NV - 1:
-            for gg in range(8):
-                mm(ap("M", 72, 73), ap("ONE", 0, 128), ap("ACT", gg, gg + 1), gg == 0, gg == 7)
-        tt(ap("LT", 0, nl), ap("PRE", 0, nl), ap("M", 48, 48 + nl), A.mult)
+            for gg in range(9):
+                mm(ap(b, 72, 73), ap("ONE", 0, 128), ap("ACT", gg, gg + 1), gg == 0, gg == 8)
+        mm(ap(b, 48, 48 + nl), ap("AC", 0, 128), ap("BK3", 0, nl))
+        tt(ap("LT", 0, nl), ap("PRE", 0, nl), ap(b, 48, 48 + nl), A.mult)
         if t < NV - 1:
-            cp(ap("AI", 0, 1), ap("M", 72, 73))
-            ts(ap("AJ", 0, 1), ap("AI", 0, 1), 1, A.bitwise_and)
+            ts(ap("KT", 0, 1), ap(b, 72, 73), RN2, A.add, RN2, A.subtract)
+            ts(ap("KT", 8, 9), ap("KT", 0, 1), ap(b, 72, 73), A.subtract, 4.5, A.subtract)
             ks = ap("KS", 8 * t, 8 * t + 8)
-            cp(ap("KT", 0, 1), ap("AJ", 0, 1))
-            ts(ap("KT", 8, 16), ap("KA", 0, 8), ap("KT", 0, 1), A.mult)
-            tt(ks, ap("K0", 0, 8), ap("KT", 8, 16), A.subtract)
+            ts(ks, ap("KA", 0, 8), ap("KT", 8, 9), A.mult, 16.0, A.add)
             sends["ks", t + 1] = send([(1, ap("KR", 8 * t + 8, 8 * t + 16), ks, "ks%d" % (t + 1), 0)], [ks])
         tt(ap("LU", 0, nl), ap("LT", 0, nl), ap("DUM", 0, nl), A.add)
         cp(ap("LS", 0, nl), ap("LU", 0, nl))
 
     def split_rows(t):
-        eb = ap("EB", 0, 128)
-        mm(ap("M2", 136, 264), ap("GE", 0, 128), ap("IB", 0, 128))
-        mm(ap("M2", 264, 392), ap("GE", 0, 128), ap("IB", 0, 128), True, False)
-        mm(ap("M2", 264, 392), ap("GE", 128, 256), ap("IB", 0, 128), False, True)
-        ts(ap("ST", 0, 128), ap("M2", 264, 392), -2.0, A.is_equal)
-        tt(ap("YS", 256, 384), eb, ap("M2", 136, 264), A.mult)
-        mm(ap("M2", 264, 392), ap("TRC", 0, 128), ap("ST", 0, 128))
-        tt(ap("W1", 0, 128), eb, ap("M2", 264, 392), A.add)
-        tt(ap("U", 0, 128), ap("W1", 0, 128), ap("ST", 0, 128), A.mult)
+        n = spans(t, 0, 0)[0][1]
+        mm(ap("M", 128, 384), ap("ONE", 0, 128, 1, 0, 64), ap("CK", 512, 768, 1, 0, 64), True, False)
+        mm(ap("M", 128, 384, 1, 0, n), ap("XZ", 256 * t, 256 * t + n), ap("SX", 128 * t, 128 * t + 256), False, False, **arrived("in", t))
+        by_entry(t, 0, 0, "M", 128, 384, ap("SCT", 16 * t + 8, 16 * t + 24))
+        mm(ap("M", 128, 144), ap("ONE", 0, 128, 1, 0, 64), ap("CK", 512, 528, 1, 0, 64), False, True)
+        act(ap("GE", 0, 256), ap("M", 128, 384), F.Sign, bias=0.5)
+        mm(ap("M", 128, 256), ap("GE", 0, 128), ap("IB", 0, 128))
+        mm(ap("M", 256, 384), ap("GE", 0, 128), ap("IB", 0, 128), True, False)
+        mm(ap("M", 256, 384), ap("GE", 128, 256), ap("IB", 0, 128), False, True)
+        ts(ap("ST", 0, 128), ap("M", 256, 384), -2.0, A.is_equal)
+        tt(ap("YS", 256, 384), eb, ap("M", 128, 256), A.mult)
+        mm(ap("M", 384, 512), ap("ONE", 0, 128), ap("NCB", 256, 384), True, False)
+        mm(ap("M", 384, 512), ap("TRC", 0, 128), ap("ST", 0, 128), False, True)
+        tt(ap("U", 0, 128), eb, ap("M", 384, 512), A.add)
         act(ap("U", 128, 256), ap("U", 0, 128))
         act(ap("U", 256, 512), ap("U", 0, 256))
-        ts(ap("W2", 0, 128), ap("YS", 256, 384), 0.0, A.min, -1.0, A.mult)
+        act(ap("W2", 0, 128), ap("YS", 256, 384), F.Relu, scale=-1.0)
 
     def place_rows(t):
         for b in range(4):
             y = "Y%d" % (b % 2)
             for j in range(4):
                 c = 512 * b + 128 * j
-                mm(ap(y, 128 * j, 128 * j + 128), ap("PBC", c, c + 128), ap("FR", 0, 128))
+                mm(ap(y, 128 * j, 128 * j + 128), ap("PBC", c, c + 128), fr)
             for c0, c1, u in ((0, 128, 0), (128, 256, 0), (256, 512, 0)) if b == 0 else ((0, 512, 0),):
                 tt(ap("MM", 512 * b + c0, 512 * b + c1), ap("U", u, u + c1 - c0), ap(y, c0, c1), A.max)
             for j in range(4):
-                c, i = 512 * b + 128 * j, 4 * b + j + 1
-                mm(ap("M2", i, i + 113, 16), ap("MM", c, c + 128), ap("BKF", 0, 8))
-        cp(ap("GI", 1, 129), ap("M2", 1, 129))
-        tt(ap("GD", 0, 128), ap("GI", 0, 128), ap("GI", 1, 129), A.subtract)
-        ts(ap("GA", 0, 128), ap("GD", 0, 128), int(CC) - 1, A.bitwise_and)
-        cp(ap("VAL", 0, 128), ap("GA", 0, 128))
-        ms(ap("VAL", 0, 128, 16), 0.0)
-        mm(ap("M2", 264, 392), ap("VAL", 0, 128), ap("IF", 0, 128))
+                c, i = 512 * b + 128 * j, 4 * b + j + 129
+                mm(ap("M", i, i + 113, 16), ap("MM", c, c + 128), ap("BKF", 0, 8))
+        act(ap("SS", 1, 129), ap("M", 129, 257))
+        tt(ap("GD", 0, 128), ap("SS", 0, 128), ap("M", 129, 257), A.subtract)
+        ts(ap("GT", 0, 128), ap("GD", 0, 128), RND, A.add, RND, A.subtract)
+        mm(ap("M", 384, 512), ap("GD", 0, 128), ap("IF", 0, 128), True, False)
+        mm(ap("M", 384, 512), ap("GT", 0, 128), ap("NIF", 0, 128), False, True)
         tt(ap("W6", 0, 128), ap("MM", 1920, 2048), ap("U", 0, 128), A.is_le)
-        tt(ap("W6", 0, 128), ap("ST", 0, 128), ap("W6", 0, 128), A.is_le)
-        tt(ap("W3", 0, 128), ap("W5", 0, 128), ap("NC", 64 * t, 64 * t + 128), A.mult)
-        tt(ap("W1", 0, 128), ap("W3", 0, 128), ap("M2", 264, 392), A.add)
+        act(ap("W1", 0, 128), ap("M", 384, 512), scale=ap("NMK", 0, 1))
 
     def move_down(t):
-        act(ap("AA", 0, 128), ind(ap("GF", 240 * t, 240 * t + 40), ap("O5", 0, 8)))
-        mm(ap("M2", 136, 264), ap("AA", 0, 128), ap("IF", 0, 128))
-        tt(ap("W1", 0, 128), ap("EA", 0, 128), ap("M2", 136, 264), A.not_equal)
-        tt(ap("W2", 0, 128), ap("W5", 0, 128), ap("M2", 136, 264), A.mult)
+        scan(ap("GP", 1, 41), ap("D0", 0, 40), ap("D1", 0, 40), A.mult, A.max)
+        act(ap("AA", 0, 128), ind(ap("GP", 0, 41), ap("O5", 0, 8)))
+        mm(ap("M", 256, 384), ap("AA", 0, 128), ap("IF", 0, 128))
+        tt(ap("W1", 0, 128), ea, ap("M", 256, 384), A.not_equal)
+        mm(ap("M", 384, 512), ap("AA", 0, 128), ap("IF", 0, 128), True, False)
+        mm(ap("M", 384, 512), ap("ONE", 0, 128), ap("NCB", 384, 512), False, False)
+        mm(ap("M", 384, 512), ap("TRZ", 0, 128), fr, False, True)
+        tt(ap("E2", 128, 256), eb, ap("M", 384, 512), A.max)
 
     def write_back(t):
-        even = t % 2 == 0
-        tt(ind(ap("D", 0, 2304), ap("LS", 8, 16)), ap("W2", 0, 128), ap("W6" if even else "EB", 0, 128), A.mult if even else A.add)
-        tt(ind(ap("D", 0, 2304), ap("LS", 0, 8)), ap("W1", 0, 128), ap("EA", 0, 128), A.add if even else A.mult)
-        if t % 2 == 0:
-            n0, ln = 1792 + 64 * t, ap("LS", 16, 24)
-            act(ap("D", n0, n0 + 128), ind(ap("YS", 256, 512), ln), F.Relu)
-            for c in (0, 4096, 8192):
-                tt(ind(ap("RW", c, c + 2304), ap("LS", 8, 16)), ap("RB", 0, 128), ap("XS", 0, 128), A.add)
-                if c < 8192:
-                    act(ap("RW", c + n0, c + n0 + 128), ind(ap("HB", 0, 256), ln))
-                    r = 128 * (c // 4096)
-                    act(ap("RW", c + 2176, c + 2304), ap("RSV", r, r + 128))
+        if t % 2:
+            tt(ind(ap("D", 0, 2304), ap("LS", 0, 16)), ap("E2", 0, 256), ap("W1", 0, 256), A.mult)
+            return
+        n0, ln = 1792 + 64 * t, ap("LS", 16, 24)
+        tt(ind(ap("D", 0, 2304), ap("LS", 8, 16)), ap("W2", 0, 128), ap("W6", 0, 128), A.mult)
+        act(ap("D", n0, n0 + 128), ind(ap("YS", 256, 512), ln), F.Relu)
+        for c in (0, 4096, 8192):
+            tt(ind(ap("RW", c, c + 2304), ap("LS", 8, 16)), ap("RB", 0, 128), ap("XS", 0, 128), A.add)
+            if c < 8192:
+                act(ap("RW", c + n0, c + n0 + 128), ind(ap("HB", 0, 256), ln))
+                r = 128 * (c // 4096)
+                act(ap("RW", c + 2176, c + 2304), ap("RSV", r, r + 128))
+        tt(ind(ap("D", 0, 2304), ap("LS", 0, 8)), ap("W1", 0, 128), ap("E2", 128, 256), A.add)
 
     prep(0)
+    spread(0)
     for t in range(NV):
-        steps = [(start_nodes, 0), (start_nodes, 1), (guards, 0), (gather, 2, 0), (gather, 2, 1), (tail, 2, 0), (guards, 1),
-                 (gather, 1, 0), (tail, 2, 1), (gather, 1, 1), (prep_next,), (tail, 1, 0), (tail, 1, 1), (gather, 0, 1)]
         if t % 2:
-            steps += [(gather, 0, 0), (early3,), (tail, 0, 0), (source,), (final_guards, 0), (move_down,), (meet,), (acts,)]
+            ms(ap("D0", 4, 40, 5), 1.0)
+        if t + 1 < NV:
+            spread(t + 1)
+        steps = [(start_nodes, 0), (start_nodes, 1), (guards, 0), (gather, 2, 0), (compare, 2, 0), (gather, 2, 1), (compare, 2, 1), (tail, 2, 0), (guards, 1),
+                 (gather, 1, 0), (compare, 1, 0), (tail, 2, 1), (gather, 1, 1), (compare, 1, 1), (prep_next,), (tail, 1, 0), (tail, 1, 1),
+                 (gather, 0, 1), (gather, 0, 0), (early3,), (source,)]
+        late = [(compare, 0, 1)]
+        if t % 2:
+            steps += late * ORDER[1] + [(move_down,), (compare, 0, 0), (meet,)] + late * (1 - ORDER[1]) + [(tail, 0, 0), (acts,), (final_guards, 0)]
         else:
-            steps += [[(early3,), (source,), (meet,), (acts,), (gather, 0, 0), (tail, 0, 0)],
-                      [(gather, 0, 0), (early3,), (source,), (meet,), (tail, 0, 0), (acts,)],
-                      [(gather, 0, 0), (early3,), (source,), (meet,), (acts,), (tail, 0, 0)],
-                      [(early3,), (source,), (meet,), (gather, 0, 0), (tail, 0, 0), (acts,)]][EVEN]
-            steps += [(final_guards, 0), (split_rows,), (place_rows,)]
+            steps += late * ORDER[0] + [(split_rows,), (compare, 0, 0), (meet,), (acts,)] + late * (1 - ORDER[0]) + [(tail, 0, 0), (final_guards, 0), (place_rows,)]
         steps += [(tail, 0, 1), (final_guards, 1), (write_back,)]
         for s_ in steps:
             stage[0] += 1
@@ -659,7 +715,8 @@ def rank_program(g, core, T, topo):
         for k in seq:
             t0 = first[k]
             for j, l in pre[k]:
-                t0 = max(t0, at[j] + cost[j] + l)
+                if at[j] + cost[j] + l > t0:
+                    t0 = at[j] + cost[j] + l
             st, en = busy[engs[k]]
             lo, hi = 0, len(en)
             while lo < hi:
@@ -708,7 +765,8 @@ def rank_program(g, core, T, topo):
                 key = (base + near * (rng.normal(0.0, SHAKE, n) + st_[stages])).tolist()
             for k in range(n):
                 for j, l in fwd[k]:
-                    key[k] = max(key[k], key[j] + 0.001)
+                    if key[j] + 0.001 > key[k]:
+                        key[k] = key[j] + 0.001
             seq = sorted(range(n), key=lambda k: key[k])
             for it in range(PASSES):
                 at = place(seq, fwd, zero)

@@ -1,3 +1,4 @@
+import math
 import numpy as np
 from concourse.bass import DstId, RemoteDMATransfer
 from concourse.mybir import AluOpType as A, ActivationFunctionType as F
@@ -9,6 +10,9 @@ HUGE = float(2 ** 40)
 MEET = ("X", "Y")
 ACTS = ("X0", "M")
 ORDER = (0, 0)
+JOIN = 1
+PBCS = 3
+OWN = 16
 FAR = 16384.0
 CC = 32768.0
 RND, RN2 = 1.5 * 2 ** 38, 1.5 * 2 ** 24
@@ -16,28 +20,28 @@ f32, bf, i32, u16, f16 = "float32", "bfloat16", "int32", "uint16", "float16"
 
 SB = {
     "RW": (10496, bf), "RSV": (256, bf), "D": (2304, f32), "NDI": (1792, i32),
-    "XZ": (1024, bf), "VSO": (64, i32), "VSR": (64, i32), "XT": (1024, bf), "L2": (64, u16),
+    "XZ": (2048, bf), "VSO": (64, i32), "VSR": (64, i32), "L2": (64, u16),
     "GF": (960, f32), "GR": (960, f32), "KS": (32, f32), "KR": (32, f32), "K0": (8, f32),
-    "KA": (8, f32), "KT": (16, f32), "NIB": (128, bf), "R0": (16, bf), "HB": (256, bf), "IB": (128, bf), "IF": (128, f32), "ONE": (128, bf), "RBIG": (512, bf),
+    "KA": (8, f32), "KT": (16, f32), "NIB": (128, bf), "R0": (16, bf), "HB": (384, bf), "IB": (128, bf), "IF": (128, f32), "ONE": (128, bf), "RBIG": (512, bf),
     "BK3": (24, bf), "BKF": (8, f32), "SC": (24, bf), "SCT": (64, bf), "SX": (512, bf),
-    "TRC": (128, bf), "PBC": (2048, bf), "BLK": (128, bf), "TRL": (512, bf), "SELG": (1024, bf),
-    "CK": (768, bf), "RS": (384, f32), "MKI": (384, i32), "MKJ": (384, i32), "MK": (384, f32), "NMK": (16, f32),
+    "TRC": (128, bf), "PBC": (2048, bf), "OP": (128, u16), "XQ": (128, bf), "WL": (136, f32), "GZ": (48, bf), "FX": (512, f16), "FT": (512, f16), "SQ": (16, f32), "PP": (8, f32),
+    "CK": (768, bf), "RS": (384, f32), "MKI": (128, i32), "MKJ": (128, i32), "MK": (128, f32), "NMK": (16, f32),
     "PM": (4, f32), "DU0": (24, f32), "DUM": (24, f32), "NCB": (512, bf), "NIF": (128, f32), "TRZ": (128, bf),
     "XR": (8192, bf), "RF": (2048, f16), "GP": (48, f32), "THA": (16, f32), "SS": (136, f32), "GT": (128, f32),
     "OCI": (128, i32), "OC": (128, u16), "O5I": (48, i32), "O5": (48, u16),
     "EU": (256, u16), "FA": (256, bf), "FB": (256, bf), "FW": (768, f16),
     "R": (4096, bf), "CMP": (4096, bf), "PEN": (256, bf), "SCN": (768, f32),
     "MI": (48, i32), "LO": (48, i32), "THR": (48, i32), "D0": (240, f32), "D1": (240, f32),
-    "VS": (160, f32), "AX": (256, f16), "LV": (32, u16), "AV": (256, f16), "AL": (128, f16),
-    "AG": (768, f32), "LG": (48, u16), "RG": (768, bf), "CG": (768, bf), "T1": (48, f32), "T2": (48, f32),
-    "DH": (40, f32), "HS": (40, f32), "AA": (128, f32), "LA": (8, u16), "PRE": (24, f32),
-    "EB": (128, f32), "FR": (128, bf), "S8": (8, f32), "DD": (8, f32), "HH": (8, f32),
-    "NQ": (8, f32), "Q8": (8, f32), "ASK": (16, bf), "ACT": (16, bf), "ABT": (256, f16),
-    "AB": (2048, f32), "EQ": (2048, bf), "AC": (128, bf), "LT": (24, f32), "LU": (24, f32), "LS": (24, u16),
+    "VS": (200, f32), "AX": (256, f16), "LV": (128, u16), "AV": (256, f16), "AL": (128, f16),
+    "AG": (256, f32), "LG": (192, u16), "RG": (768, bf), "CG": (768, bf), "T1": (48, f32), "T2": (48, f32),
+    "DH": (40, f32), "AA": (128, f32), "LA": (8, u16), "LC": (24, f16), "SD": (24, bf), "DG": (1024, bf),
+    "EB": (128, f32), "FR": (128, bf),
+    "NQ": (8, f32), "Q8": (8, f32), "ASK": (16, bf), "ACT": (16, bf),
+    "EQ": (2048, bf), "AC": (128, bf), "LU": (24, f32), "LS": (24, u16),
     "YS": (512, f32), "GE": (256, bf), "ST": (128, bf),
     "W1": (256, f32), "W2": (128, f32), "W6": (128, f32), "E2": (256, f32),
     "U": (512, f32), "MM": (2048, f32), "GD": (128, f32),
-    "RB": (256, bf), "XS": (256, bf), "YG": (768, f32),
+    "RB": (128, bf), "YG": (256, f32),
 }
 PS = ["X0", "X1", "Y0", "Y1", "C", "K", "M", "M2"]
 SCRATCH, AT = {}, {}
@@ -47,16 +51,21 @@ for k_, (n_, d_) in SB.items():
     AT[k_] = (pool_, used_)
     SCRATCH[pool_] = ("sbuf", [128, used_ + (n_ + 31) // 32 * 32], d_)
 SCRATCH.update({k: ("psum", [128, 512], f32) for k in PS})
-DMAS = ["ld%d" % i for i in range(8)] + ["st%d" % i for i in range(6)]
-SEMAPHORES = ["qv", "qs", "qp", "qg", "sent"] + DMAS + ["%s%d" % (a, t) for a in ("in", "ga", "gb", "ks") for t in (1, 2, 3)]
-CHUNKS = (((0, 512), (512, 1024), (1024, 1536), (1536, 2048)), ((0, 1024), (1024, 1536), (1536, 2048)), ((0, 1024), (1024, 2048)))
+DMAS = ["ld%d" % i for i in range(8)] + ["st%d" % i for i in range(5)]
+SEMAPHORES = ["qv", "qs", "qp", "qg", "sent"] + DMAS + ["%s%d" % (a, t) for a in ("in", "ga", "gb", "la", "lb", "ks") for t in (1, 2, 3)]
+CHUNKS = (((0, 512), (512, 1024), (1024, 1536), (1536, 2048)), ((0, 1024), (1024, 1536), (1536, 2048)), ((0, 1024), (1024, 2048)),
+          ((0, 512), (512, 1024), (1024, 2048)))
 BOTH = [("DDAA", 0, 1, 0), ("DDDA", 0, 1, 0)]
 CFG = BOTH * 2 + [("DCCE", 0, 0, 0), ("DDDD", 0, 0, 0)] + BOTH * 9
 LEADS = [1000.0 * i for i in range(-2, 14)]
 SHARE = {1: (0, 4), 2: (4, 6), 3: (6, 8)}
 OTHERS = [(1.1, 2.2, 0.87, 200.0, 1.6), (1.3, 3.0, 0.9, 120.0, 2.0), (2.0, 5.0, 1.0, 150.0, 1.0)]
 WINDOW = 8000.0
-ROUNDS, PASSES, SHAKE = 1900, 2, 200.0
+RUN = 8
+ROUNDS, PASSES, SHAKE = 700, 2, 200.0
+CALM, FRESH = 120, 3
+SLOWG = 1.2
+MOVES, TRIES, REACH, HEAT, KEEP = 46000, 40, 6, 100.0, (0, 2)
 PLAN = {}
 
 GATH, SCAT = 1.35, 3.4
@@ -180,8 +189,8 @@ def rank_program(g, core, T, topo):
     def ms(out, c):
         return op("v", lambda: g.vector.memset(real(out), c), [out], [], 60.0 + width(out) * (0.5 if two(out) else 1.0))
 
-    def scan(out, d0, d1, o0, o1):
-        return op("v", lambda: g.vector.tensor_tensor_scan(real(out), real(d0), real(d1), 0.0, o0, o1), [out], [d0, d1], 60.0 + width(out))
+    def scan(out, d0, d1, o0, o1, first=0.0):
+        return op("v", lambda: g.vector.tensor_tensor_scan(real(out), real(d0), real(d1), first, o0, o1), [out], [d0, d1], 60.0 + width(out))
 
     def act(out, a, fn=F.Identity, bias=None, scale=None, **kw):
         ar = {}
@@ -197,15 +206,21 @@ def rank_program(g, core, T, topo):
         c = max(min(64, width(l)), width(r)) * (4 if SB[l[0]][1] == f32 else 1)
         return op("p", lambda: g.tensor.matmul(real(out), real(l), real(r), start, stop), [out], [l, r], PE0 + PE1 * c, **kw)
 
+    def mms(calls, **kw):
+        c = sum(PE0 + PE1 * max(min(64, width(l)), width(r)) * (4 if SB[l[0]][1] == f32 else 1) for o, l, r, a, b in calls)
+        def call():
+            return [g.tensor.matmul(real(o), real(l), real(r), a, b) for o, l, r, a, b in calls][-1]
+        return op("p", call, [calls[0][0]], sorted(set(x for o, l, r, a, b in calls for x in (l, r))), c, **kw)
+
     def iota(out, pat, base, cm):
         if SB[out[0]][1] == i32:
             fn = lambda: g.iota(real(out), pat, base, cm)
         else:
             fn = lambda: g.iota(real(out), pat, base, cm, allow_small_or_imprecise_dtypes=True)
-        return op("g", fn, [out], [], 150.0 + 2 * width(out))
+        return op("g", fn, [out], [], SLOWG * (150.0 + 2 * width(out)))
 
     def sel(out, a, pat, cmp, base, cm, fill=0.0, **kw):
-        return op("g", lambda: g.affine_select(real(out), real(a), pat, cmp, fill, base, cm), [out], [a], 200.0 + 2 * width(out), **kw)
+        return op("g", lambda: g.affine_select(real(out), real(a), pat, cmp, fill, base, cm), [out], [a], SLOWG * (200.0 + 2 * width(out)), **kw)
 
     nd_ = [0, 0]
     outs_ = []
@@ -221,7 +236,7 @@ def rank_program(g, core, T, topo):
         nd_[1] += 1
         outs_.append(s)
         e = g.sync if q == "y" else g.scalar
-        return op(q, lambda: e.dma_start(dst, real(a)), [], [a], 60.0, sem=s, lat=ns)
+        return op(q, lambda: e.dma_start(dst, real(a)), [], [a], 400.0 if q == "y" else 60.0, sem=s, lat=ns)
 
     sent = [0]
 
@@ -247,7 +262,7 @@ def rank_program(g, core, T, topo):
                                                       remote_sem=T.sem[sem], src=real(s), dst=real(o))
                                     for dst, rid, pid, o, s, sem, e0 in trs], local_sem=T.sem["sent"])
             return None
-        return op("g", call, [], ins, 1000.0)
+        return op("g", call, [], ins, 1000.0 if sent[0] > 16 else 2500.0)
 
     l0 = load("y", ap("RW", 0, 2048), T.rg[:, 0:2048], 3500.0)
     load("s", ap("VSO", 0, 64), T.vs[:, :], 2000.0)
@@ -261,25 +276,27 @@ def rank_program(g, core, T, topo):
     cp(ap("OC", 0, 128), ap("OCI", 0, 128))
     sel(ap("IB", 0, 128), ap("ONE", 0, 128), [[-1, 128]], A.is_equal, 0, 1)
     act(ap("RW", 6144, 8192), ind(ap("IB", 0, 128), ap("OC", 0, 128)))
-    cp(ap("IF", 0, 128), ap("IB", 0, 128))
-    ms(ap("RBIG", 0, 128), 0.0)
-    ms(ap("RBIG", 384, 512), 0.0)
-    ts(ap("RBIG", 128, 256), ap("IB", 0, 128), BIG, A.mult)
-    ts(ap("RBIG", 256, 384), ap("IB", 0, 128), -BIG, A.mult)
+    act(ap("IF", 0, 128), ap("IB", 0, 128))
+    for c, w_ in ((128, BIG), (256, -BIG), (384, 0.0)):
+        act(ap("RBIG", c, c + 128), ap("IB", 0, 128), scale=w_)
     sel(ap("BK3", 0, 24), ap("ONE", 0, 24), [[0, 3], [-16, 8]], A.is_ge, 0, 1)
     sel(ap("BK3", 0, 24), ap("BK3", 0, 24), [[0, 3], [16, 8]], A.is_ge, 15, -1)
     cp(ap("BKF", 0, 8), ap("BK3", 0, 8))
     ts(ap("SC", 0, 24), ap("BK3", 0, 24), -4096.0, A.mult)
-    iota(ap("O5I", 0, 48), [[5, 48]], 4, 0)
-    cp(ap("O5", 0, 48), ap("O5I", 0, 48))
-    iota(ap("MKI", 0, 384), [[0, 24], [-1, 16]], 16, 1)
-    ts(ap("MKJ", 0, 384), ap("MKI", 0, 384), 15, A.bitwise_and)
-    ts(ap("MK", 0, 384), ap("MKJ", 0, 384), 0.0, A.is_equal)
+    iota(ap("O5I", 0, 8), [[5, 8]], 4, 0)
+    cp(ap("O5", 0, 8), ap("O5I", 0, 8))
+    iota(ap("MKI", 0, 128), [[0, 8], [-1, 16]], 16, 1)
+    ts(ap("MKJ", 0, 128), ap("MKI", 0, 128), 15, A.bitwise_and)
+    ts(ap("MK", 0, 128), ap("MKJ", 0, 128), 0.0, A.is_equal)
     ts(ap("NMK", 0, 16), ap("MK", 0, 16), -1.0, A.mult, 1.0, A.add)
     cp(ap("PM", 0, 1), ap("MKJ", 0, 1))
     iota(ap("DU0", 0, 16), [[16, 16]], 2048, 0)
     iota(ap("DU0", 16, 24), [[16, 8]], 128, 0)
     ts(ap("DUM", 0, 24), ap("DU0", 0, 24), ap("PM", 0, 1), A.add)
+    ts(ap("LC", 0, 16), ap("ONE", 0, 16), 4096.0, A.mult)
+    ts(ap("LC", 16, 24), ap("DUM", 16, 24), 128.0, A.add)
+    sel(ap("SD", 0, 16), ap("SC", 0, 16), [[0, 16]], A.is_equal, 0, 0)
+    act(ap("SD", 16, 24), ap("BK3", 0, 8), scale=-256.0)
     ms(ap("CK", 0, 768), 0.0)
     ms(ap("CK", 128, 384, 1, 0, 32), BIG / 32)
     ms(ap("CK", 0, 512, 1, 32, 64), 64.0)
@@ -288,20 +305,16 @@ def rank_program(g, core, T, topo):
     ms(ap("D0", 0, 240), 1.0)
     ms(ap("D0", 0, 240, 5), 0.0)
     ms(ap("D1", 0, 240), 0.0)
-    ms(ap("DH", 0, 40), 0.0)
     ms(ap("THR", 0, 48), 2 ** 25)
-    ms(ap("SS", 0, 1), 0.0)
-    ms(ap("GP", 0, 1), 0.0)
     ms(ap("ACT", 8, 9), -1.0 / 256)
-    ms(ap("W1", 128, 256), 1.0)
-    ms(ap("RW", 10240, 10496), 0.0)
-    ms(ap("D", 1792, 2304), 0.0)
-    iota(ap("YS", 384, 512), [[0, 128]], 0, 0)
-    ms(ap("PRE", 16, 24), -128.0)
+    act(ap("D", 1792, 2048), ap("CK", 512, 768))
+    for name, c0, c1, x in (("SS", 0, 1, 0), ("GP", 0, 1, 0), ("W1", 128, 256, 1), ("RW", 10240, 10496, 0), ("D", 2048, 2304, 0), ("YS", 384, 512, 0),
+                            ("DH", 0, 40, 0), ("SX", 0, 256, -1), ("SX", 256, 512, -1), ("NCB", 256, 384, CC / 8), ("NCB", 384, 512, -FAR / 128), ("NIF", 0, 128, -1)):
+        iota(ap(name, c0, c1), [[0, c1 - c0]], int(x), 0)
     for name, plain, sums in (("K0", 12, 8.0), ("KA", 1, 2.0)):
         iota(ap(name, 0, 8), [[0, 8]], plain, 0)
         sel(ap(name, 0, 8), ap(name, 0, 8), [[-32, 8]], A.is_ge, 0, 1, sums)
-    ts(ap("NIB", 0, 128), ap("IB", 0, 128), -1.0, A.mult)
+    act(ap("NIB", 0, 128), ap("IB", 0, 128), scale=-1.0)
     cp(ap("D", 0, 896), ap("NDI", 0, 896))
     cp(ap("D", 896, 1792), ap("NDI", 896, 1792))
     act(ap("RW", 4096, 6144), ap("RW", 0, 2048))
@@ -311,34 +324,46 @@ def rank_program(g, core, T, topo):
         ms(ap("RW", c, c + 1), 300.0)
     act(ap("RSV", 0, 128), ap("RW", 2176, 2304))
     act(ap("RSV", 128, 256), ap("RW", 6272, 6400))
-    sz = send([(t, ap("XZ", 256 * t, 256 * t + 256), ap("XZ", 0, 256), "in%d" % t, SHARE[t]) for t in (1, 2, 3)], [ap("XZ", 0, 256)])
+    mms([(ap("C", 256 + 128 * h, 384 + 128 * h), ap("XZ", 128 * h, 128 * h + 128), ap("IB", 0, 128), True, True) for h in range(2)])
+    act(ap("XZ", 256, 512), ap("C", 256, 512))
+    sz = send([(t, ap("XZ", 512 * t, 512 * t + 512), ap("XZ", 0, 512), "in%d" % t, SHARE[t]) for t in (1, 2, 3)], [ap("XZ", 0, 512)])
     sv = send([(t, ap("VSR", 16 * t, 16 * t + 16), ap("VSO", 16 * t, 16 * t + 16), "in%d" % t, SHARE[t]) for t in (1, 2, 3)], [ap("VSO", 0, 64)])
-    ms(ap("SX", 0, 512), -1.0)
     for j, t in enumerate((0, 2)):
         sel(ap("SCT", 32 * j + 8, 32 * j + 24), ap("ONE", 0, 16), [[-8, 2], [-16, 8]], A.is_equal, -t, 1)
         sel(ap("SX", 256 * j, 256 * j + 256), ap("SX", 256 * j, 256 * j + 256), [[-8, 2], [-16, 8], [0, 16]], A.is_equal, -t, 1)
+    for j, i in enumerate((8, 0, 10, 2)):
+        for c, how in ((256 * j, A.not_equal), (256 * j + 128, A.is_equal)):
+            sel(ap("DG", c, c + 128), ap("IB", 0, 128), [[0, 8], [1, 16]], how, -i, 0)
     for name, above, on in (("TRZ", -FAR, FAR), ("TRC", CC, -15 * CC)):
         iota(ap(name, 0, 128), [[0, 128]], int(above), 0)
         sel(ap(name, 0, 128), ap(name, 0, 128), [[-16, 8], [0, 16]], A.is_ge, 0, 1)
         sel(ap(name, 0, 128), ap(name, 0, 128), [[16, 8], [1, 16]], A.is_ge, 0, -1)
+        if name == "TRC":
+            if PBCS:
+                iota(ap("MKI", 0, 128), [[1, 16], [16, 8]], 0, 0)
+                cp(ap("OP", 0, 128), ap("MKI", 0, 128))
+            for c in range(8, 8 + 40 * PBCS, 40):
+                act(ap("PBC", 16 * c, 16 * c + 640), ind(ap("TRC", 0, 128), ap("OP", c, c + 40)))
+            if PBCS < 3:
+                iota(ap("PBC", 0, 128), [[0, 128]], int(CC), 0)
+                sel(ap("PBC", 0, 128), ap("PBC", 0, 128), [[-16, 8], [0, 16]], A.is_ge, 0, 1)
+            for i in range(1 + 5 * PBCS, 16):
+                sel(ap("PBC", 128 * i, 128 * i + 128), ap("PBC", 0, 128), [[16, 8], [0, 16]], A.is_ge, i, -1)
         sel(ap(name, 0, 128), ap(name, 0, 128), [[-1, 128]], A.not_equal, 0, 1, on)
-    act(ap("NIF", 0, 128), ap("IB", 0, 128), scale=-1.0)
-    ms(ap("TRL", 0, 512), 4096.0)
-    sel(ap("TRL", 0, 512), ap("TRL", 0, 512), [[0, 4], [-1, 128]], A.is_ge, 0, 1)
-    sg = ap("SELG", 0, 1024, 1, 0, 8)
-    ms(sg, 1.0)
-    sel(sg, sg, [[-1, 8], [0, 128]], A.is_equal, 0, 1)
-    nc = ap("NCB", 0, 256, 1, 0, 32)
-    iota(nc, [[0, 2], [1, 128]], 0, 0)
-    sel(nc, nc, [[0, 256]], A.is_equal, 0, 1)
+    sel(ap("NIF", 0, 128), ap("NIF", 0, 128), [[-1, 128]], A.is_equal, 0, 1)
+    sel(ap("GT", 0, 128), ap("W1", 128, 256), [[1, 128]], A.is_ge, 0, -1, 1.0 / 3)
+    scan(ap("WL", 0, 128), ap("GT", 0, 128), ap("W1", 128, 256), A.mult, A.mult, 1e29)
+    act(ap("WL", 128, 129), ap("WL", 127, 128), scale=4.0)
+    for c in (0, 256):
+        cp(ap("FX", c, c + 256), ap("CK", 512, 768))
+    for c in (257, 258, 401, 402):
+        ts(ap("FX", c, 384 + c // 384 * 128, 32), ap("ONE", 0, 4), -64.0, A.mult)
     for j in range(2):
+        nc = ap("NCB", 128 * j, 128 * j + 128, 1, 0, 32)
+        iota(nc, [[1, 128]], 0, 0)
+        sel(nc, nc, [[0, 128]], A.is_equal, 0, 1)
         ms(ap("NCB", 128 * j, 128 * j + 128, 1, 32, 64), (4096 + 1792 + 128 * j - FAR) / 32)
-    ms(ap("NCB", 256, 384), CC / 8)
-    ms(ap("NCB", 384, 512), -FAR / 128)
-    iota(ap("BLK", 0, 128), [[0, 128]], int(CC), 0)
-    sel(ap("BLK", 0, 128), ap("BLK", 0, 128), [[-16, 8], [0, 16]], A.is_ge, 0, 1)
-    for i in range(16):
-        sel(ap("PBC", 128 * i, 128 * i + 128), ap("BLK", 0, 128), [[16, 8], [0, 16]], A.is_ge, i, -1)
+
 
     xb = [0, 0]
     KB, CB = ("M2", "K"), ("M", "C")
@@ -357,15 +382,12 @@ def rank_program(g, core, T, topo):
         return {"waits": [("%s%d" % (kind, t), 8)], "after": {sends[kind, t]: 3000.0}}
 
     def xs(t, h):
-        return ap("XZ", 256 * t + 128 * h, 256 * t + 128 * h + 128)
+        return ap("XZ", 512 * t + 128 * h, 512 * t + 128 * h + 128)
 
     def kcol(t, j=0):
         return ap("K0", j, j + 1) if t == 0 else ap("KR", 8 * t + j, 8 * t + j + 1)
 
     def prep(t):
-        for h in range(2):
-            mm(ap("C", 256 + 128 * h, 384 + 128 * h), xs(t, h), ap("IB", 0, 128), **arrived("in", t))
-        act(ap("XT", 256 * t, 256 * t + 256), ap("C", 256, 512))
         cp(ap("L2", 16 * t, 16 * t + 16), ap("VSR" if t else "VSO", 16 * t, 16 * t + 16), **arrived("in", t))
 
     def prep_next(t):
@@ -376,32 +398,31 @@ def rank_program(g, core, T, topo):
         c = 16 * t + 8 * h
         tt(ap("AV", 128 * h, 128 * h + 128), ind(ap("VSR" if t else "VSO", c, c + 8), ap("OC", 0, 8)), ap("MK", 0, 128), A.mult, **arrived("in", t))
         mm(ap(CB[h], 200, 208), ap("AV", 128 * h, 128 * h + 128), ap("BK3", 0, 8))
-        cp(ap("D1", 120 * h + 80, 120 * h + 120, 5), ap(CB[h], 200, 208))
+        act(ap("D1", 120 * h + 80, 120 * h + 120, 5), ap(CB[h], 200, 208))
 
     def guards(t, h):
         o, w = 384 * h, 24 * h
-        gr = 240 * t + 120 * h
-        tt(ap("AG", o, o + 384), ind(ap("GR", gr, gr + 120), ap("O5", 0, 24)), ap("MK", 0, 384), A.mult, **arrived("ga" if h == 0 else "gb", t))
+        gr, lg, kind = 240 * t + 120 * h, 48 * t + w, "ga" if h == 0 else "gb"
+        tt(ap("AG", 128 * h, 128 * h + 128), ind(ap("GR", gr, gr + 40), ap("O5", 0, 8)), ap("MK", 0, 128), A.mult, **arrived(kind, t))
+        act(ap("GZ", w, w + 24), ap("GR", gr + 4, gr + 120, 5), F.Relu, bias=1.0, scale=-1.0, **arrived(kind, t))
         x = b = "Y0" if h == 0 else xbank(h)
-        for k in range(3):
-            mm(ap(b, 448 + 8 * k, 456 + 8 * k), ap("AG", o + 128 * k, o + 128 * k + 128), ap("BKF", 0, 8))
-        cp(ap("LG", w, w + 24), ap(b, 448, 472))
-        act(ap("RG", o, o + 384), ind(ap("RW", 0, 4096), ap("LG", w, w + 24)))
-        for k in range(3):
-            mm(ap(x, 128 * k, 128 * k + 128), ap("IB", 0, 128), xs(t, h), **arrived("in", t))
-        tt(ap("CG", o, o + 384), ap("RG", o, o + 384), ap(x, 0, 384), A.is_le)
-        for k in range(3):
-            mm(ap(b, 416 + 8 * k, 424 + 8 * k), ap("RG", o + 128 * k, o + 128 * k + 128), ap("SC", 0, 8))
-        for k in range(3):
-            mm(ap(b, 384 + 8 * k, 392 + 8 * k), ap("CG", o + 128 * k, o + 128 * k + 128), ap("BK3", 0, 8))
+        mm(ap(b, 448, 456), ap("AG", 128 * h, 128 * h + 128), ap("BKF", 0, 8))
+        cp(ap("LG", lg, lg + 8), ap(b, 448, 456))
+        act(ap("RG", o, o + 384), ind(ap("RW", 0, 4096), ap("LG", lg, lg + 24)), **arrived("la" if h == 0 else "lb", t))
+        mms([c for k in range(3) for c in ((ap(x, 128 * k, 128 * k + 128), ap("IB", 0, 128), xs(t, h), True, False),
+                                           (ap(x, 128 * k, 128 * k + 128), ap("NIB", 0, 128), ap("RG", o + 128 * k, o + 128 * k + 128), False, True))], **arrived("in", t))
+        mms([(ap(b, 416 + 8 * k, 424 + 8 * k), ap("RG", o + 128 * k, o + 128 * k + 128), ap("SC", 0, 8), True, True) for k in range(3)])
+        act(ap("CG", o, o + 384), ap(x, 0, 384), F.Sign, bias=0.5)
+        mms([(ap(b, 384, 408), ap("RBIG", 256, 384), ap("GZ", w, w + 24), True, False)]
+            + [(ap(b, 384 + 8 * k, 392 + 8 * k), ap("CG", o + 128 * k, o + 128 * k + 128), ap("BK3", 0, 8), False, k == 2) for k in range(3)])
         cnt = ap(b, 384, 408)
-        ts(ap("T1", w, w + 24), cnt, kcol(t), A.is_lt, NOG, A.mult, **arrived("ks", t))
+        ts(ap("T1", w, w + 24), cnt, kcol(t, 4), A.is_lt, NOG, A.mult, **arrived("ks", t))
         tt(ap("THR", w, w + 24), ap("T1", w, w + 24), ap(b, 416, 440), A.add)
-        ts(ap("D0", 120 * h + 1, 120 * h + 120, 5), ap("T1", w, w + 24), 0.0, A.is_gt)
+        act(ap("D0", 120 * h + 1, 120 * h + 120, 5), ap("T1", w, w + 24), F.Sign)
         tt(ap("D1", 120 * h + 1, 120 * h + 120, 5), ap("GR", gr + 4, gr + 120, 5), ap("T1", w, w + 24), A.subtract, **arrived("ga" if h == 0 else "gb", t))
 
     def vlist(t, s, h):
-        return ap("L2", 16 * t + 8 * h, 16 * t + 8 * h + 8) if s == 2 else ap("LV", 16 * s + 8 * h, 16 * s + 8 * h + 8)
+        return ap("L2", 16 * t + 8 * h, 16 * t + 8 * h + 8) if s == 2 else ap("LV", 32 * t + 16 * h + 8 * s, 32 * t + 16 * h + 8 * s + 8)
 
     def cfg(t, s, h):
         return CFG[6 * t + 2 * s + h]
@@ -410,11 +431,18 @@ def rank_program(g, core, T, topo):
         n = 128 - 32 * cfg(t, s, h)[0].count("A")
         return [(0, n, "R", 2048 * h)] + [(n, 128, "RF", 1024 * h - 1024)] * (n < 128)
 
+    def fused(t):
+        return [32 * max(cfg(t, s, h)[0].count("A") for s in range(3)) for h in range(2)]
+
     def spread(t):
+        n = fused(t)
+        def copy(out, a, own, **kw):
+            (cp(out, a) if own else sel(out, a, [[0, width(a)]], A.is_equal, 0, 0, **kw))
         for h in range(2):
-            n, e = 32 * max(cfg(t, s, h)[0].count("A") for s in range(3)), 2048 * t + 1024 * h + 1024
-            for i in range(16 if n else 0):
-                sel(ap("XR", e - 16 * n + i, e, 16), ap("XZ", 256 * t + 128 * h + 128 - n, 256 * t + 128 * h + 128), [[0, n]], A.is_equal, 0, 0, **arrived("in", t))
+            c = 512 * t + 128 * h + 128
+            copy(ap("XQ", h * n[0], n[0] + h * n[1]), ap("XZ", c - n[h], c), t == 0 and OWN, **arrived("in", t))
+        for i in range(16):
+            copy(ap("XR", 2048 * t + i, 2048 * t + 16 * sum(n), 16), ap("XQ", 0, sum(n)), t == 0 and i < OWN)
 
     def gather(t, s, h):
         o = 128 * h
@@ -428,16 +456,21 @@ def rank_program(g, core, T, topo):
         for c0, c1 in CHUNKS[ch]:
             src, kind = ind(ap("RW", 0, 10240), ap("EU", o + c0 // 16, o + c1 // 16)), kinds[c0 // 512]
             if kind == "A":
-                c = 1024 * h - 1024
-                tt(ap("RF", c + c0, c + c1), src, ap("XR", 2048 * t + c + c0, 2048 * t + c + c1), A.subtract)
+                c, x = 1024 * h - 1024, 2048 * t + 16 * sum(fused(t)[:h + 1]) - 2048
+                tt(ap("RF", c + c0, c + c1), src, ap("XR", x + c0, x + c1), A.subtract)
             else:
                 (cp if kind == "E" else act)(ap("R", 2048 * h + c0, 2048 * h + c1), src)
+        if s == 2 and JOIN:
+            if h == 0:
+                return
+            o, e = 0, ap("EU", 0, 256)
+        n = width(e)
         if s or whole:
-            ts(ap("FA", o, o + 128), e, 4096.0, A.is_ge)
+            ts(ap("FA", o, o + n), e, 4096.0, A.is_ge)
         if s == 2:
-            ts(ap("FB", o, o + 128), e, 8192.0, A.is_ge)
+            ts(ap("FB", o, o + n), e, 8192.0, A.is_ge)
         for k in range(s + 1):
-            ts(ap("FW", 384 * h + 128 * k, 384 * h + 128 * k + 128), e, -4096.0 * k - 2048.0, A.add)
+            ts(ap("FW", 256 * k + o, 256 * k + o + n), e, -4096.0 * k - 2048.0, A.add)
 
     def compare(t, s, h):
         o = 128 * h
@@ -445,10 +478,12 @@ def rank_program(g, core, T, topo):
         for q in range(4):
             c = 2048 * h + 512 * q
             if kinds[q] == "A":
-                ts(ap("CMP", c, c + 512), ap("RF", c - 1024 * (h + 1), c - 1024 * (h + 1) + 512), 0.0, A.is_le)
+                for c0, c1 in CHUNKS[cfg(t, s, h)[1]]:
+                    if c0 == 512 * q:
+                        ts(ap("CMP", c, c + c1 - c0), ap("RF", 1024 * h - 1024 + c0, 1024 * h - 1024 + c1), 0.0, A.is_le)
                 continue
             x = "Y1" if t and s == 2 and h == 0 else xbank(h)
-            mm(ap(x, 0, 512), ap("XT", 256 * t + o, 256 * t + o + 128), ap("RW", 6144 + 512 * q, 6656 + 512 * q), True, kinds[q] != "D")
+            mm(ap(x, 0, 512), ap("XZ", 512 * t + 256 + o, 512 * t + 384 + o), ap("RW", 6144 + 512 * q, 6656 + 512 * q), True, kinds[q] != "D", **arrived("in", t))
             if kinds[q] == "D":
                 mm(ap(x, 0, 512), ap("NIB", 0, 128), ap("R", c, c + 512), False, True)
                 act(ap("CMP", c, c + 512), ap(x, 0, 512), F.Sign, bias=0.5)
@@ -457,8 +492,8 @@ def rank_program(g, core, T, topo):
 
     def by_entry(t, s, h, bank, c0, c1, w):
         for p0, p1, name, base in spans(t, s, h):
-            for i in range(16):
-                mm(ap(bank, c0 + i, c1, 16, p0, p1), ap(name, base + 16 * p0 + i, base + 16 * p1, 16), w, False, False)
+            for i0 in range(0, 16, RUN):
+                mms([(ap(bank, c0 + i, c1, 16, p0, p1), ap(name, base + 16 * p0 + i, base + 16 * p1, 16), w, False, False) for i in range(i0, i0 + RUN)])
 
     def tail(t, s, h):
         o, n, w, W = 128 * h, 128 * (s + 1), 24 * h, 8 * (s + 1)
@@ -471,17 +506,16 @@ def rank_program(g, core, T, topo):
         if s == 2:
             mm(ap(K, 128, n), ap("FB", o, o + 128), ap("RBIG", 128, n), False, False)
         for k in range(s + 1):
-            mm(ap(K, 128 * k, 128 * k + 128), ap("FW", 384 * h + 128 * k, 384 * h + 128 * k + 128), ap("IB", 0, 128), False, False)
+            mm(ap(K, 128 * k, 128 * k + 128), ap("FW", 256 * k + o, 256 * k + o + 128), ap("IB", 0, 128), False, False)
         by_entry(t, s, h, K, 0, n, ap("SC", 0, W))
         for p0, p1 in ((0, 64), (64, 128)) if cfg(t, s, h)[3] else ((0, 128),):
-            for i in range(16):
-                mm(ap(C, c0 + i, c0 + 128, 16, p0, p1), ap("CMP", 2048 * h + 16 * p0 + i, 2048 * h + 16 * p1, 16), ap("BK3", 0, 8))
+            for i0 in range(0, 16, RUN):
+                mms([(ap(C, c0 + i, c0 + 128, 16, p0, p1), ap("CMP", 2048 * h + 16 * p0 + i, 2048 * h + 16 * p1, 16), ap("BK3", 0, 8), True, True) for i in range(i0, i0 + RUN)])
         if cfg(t, s, h)[2]:
             act(ap("PEN", o, o + 128), ap(C, c0, c0 + 128), F.Relu, bias=kc, scale=-1.0, **arrived("ks", t))
         else:
             ts(ap("PEN", o, o + 128), ap(C, c0, c0 + 128), kc, A.is_lt, **arrived("ks", t))
-        for k in range(s + 1):
-            mm(ap(K, 128 * k, 128 * k + 128), ap("RBIG", 128, 256), ap("PEN", o, o + 128), False, k == s)
+        mms([(ap(K, 128 * k, 128 * k + 128), ap("RBIG", 128, 256), ap("PEN", o, o + 128), False, k == s) for k in range(s + 1)])
         scan(ap("SCN", 384 * h, 384 * h + n), ap("RS", 0, n), ap(K, 0, n), A.add, A.min)
         if s == 0 and h == 0 and t % 2:
             tt(ap("ASK", 0, 8), ap("SCN", 15, 128, 16), ap("THA", 8, 16), A.is_ge)
@@ -490,63 +524,59 @@ def rank_program(g, core, T, topo):
         ts(lo, mi, 4095, A.bitwise_and)
         c = 120 * h + 4 - s
         cp(ap("D1", c, 120 * h + 40 * (s + 1), 5), lo)
-        ts(ap("D0", c, 120 * h + 40 * (s + 1), 5), lo, 0.0, A.is_equal)
         if s:
-            v = 80 * h + 40 * (2 - s)
+            ts(ap("D0", c, 120 * h + 40 * (s + 1), 5), lo, 0.0, A.is_equal)
+        else:
+            act(ap("D0", c, 120 * h + 40, 5), ap("D1", c, 120 * h + 40, 5), F.Relu, bias=1.0, scale=-1.0)
+        if s:
+            v = 80 * (1 - h) + 40 * (2 - s)
             scan(ap("VS", v, v + 40), ap("D0", 120 * h + 40 * s, 120 * h + 40 * s + 40), ap("D1", 120 * h + 40 * s, 120 * h + 40 * s + 40), A.mult, A.max)
             tt(ap("AX", o, o + 128), ind(ap("VS", v, v + 40), ap("O5", 0, 8)), ap("MK", 0, 128), A.mult)
             mm(ap(C, 192, 200), ap("AX", o, o + 128), ap("BK3", 0, 8))
             cp(vlist(t, s - 1, h), ap(C, 192, 200))
-            if s == 1 and h == 0:
-                tt(ap("PRE", 8, 16), ap(C, 192, 200), ap("DUM", 8, 16), A.subtract)
+            if s == 1 and t + 1 < NV:
+                kind, lv, lg = "la" if h == 0 else "lb", ap("LV", 32 * t + 16 * h, 32 * t + 16 * h + 16), 48 * (t + 1) + w + 8
+                sends[kind, t + 1] = send([(1, ap("LG", lg, lg + 16), lv, "%s%d" % (kind, t + 1), 0)], [lv])
             tt(ap("THR", w, w + W - 8), ap("MI", w, w + W - 8), ap("LO", w, w + W - 8), A.subtract)
             if s == 2:
-                cp(ap("D1", 120 * h + 40, 120 * h + 80, 5), ap("VS", v + 4, v + 40, 5))
+                act(ap("D1", 120 * h + 40, 120 * h + 80, 5), ap("VS", v + 4, v + 40, 5))
 
     def final_guards(t, h):
-        ms(ap("D1", 120 * h + 40, 120 * h + 120, 5), 0.0)
+        act(ap("D1", 120 * h + 40, 120 * h + 120, 5), ap("D0", 120 * h + 40, 120 * h + 120, 5))
         scan(ap("GF", 240 * t + 120 * h, 240 * t + 120 * h + 120), ap("D0", 120 * h, 120 * h + 120), ap("D1", 120 * h, 120 * h + 120), A.mult, A.max)
         if t + 1 < NV:
             c, kind = 240 * t + 120 * h, "ga" if h == 0 else "gb"
             gf = ap("GF", c, c + 120)
             sends[kind, t + 1] = send([(1, ap("GR", c + 240, c + 360), gf, "%s%d" % (kind, t + 1), 0)], [gf])
 
-    v2, v1, v0 = ap("D1", 80, 120, 5), ap("D1", 40, 80, 5), ap("VS", 44, 80, 5)
-    av = ap("HS", 4, 40, 5)
+    v2, v1, v0 = ap("D1", 80, 120, 5), ap("D1", 40, 80, 5), ap("VS", 124, 160, 5)
+    av = ap("VS", 164, 200, 5)
     ea, eb, fr = ap("E2", 0, 128), ap("EB", 0, 128), ap("FR", 0, 128)
 
     def early3(t):
-        ts(ap("DH", 1, 40, 5), v2, -1.0, A.mult)
+        act(ap("DH", 1, 40, 5), v2, scale=-1.0)
         tt(ap("DH", 2, 40, 5), v2, v1, A.subtract)
-        tt(ap("DH", 3, 40, 5), v1, v0, A.subtract)
-        cp(ap("DH", 4, 40, 5), v0)
+        act(ap("DH", 3, 40, 5), v1)
         act(eb, ind(ap("D", 0, 2048), vlist(t, 0, 0)))
         if t % 2 == 0:
-            lb = ind(ap("RW", 0, 2048), vlist(t, 0, 0))
-            act(ap("RB", 0, 128), lb, scale=ap("NMK", 8 + t, 9 + t))
-            act(ap("RB", 128, 256), lb, scale=ap("NMK", t, t + 1))
-            act(ap("XS", 0, 128), xs(t, 0), scale=ap("MK", 8 + t, 9 + t), **arrived("in", t))
-            act(ap("XS", 128, 256), xs(t, 0), scale=ap("MK", t, t + 1), **arrived("in", t))
-            tt(ap("HB", 0, 128), ap("RB", 128, 256), ap("XS", 128, 256), A.add)
-            act(ap("HB", 128, 256), ap("RW", 1792 + 64 * t, 1920 + 64 * t))
+            act(ap("RB", 0, 128), ind(ap("RW", 0, 2048), vlist(t, 0, 0)))
+            for j in range(2):
+                d = 256 * t + 256 * j
+                mms([(ap("M", 128 + 128 * j, 256 + 128 * j), ap("DG", d, d + 128), ap("RB", 0, 128), True, False),
+                     (ap("M", 128 + 128 * j, 256 + 128 * j), ap("DG", d + 128, d + 256), xs(t, 0), False, True)], **arrived("in", t))
+            act(ap("HB", 0, 256), ap("M", 128, 384))
+            act(ap("HB", 256, 384), ap("RW", 1792 + 64 * t, 1920 + 64 * t))
 
     def source(t):
         k = 1 - t % 2
-        scan(ap("HS", 0, 40), ap("D0", 40 * k, 40 * k + 40), ap("DH", 0, 40), A.mult, A.add)
-        tt(ap("AL", 0, 128), ind(ap("HS", 0, 40), ap("O5", 0, 8)), ap("MK", 0, 128), A.mult)
-        mm(ap("M", 128, 256, 1, 0, 8), av, ap("IF", 0, 128))
-        mm(ap("M", 256, 384, 1, 0, 8), v0, ap("IF", 0, 128))
-        cp(ap("ABT", 0, 256, 1, 0, 8), ap("M", 128, 384, 1, 0, 8))
+        scan(ap("VS", 160, 200), ap("D0", 40 * k, 40 * k + 40), ap("DH", 0, 40), A.mult, A.add)
+        tt(ap("AL", 0, 128), ind(ap("VS", 160, 200), ap("O5", 0, 8)), ap("MK", 0, 128), A.mult)
         mm(ap("M", 80, 88), ap("AL", 0, 128), ap("BK3", 0, 8))
         cp(ap("LA", 0, 8), ap("M", 80, 88))
-        tt(ap("PRE", 0, 8), ap("M", 80, 88), ap("DUM", 0, 8), A.subtract)
         act(ea, ind(ap("D", 0, 2048), ap("LA", 0, 8)))
-        tt(ap("S8", 0, 8), av, v0, A.add)
-        tt(ap("DD", 0, 8), av, v0, A.subtract)
-        act(ap("HH", 0, 8), ap("DD", 0, 8), F.Abs)
-        ts(ap("NQ", 0, 8), ap("DD", 0, 8), 0.0, A.not_equal)
+        tt(ap("NQ", 0, 8), av, v0, A.not_equal)
         tt(ap("Q8", 0, 8), ap("NQ", 0, 8), av, A.min)
-        ts(fr, ea if k else eb, 0.0, A.is_equal)
+        act(fr, ea if k else eb, F.Relu, bias=1.0, scale=-1.0)
         mm(ap("M", 32, 40), fr, ap("BK3", 0, 8))
         tt(ap("ASK", 8 - 8 * k, 16 - 8 * k), ap("Q8", 0, 8), ap("M", 32, 40), A.min)
         if k:
@@ -554,55 +584,63 @@ def rank_program(g, core, T, topo):
             mm(ap("M", 384, 512), ap("TRZ", 0, 128), fr, False, True)
             tt(ap("E2", 128, 256), ea, ap("M", 384, 512), A.max)
         else:
-            ts(ap("THA", 0, 8), ap("ASK", 8, 16), -HUGE, A.mult, HUGE, A.add)
+            act(ap("THA", 0, 8), ap("ASK", 8, 16), bias=HUGE, scale=-HUGE)
             tt(ap("THA", 8, 16), ap("THA", 0, 8), ap("THR", 0, 8), A.add)
 
     def meet(t):
+        ba = ap("VS", 124, 200, 5)
+        ts(ap("FX", 0, 256, 16), ba, -1024.0, A.add)
+        act(ap("SQ", 0, 16), ba, F.Square, bias=-128.0, scale=0.125)
+        cp(ap("FX", 1, 256, 16), ap("SQ", 0, 16))
+        tt(ap("FX", 2, 256, 16), ap("SQ", 0, 16), ap("FX", 1, 256, 16), A.subtract)
+        for w in range(2):
+            tt(ap("FX", 256 + 144 * w, 384 + 128 * w, 32), ap("FX", 16 * w, 128, 32), ap("FX", 128 + 16 * w, 256, 32), A.add)
+        tt(ap("PP", 0, 8), ap("FX", 0, 128, 16), ap("FX", 128, 256, 16), A.mult)
+        y = MEET[t % 2] + "1"
+        for j in range(4):
+            mm(ap(y, 128 * j, 128 * j + 128), ap("FX", 128 * j, 128 * j + 128), ap("IB", 0, 128))
+        cp(ap("FT", 0, 512), ap(y, 0, 512))
         for b in range(4):
             y = MEET[t % 2] + "%d" % (b % 2)
-            mm(ap(y, 0, 512), ap("IB", 0, 128), ap("TRL", 0, 512), True, False)
+            mms([(ap(y, 256 * j, 256 * j + 256), ap("FT", 256 + 128 * j, 384 + 128 * j, 1, 32 * b, 32 * b + 32), ap("FT", 0, 256, 1, 32 * b, 32 * b + 32), True, True)
+                 for j in range(2)])
             for j in range(2):
                 gg = 2 * b + j
-                mm(ap(y, 256 * j, 256 * j + 256), ap("SELG", 128 * gg, 128 * gg + 128, 1, 0, 8), ap("ABT", 0, 256, 1, 0, 8), False, j == 1)
-            for j in range(2):
-                gg = 2 * b + j
-                act(ap("AB", 256 * gg, 256 * gg + 256), ap(y, 256 * j, 256 * j + 256), F.Abs, bias=ap("S8", gg, gg + 1), scale=-2.0)
-                ts(ap("EQ", 256 * gg, 256 * gg + 256), ap("AB", 256 * gg, 256 * gg + 256), ap("HH", gg, gg + 1), A.is_equal)
+                ts(ap("EQ", 256 * gg, 256 * gg + 256), ap(y, 256 * j, 256 * j + 256), ap("PP", gg, gg + 1), A.is_equal, ap("WL", 127, 128), A.mult)
 
     def acts(t):
         b = ACTS[t % 2]
-        for gg in range(8):
-            for x in range(2):
-                c = 256 * gg + 128 * x
-                mm(ap(b, 40 + gg, 41 + gg), ap("EQ", c, c + 128), ap("ASK", gg, gg + 1), x == 0, x == 1)
-        tt(ap("ACT", 0, 8), ap("ASK", 0, 8), ap(b, 40, 48), A.is_gt)
+        for g0 in range(0, 8, 2):
+            mms([(ap(b, 40 + gg, 41 + gg), ap("EQ", 256 * gg + 128 * x, 256 * gg + 128 * x + 128), ap("ASK", gg, gg + 1), x == 0, x == 1)
+                 for gg in (g0, g0 + 1) for x in range(2)])
+        act(ap("Q8", 0, 8), ap("ASK", 0, 8), scale=ap("WL", 128, 129))
+        tt(ap("ACT", 0, 8), ap("Q8", 0, 8), ap(b, 40, 48), A.is_gt)
         nl = 24 if t % 2 == 0 else 16
         tt(ap("AC", 0, 128), ind(ap("ACT", 0, 8), ap("OC", 0, 8)), ap("MK", 0, 128), A.mult)
         if t < NV - 1:
-            for gg in range(9):
-                mm(ap(b, 72, 73), ap("ONE", 0, 128), ap("ACT", gg, gg + 1), gg == 0, gg == 8)
-        mm(ap(b, 48, 48 + nl), ap("AC", 0, 128), ap("BK3", 0, nl))
-        tt(ap("LT", 0, nl), ap("PRE", 0, nl), ap(b, 48, 48 + nl), A.mult)
+            mms([(ap(b, 72, 73), ap("ONE", 0, 128), ap("ACT", gg, gg + 1), gg == 0, gg == 8) for gg in range(9)])
+        mms([(ap(b, 48, 48 + nl), ap("IB", 0, 128), ap("LC", 0, nl), True, False), (ap(b, 48, 56), ap("AL", 0, 128), ap("BK3", 0, 8), False, False),
+             (ap(b, 56, 64), ap("AX", 0, 128), ap("BK3", 0, 8), False, False), (ap(b, 48, 48 + nl), ap("AC", 0, 128), ap("SD", 0, nl), False, True)])
+        tt(ap("LU", 0, nl), ap("DUM", 0, nl), ap(b, 48, 48 + nl), A.min)
         if t < NV - 1:
             ts(ap("KT", 0, 1), ap(b, 72, 73), RN2, A.add, RN2, A.subtract)
             ts(ap("KT", 8, 9), ap("KT", 0, 1), ap(b, 72, 73), A.subtract, 4.5, A.subtract)
             ks = ap("KS", 8 * t, 8 * t + 8)
-            ts(ks, ap("KA", 0, 8), ap("KT", 8, 9), A.mult, 16.0, A.add)
+            act(ks, ap("KA", 0, 8), bias=16.0, scale=ap("KT", 8, 9))
             sends["ks", t + 1] = send([(1, ap("KR", 8 * t + 8, 8 * t + 16), ks, "ks%d" % (t + 1), 0)], [ks])
-        tt(ap("LU", 0, nl), ap("LT", 0, nl), ap("DUM", 0, nl), A.add)
         cp(ap("LS", 0, nl), ap("LU", 0, nl))
 
     def split_rows(t):
         n = spans(t, 0, 0)[0][1]
         mm(ap("M", 128, 384), ap("ONE", 0, 128, 1, 0, 64), ap("CK", 512, 768, 1, 0, 64), True, False)
-        mm(ap("M", 128, 384, 1, 0, n), ap("XZ", 256 * t, 256 * t + n), ap("SX", 128 * t, 128 * t + 256), False, False, **arrived("in", t))
+        mm(ap("M", 128, 384, 1, 0, n), ap("XZ", 512 * t, 512 * t + n), ap("SX", 128 * t, 128 * t + 256), False, False, **arrived("in", t))
         by_entry(t, 0, 0, "M", 128, 384, ap("SCT", 16 * t + 8, 16 * t + 24))
         mm(ap("M", 128, 144), ap("ONE", 0, 128, 1, 0, 64), ap("CK", 512, 528, 1, 0, 64), False, True)
         act(ap("GE", 0, 256), ap("M", 128, 384), F.Sign, bias=0.5)
         mm(ap("M", 128, 256), ap("GE", 0, 128), ap("IB", 0, 128))
         mm(ap("M", 256, 384), ap("GE", 0, 128), ap("IB", 0, 128), True, False)
         mm(ap("M", 256, 384), ap("GE", 128, 256), ap("IB", 0, 128), False, True)
-        ts(ap("ST", 0, 128), ap("M", 256, 384), -2.0, A.is_equal)
+        act(ap("ST", 0, 128), ap("M", 256, 384), F.Relu, bias=-1.0, scale=-1.0)
         tt(ap("YS", 256, 384), eb, ap("M", 128, 256), A.mult)
         mm(ap("M", 384, 512), ap("ONE", 0, 128), ap("NCB", 256, 384), True, False)
         mm(ap("M", 384, 512), ap("TRC", 0, 128), ap("ST", 0, 128), False, True)
@@ -614,20 +652,19 @@ def rank_program(g, core, T, topo):
     def place_rows(t):
         for b in range(4):
             y = "Y%d" % (b % 2)
-            for j in range(4):
-                c = 512 * b + 128 * j
-                mm(ap(y, 128 * j, 128 * j + 128), ap("PBC", c, c + 128), fr)
-            for c0, c1, u in ((0, 128, 0), (128, 256, 0), (256, 512, 0)) if b == 0 else ((0, 512, 0),):
-                tt(ap("MM", 512 * b + c0, 512 * b + c1), ap("U", u, u + c1 - c0), ap(y, c0, c1), A.max)
+            mms([(ap(y, 128 * j, 128 * j + 128), ap("PBC", 512 * b + 128 * j, 512 * b + 128 * j + 128), fr, True, True) for j in range(b == 0, 4)])
+            for c0, c1 in ((128, 256), (256, 512)) if b == 0 else ((0, 512),):
+                tt(ap("MM", 512 * b + c0, 512 * b + c1), ap("U", 0, c1 - c0), ap(y, c0, c1), A.max)
+            if b == 3:
+                tt(ap("W6", 0, 128), ap("U", 0, 128), ap(y, 384, 512), A.is_ge)
             for j in range(4):
                 c, i = 512 * b + 128 * j, 4 * b + j + 129
-                mm(ap("M", i, i + 113, 16), ap("MM", c, c + 128), ap("BKF", 0, 8))
+                mm(ap("M", i, i + 113, 16), ap("MM" if c else "U", c, c + 128), ap("BKF", 0, 8))
         act(ap("SS", 1, 129), ap("M", 129, 257))
         tt(ap("GD", 0, 128), ap("SS", 0, 128), ap("M", 129, 257), A.subtract)
         ts(ap("GT", 0, 128), ap("GD", 0, 128), RND, A.add, RND, A.subtract)
         mm(ap("M", 384, 512), ap("GD", 0, 128), ap("IF", 0, 128), True, False)
         mm(ap("M", 384, 512), ap("GT", 0, 128), ap("NIF", 0, 128), False, True)
-        tt(ap("W6", 0, 128), ap("MM", 1920, 2048), ap("U", 0, 128), A.is_le)
         act(ap("W1", 0, 128), ap("M", 384, 512), scale=ap("NMK", 0, 1))
 
     def move_down(t):
@@ -648,9 +685,9 @@ def rank_program(g, core, T, topo):
         tt(ind(ap("D", 0, 2304), ap("LS", 8, 16)), ap("W2", 0, 128), ap("W6", 0, 128), A.mult)
         act(ap("D", n0, n0 + 128), ind(ap("YS", 256, 512), ln), F.Relu)
         for c in (0, 4096, 8192):
-            tt(ind(ap("RW", c, c + 2304), ap("LS", 8, 16)), ap("RB", 0, 128), ap("XS", 0, 128), A.add)
+            cp(ind(ap("RW", c, c + 2304), ap("LS", 8, 16)), ap("HB", 0, 128))
             if c < 8192:
-                act(ap("RW", c + n0, c + n0 + 128), ind(ap("HB", 0, 256), ln))
+                act(ap("RW", c + n0, c + n0 + 128), ind(ap("HB", 128, 384), ln))
                 r = 128 * (c // 4096)
                 act(ap("RW", c + 2176, c + 2304), ap("RSV", r, r + 128))
         tt(ind(ap("D", 0, 2304), ap("LS", 0, 8)), ap("W1", 0, 128), ap("E2", 128, 256), A.add)
@@ -659,7 +696,7 @@ def rank_program(g, core, T, topo):
     spread(0)
     for t in range(NV):
         if t % 2:
-            ms(ap("D0", 4, 40, 5), 1.0)
+            act(ap("D0", 4, 40, 5), ap("ONE", 0, 8))
         if t + 1 < NV:
             spread(t + 1)
         steps = [(start_nodes, 0), (start_nodes, 1), (guards, 0), (gather, 2, 0), (compare, 2, 0), (gather, 2, 1), (compare, 2, 1), (tail, 2, 0), (guards, 1),
@@ -682,13 +719,12 @@ def rank_program(g, core, T, topo):
             store("y", T.yr[:, 16:2048], ap("RW", 4112, 6144), 4000.0)
     store("y", T.yn[:, 0:1024], ap("D", 0, 1024), 4000.0)
     store("s", T.yn[:, 1024:2048], ap("D", 1024, 2048), 4000.0)
-    for k in range(3):
-        for h in range(2):
-            c, b = 256 * k + 128 * h, 720 + 120 * h + 40 * k
-            mm(ap("Y%d" % (c // 512), c % 512, c % 512 + 128, 1, 0, 8), ap("GF", b + 4, b + 40, 5), ap("IF", 0, 128))
-    act(ap("YG", 0, 512, 1, 0, 8), ap("Y0", 0, 512, 1, 0, 8))
-    act(ap("YG", 512, 768, 1, 0, 8), ap("Y1", 0, 256, 1, 0, 8))
-    store("y", T.yg[:, :], ap("YG", 0, 768, 1, 0, 8), 2000.0)
+    for h in range(2):
+        for k in range(3):
+            (cp if k else act)(ap("T1", 24 * h + k, 24 * h + 24, 3), ap("GF", 724 + 120 * h + 40 * k, 760 + 120 * h + 40 * k, 5))
+        mm(ap(KB[h], 0, 128, 1, 0, 24), ap("T1", 24 * h, 24 * h + 24), ap("IF", 0, 128))
+        act(ap("YG", 128 * h, 128 * h + 128, 1, 0, 24), ap(KB[h], 0, 128, 1, 0, 24))
+    store("y", T.yg[:, :], ap("YG", 0, 256, 1, 0, 24), 2000.0)
 
     n = len(ops)
     succ = [[] for _ in range(n)]
@@ -781,8 +817,143 @@ def rank_program(g, core, T, topo):
                     break
                 back = place(sorted(range(n), key=lambda k: (-at[k] - cost[k], -k)), bwd, tails)
                 seq = sorted(range(n), key=lambda k: (-back[k] - cost[k], k))
-        PLAN["order"] = sorted(range(n), key=lambda k: (best[1][k], k))
-        PLAN["at"], PLAN["fin"], PLAN["each"] = best[1], best[0], best[3]
+        seq = sorted(range(n), key=lambda k: (best[1][k], k))
+        sets = [(cost, fwd)] + [others[i] for i in KEEP]
+        sets = [(cs, pre, [[(j, dict(pre[j])[k]) for j in succ[k]] for k in range(n)]) for cs, pre in sets]
+        qn = ["vspgy".index(e) for e in engs]
+        above = [set(edge[k]) for k in range(n)]
+
+        def ways(seq, a, b, old, cs, pre, post):
+            done, rest = list(old[1]), list(old[2])
+            free, calm = [0.0] * 5, b - a + CALM
+            for k in seq[max(a - CALM, 0):a]:
+                free[qn[k]] = done[k]
+            for k in seq[a:]:
+                t0 = free[qn[k]]
+                for j, l in pre[k]:
+                    if done[j] + l > t0:
+                        t0 = done[j] + l
+                t0 += cs[k]
+                free[qn[k]] = t0
+                if t0 != done[k]:
+                    done[k] = t0
+                    if calm < CALM:
+                        calm = CALM
+                calm -= 1
+                if calm < 0:
+                    break
+            free, calm = [0.0] * 5, b - a + CALM
+            for k in seq[b + CALM:b:-1]:
+                free[qn[k]] = rest[k]
+            for k in seq[b::-1]:
+                t0 = free[qn[k]]
+                if tails[k] > t0:
+                    t0 = tails[k]
+                for j, l in post[k]:
+                    if rest[j] + l > t0:
+                        t0 = rest[j] + l
+                t0 += cs[k]
+                free[qn[k]] = t0
+                if t0 != rest[k]:
+                    rest[k] = t0
+                    if calm < CALM:
+                        calm = CALM
+                calm -= 1
+                if calm < 0:
+                    break
+            return max(rest), done, rest
+
+        st = [ways(seq, 0, n - 1, (0, zero, zero), *m) for m in sets]
+        cur = sum(x[0] for x in st)
+        top = (cur, seq)
+        for rnd in range(MOVES):
+            heat = max(HEAT * (1.0 - rnd / MOVES), 1.0) * len(sets)
+            dice = rng.random(5 * TRIES + 1).tolist()
+            mi = int(dice.pop() * len(sets))
+            if rnd % FRESH == 0:
+                if rnd % (8 * FRESH) == 0:
+                    seq = sorted(seq, key=lambda k: st[0][1][k] - cost[k])
+                    st = [ways(seq, 0, n - 1, x, *m) for x, m in zip(st, sets)]
+                    cur = sum(x[0] for x in st)
+                    if cur < top[0]:
+                        top = (cur, seq)
+                (end, done, rest), cs = st[mi], sets[mi][0]
+                pos, last, held = [0] * n, [-1] * 5, []
+                for i, k in enumerate(seq):
+                    pos[k] = i
+                    j = last[qn[k]]
+                    if done[k] + rest[k] - cs[k] > end - 1.0 and j >= 0 and done[j] + cs[k] > done[k] - 0.5 and j not in above[k]:
+                        held.append((j, k))
+                    last[qn[k]] = k
+            while dice and held:
+                u, v = held[int(dice.pop() * len(held))]
+                e, m, back_, lim = qn[v], int(dice.pop() * REACH), dice.pop() < 0.5, cur - heat * math.log(dice.pop() + 1e-12)
+                a, b = pos[u], pos[v]
+                dice.pop()
+                if a > b:
+                    continue
+                if back_:
+                    while m and a > 0:
+                        a -= 1
+                        m -= qn[seq[a]] == e
+                    w, go = seq[a:b + 1], {v}
+                    for k in reversed(w):
+                        if k in go:
+                            go.update(above[k])
+                    if u in go:
+                        continue
+                    w = [k for k in w if k in go] + [k for k in w if k not in go]
+                else:
+                    while m and b < n - 1:
+                        b += 1
+                        m -= qn[seq[b]] == e
+                    w, go = seq[a:b + 1], {u}
+                    for k in w:
+                        if not go.isdisjoint(above[k]):
+                            go.add(k)
+                    if v in go:
+                        continue
+                    w = [k for k in w if k not in go] + [k for k in w if k in go]
+                bef, aft = [-1] * 5, [-1] * 5
+                for k in seq[max(a - 100, 0):a]:
+                    bef[qn[k]] = k
+                for k in reversed(seq[b + 1:b + 100]):
+                    aft[qn[k]] = k
+                tot = 0.0
+                for (c1, dn, rs), (c_, pre, post) in zip(st, sets):
+                    free = [dn[k] if k >= 0 else 0.0 for k in bef]
+                    d2, far, old = {}, 0.0, 0.0
+                    for k in w:
+                        x = free[qn[k]]
+                        for j, l in pre[k]:
+                            y = (d2[j] if j in d2 else dn[j]) + l
+                            if y > x:
+                                x = y
+                        x += c_[k]
+                        d2[k] = free[qn[k]] = x
+                        y = tails[k]
+                        for j, l in post[k]:
+                            if pos[j] > b and rs[j] + l > y:
+                                y = rs[j] + l
+                        if x + y > far:
+                            far = x + y
+                        if dn[k] + rs[k] - c_[k] > old:
+                            old = dn[k] + rs[k] - c_[k]
+                    for x, k in zip(free, aft):
+                        if k >= 0 and x + rs[k] > far:
+                            far = x + rs[k]
+                    tot += far if far > c1 or old > c1 - 1.0 else c1
+                if tot <= lim:
+                    new = seq[:a] + w + seq[b + 1:]
+                    s2 = [ways(new, a, b, x, *m_) for x, m_ in zip(st, sets)]
+                    if sum(x[0] for x in s2) <= lim:
+                        seq, st, cur = new, s2, sum(x[0] for x in s2)
+                        for i, k in enumerate(w):
+                            pos[k] = a + i
+                        break
+        end, done, rest = ways(top[1], 0, n - 1, (0, zero, zero), *sets[0])
+        PLAN["order"], PLAN["at"], PLAN["fin"] = top[1], [done[k] - cost[k] for k in range(n)], end
+        PLAN["each"] = [replay(top[1], c_, p_) for c_, p_ in others]
     order, fin = PLAN["order"], PLAN["fin"]
     for k in range(n):
         ops[k]["at"] = PLAN["at"][k]

import math
import numpy as np
from concourse.bass import DstId, RemoteDMATransfer
from concourse.mybir import AluOpType as A, ActivationFunctionType as F

N, NV = 4, 4
BIG = float(2 ** 27)
NOG = float(2 ** 26)
HUGE = float(2 ** 40)
MEET = ("X", "Y")
ACTS = ("X0", "M")
ORDER = (0, 0)
JOIN = 1
PBCS = 3
OWN = 16
FAR = 16384.0
CC = 32768.0
RND, RN2 = 1.5 * 2 ** 38, 1.5 * 2 ** 24
f32, bf, i32, u16, f16 = "float32", "bfloat16", "int32", "uint16", "float16"

SB = {
    "RW": (10496, bf), "RSV": (256, bf), "D": (2304, f32), "NDI": (1792, i32),
    "XZ": (2048, bf), "VSO": (64, i32), "VSR": (64, i32), "L2": (64, u16),
    "GF": (960, f32), "GR": (960, f32), "KS": (32, f32), "KR": (32, f32), "K0": (8, f32),
    "KA": (8, f32), "KT": (16, f32), "NIB": (128, bf), "R0": (16, bf), "HB": (384, bf), "IB": (128, bf), "IF": (128, f32), "ONE": (128, bf), "RBIG": (512, bf),
    "BK3": (24, bf), "BKF": (8, f32), "SC": (24, bf), "SCT": (64, bf), "SX": (512, bf),
    "TRC": (128, bf), "PBC": (2048, bf), "OP": (128, u16), "XQ": (128, bf), "WL": (136, f32), "GZ": (48, bf), "FX": (512, f16), "FT": (512, f16), "SQ": (16, f32), "PP": (8, f32),
    "CK": (768, bf), "RS": (384, f32), "MKI": (128, i32), "MKJ": (128, i32), "MK": (128, f32), "NMK": (16, f32),
    "PM": (4, f32), "DU0": (24, f32), "DUM": (24, f32), "NCB": (512, bf), "NIF": (128, f32), "TRZ": (128, bf),
    "XR": (8192, bf), "RF": (2048, f16), "GP": (48, f32), "THA": (16, f32), "SS": (136, f32), "GT": (128, f32),
    "OCI": (128, i32), "OC": (128, u16), "O5I": (48, i32), "O5": (48, u16),
    "EU": (256, u16), "FA": (256, bf), "FB": (256, bf), "FW": (768, f16),
    "R": (4096, bf), "CMP": (4096, bf), "PEN": (256, bf), "SCN": (768, f32),
    "MI": (48, i32), "LO": (48, i32), "THR": (48, i32), "D0": (240, f32), "D1": (240, f32),
    "VS": (200, f32), "AX": (256, f16), "LV": (128, u16), "AV": (256, f16), "AL": (128, f16),
    "AG": (256, f32), "LG": (192, u16), "RG": (768, bf), "CG": (768, bf), "T1": (48, f32), "T2": (48, f32),
    "DH": (40, f32), "AA": (128, f32), "LA": (8, u16), "LC": (24, f16), "SD": (24, bf), "DG": (1024, bf),
    "EB": (128, f32), "FR": (128, bf),
    "NQ": (8, f32), "Q8": (8, f32), "ASK": (16, bf), "ACT": (16, bf),
    "EQ": (2048, bf), "AC": (128, bf), "LU": (24, f32), "LS": (24, u16),
    "YS": (512, f32), "GE": (256, bf), "ST": (128, bf),
    "W1": (256, f32), "W2": (128, f32), "W6": (128, f32), "E2": (256, f32),
    "U": (512, f32), "MM": (2048, f32), "GD": (128, f32),
    "RB": (128, bf), "YG": (256, f32),
}
PS = ["X0", "X1", "Y0", "Y1", "C", "K", "M", "M2"]
SCRATCH, AT = {}, {}
for k_, (n_, d_) in SB.items():
    pool_ = k_ if n_ > 256 else "pool" + d_
    used_ = SCRATCH[pool_][1][1] if pool_ in SCRATCH else 0
    AT[k_] = (pool_, used_)
    SCRATCH[pool_] = ("sbuf", [128, used_ + (n_ + 31) // 32 * 32], d_)
SCRATCH.update({k: ("psum", [128, 512], f32) for k in PS})
DMAS = ["ld%d" % i for i in range(8)] + ["st%d" % i for i in range(5)]
SEMAPHORES = ["qv", "qs", "qp", "qg", "sent"] + DMAS + ["%s%d" % (a, t) for a in ("in", "ga", "gb", "la", "lb", "ks") for t in (1, 2, 3)]
CHUNKS = (((0, 512), (512, 1024), (1024, 1536), (1536, 2048)), ((0, 1024), (1024, 1536), (1536, 2048)), ((0, 1024), (1024, 2048)),
          ((0, 512), (512, 1024), (1024, 2048)))
BOTH = [("DDAA", 0, 1, 0), ("DDDA", 0, 1, 0)]
CFG = BOTH * 2 + [("DCCE", 0, 0, 0), ("DDDD", 0, 0, 0)] + BOTH * 9
LEADS = [1000.0 * i for i in range(-2, 14)]
SHARE = {1: (0, 4), 2: (4, 6), 3: (6, 8)}
OTHERS = [(1.1, 2.2, 0.87, 200.0, 1.6), (1.3, 3.0, 0.9, 120.0, 2.0), (2.0, 5.0, 1.0, 150.0, 1.0)]
WINDOW = 8000.0
RUN = 8
ROUNDS, PASSES, SHAKE = 700, 2, 200.0
CALM, FRESH = 120, 3
SLOWG = 1.2
MOVES, TRIES, REACH, HEAT, KEEP = 46000, 40, 6, 100.0, (0, 2)
PLAN = {}

GATH, SCAT = 1.35, 3.4
PE0, PE1 = 5.0, 0.5
LAT = 150.0


def ap(name, c0, c1, st=1, p0=0, p1=128):
    return (name, c0, c1, st, p0, p1)


def ind(win, off):
    return ("ind", win, off)


def width(a):
    if a[0] == "ind":
        return 16 * (a[2][2] - a[2][1])
    return (a[2] - a[1] + a[3] - 1) // a[3]


def two(a):
    return a[0] != "ind" and a[0] in SB and SB[a[0]][1] in (bf, u16, f16)


def rank_program(g, core, T, topo):
    rank = T.rank_of(core)
    if rank is None:
        return
    ops = []
    stage = [0, 0]
    last_w = {}
    last_r = {}
    last_p = {}

    def real(a):
        if not isinstance(a, tuple):
            return a
        if a[0] == "ind":
            return real(a[1]).indirect(real(a[2]))
        pool, c = AT.get(a[0], (a[0], 0))
        t = T[pool]
        if a[3] == 1:
            return t[a[4]:a[5], c + a[1]:c + a[2]]
        return t[a[4]:a[5], c + a[1]:c + a[2]:a[3]]

    def meets(a, e):
        if not (e[0] < a[2] and a[1] < e[1]):
            return False
        return a[3] != e[2] or a[3] == 1 or (a[1] - e[0]) % a[3] == 0

    def op(eng, fn, outs, ins, cost, waits=(), after=(), sem=None, lat=0.0):
        k = len(ops)
        rd, wr = [], []
        for a in ins:
            if isinstance(a, tuple):
                rd += [a[1], a[2]] if a[0] == "ind" else [a]
        for a in outs:
            if a[0] == "ind":
                wr.append(a[1])
                rd.append(a[2])
            else:
                wr.append(a)
        dep = {}
        for a in rd + wr:
            if a[0] in PS:
                j = last_p.get(a[0])
                if j is not None and j != k:
                    dep[j] = dep.get(j, False) or ops[j]["eng"] != eng
                last_p[a[0]] = k
        for a in rd:
            if a[0] not in PS:
                for e in last_w.get(a[0], []):
                    if meets(a, e):
                        dep[e[3]] = True
        for a in wr:
            if a[0] not in PS:
                for e in last_w.get(a[0], []) + last_r.get(a[0], []):
                    if meets(a, e):
                        dep[e[3]] = True
        for a in wr:
            if a[0] not in PS:
                if a[4] == 0 and a[5] == 128:
                    for d in (last_w, last_r):
                        d[a[0]] = [e for e in d.get(a[0], []) if not (a[1] <= e[0] and e[1] <= a[2] and (a[3] == 1 or a[3] == e[2] and (a[1] - e[0]) % a[3] == 0))]
                last_w.setdefault(a[0], []).append((a[1], a[2], a[3], k))
        for a in rd:
            if a[0] not in PS:
                last_r.setdefault(a[0], []).append((a[1], a[2], a[3], k))
        soft = dict(after)
        ops.append({"eng": eng, "fn": fn, "dep": dep, "cost": cost, "waits": list(waits), "soft": soft, "sem": sem, "lat": lat, "out": wr[:1],
                    "half": stage[1], "stage": stage[0],
                    "ns": width(outs[0]) if outs and outs[0][0] == "ind" else 0,
                    "ng": width(outs[0]) if outs and ins and isinstance(ins[0], tuple) and ins[0][0] == "ind" else 0})
        return k

    def vcost(out, ins, rate):
        n = width(out)
        if out[0] == "ind":
            rate = SCAT
        elif ins[0][0] == "ind":
            rate = GATH
        return 60.0 + n * rate

    def tt(out, a, b, alu, **kw):
        rate = 1.0 if (a[0] in PS or b[0] in PS) else 2.0
        return op("v", lambda: g.vector.tensor_tensor(real(out), real(a), real(b), alu), [out], [a, b], vcost(out, [a], rate), **kw)

    def ts(out, a, s1, o1, s2=None, o2=None, **kw):
        rate = 0.5 if two(out) and two(a) else 1.0
        if o2 is None:
            fn = lambda: g.vector.tensor_scalar(real(out), real(a), real(s1), None, o1)
        else:
            fn = lambda: g.vector.tensor_scalar(real(out), real(a), real(s1), real(s2), o1, o2)
        return op("v", fn, [out], [a, s1, s2], vcost(out, [a], rate), **kw)

    def cp(out, a, **kw):
        rate = 0.5 if two(out) and two(a) else 1.0
        return op("v", lambda: g.vector.tensor_copy(real(out), real(a)), [out], [a], vcost(out, [a], rate), **kw)

    def ms(out, c):
        return op("v", lambda: g.vector.memset(real(out), c), [out], [], 60.0 + width(out) * (0.5 if two(out) else 1.0))

    def scan(out, d0, d1, o0, o1, first=0.0):
        return op("v", lambda: g.vector.tensor_tensor_scan(real(out), real(d0), real(d1), first, o0, o1), [out], [d0, d1], 60.0 + width(out))

    def act(out, a, fn=F.Identity, bias=None, scale=None, **kw):
        ar = {}
        def call():
            if bias is not None:
                ar["bias"] = real(bias)
            if scale is not None:
                ar["scale"] = real(scale)
            return g.scalar.activation(real(out), real(a), fn, **ar)
        return op("s", call, [out], [a, bias, scale], 70.0 + width(out) * (GATH if a[0] == "ind" else 1.0), **kw)

    def mm(out, l, r, start=True, stop=True, **kw):
        c = max(min(64, width(l)), width(r)) * (4 if SB[l[0]][1] == f32 else 1)
        return op("p", lambda: g.tensor.matmul(real(out), real(l), real(r), start, stop), [out], [l, r], PE0 + PE1 * c, **kw)

    def mms(calls, **kw):
        c = sum(PE0 + PE1 * max(min(64, width(l)), width(r)) * (4 if SB[l[0]][1] == f32 else 1) for o, l, r, a, b in calls)
        def call():
            return [g.tensor.matmul(real(o), real(l), real(r), a, b) for o, l, r, a, b in calls][-1]
        return op("p", call, [calls[0][0]], sorted(set(x for o, l, r, a, b in calls for x in (l, r))), c, **kw)

    def iota(out, pat, base, cm):
        if SB[out[0]][1] == i32:
            fn = lambda: g.iota(real(out), pat, base, cm)
        else:
            fn = lambda: g.iota(real(out), pat, base, cm, allow_small_or_imprecise_dtypes=True)
        return op("g", fn, [out], [], SLOWG * (150.0 + 2 * width(out)))

    def sel(out, a, pat, cmp, base, cm, fill=0.0, **kw):
        return op("g", lambda: g.affine_select(real(out), real(a), pat, cmp, fill, base, cm), [out], [a], SLOWG * (200.0 + 2 * width(out)), **kw)

    nd_ = [0, 0]
    outs_ = []

    def load(q, out, src, ns, prev=None):
        s = "ld%d" % nd_[0]
        nd_[0] += 1
        e = g.sync if q == "y" else g.scalar
        return op(q, lambda: e.dma_start(real(out), src), [out], [], 60.0, sem=s, lat=ns, after={} if prev is None else {prev: 0.0})

    def store(q, dst, a, ns):
        s = "st%d" % nd_[1]
        nd_[1] += 1
        outs_.append(s)
        e = g.sync if q == "y" else g.scalar
        return op(q, lambda: e.dma_start(dst, real(a)), [], [a], 400.0 if q == "y" else 60.0, sem=s, lat=ns)

    sent = [0]

    def emask(dst, a, b):
        m = 0
        for e in topo.engines(core, dst)[a:b]:
            m |= 1 << e
        return m

    def send(pairs, ins):
        trs = []
        for dt_, o, s, sem, e0 in pairs:
            dst = T.cores[(rank + dt_) % N]
            rid, pid, _ = topo.addr(dst)
            trs.append((dst, rid, pid, o, s, sem, e0))
        sent[0] += 8
        def call():
            if len(trs) == 1:
                dst, rid, pid, o, s, sem, e0 = trs[0]
                g.remote_dma(real(o), real(s), T.sem[sem], T.sem["sent"], pid, rid, emask(dst, 0, 8))
            else:
                g.remote_dma_fused([RemoteDMATransfer(dst_ids=[DstId(rid=rid, pnc=pid)], dma_engine_mask=emask(dst, *e0),
                                                      remote_sem=T.sem[sem], src=real(s), dst=real(o))
                                    for dst, rid, pid, o, s, sem, e0 in trs], local_sem=T.sem["sent"])
            return None
        return op("g", call, [], ins, 1000.0 if sent[0] > 16 else 2500.0)

    l0 = load("y", ap("RW", 0, 2048), T.rg[:, 0:2048], 3500.0)
    load("s", ap("VSO", 0, 64), T.vs[:, :], 2000.0)
    load("s", ap("XZ", 0, 256), T.z[:, :], 2200.0)
    l1 = load("y", ap("NDI", 0, 896), T.nd[:, 0:896], 4800.0, l0)
    l2 = load("y", ap("NDI", 896, 1792), T.nd[:, 896:1792], 6000.0, l1)
    load("y", ap("RW", 2048, 4096), T.rg[:, 2048:4096], 7500.0, l2)

    ms(ap("ONE", 0, 128), 1.0)
    iota(ap("OCI", 0, 128), [[1, 128]], 0, 0)
    cp(ap("OC", 0, 128), ap("OCI", 0, 128))
    sel(ap("IB", 0, 128), ap("ONE", 0, 128), [[-1, 128]], A.is_equal, 0, 1)
    act(ap("RW", 6144, 8192), ind(ap("IB", 0, 128), ap("OC", 0, 128)))
    act(ap("IF", 0, 128), ap("IB", 0, 128))
    for c, w_ in ((128, BIG), (256, -BIG), (384, 0.0)):
        act(ap("RBIG", c, c + 128), ap("IB", 0, 128), scale=w_)
    sel(ap("BK3", 0, 24), ap("ONE", 0, 24), [[0, 3], [-16, 8]], A.is_ge, 0, 1)
    sel(ap("BK3", 0, 24), ap("BK3", 0, 24), [[0, 3], [16, 8]], A.is_ge, 15, -1)
    cp(ap("BKF", 0, 8), ap("BK3", 0, 8))
    ts(ap("SC", 0, 24), ap("BK3", 0, 24), -4096.0, A.mult)
    iota(ap("O5I", 0, 8), [[5, 8]], 4, 0)
    cp(ap("O5", 0, 8), ap("O5I", 0, 8))
    iota(ap("MKI", 0, 128), [[0, 8], [-1, 16]], 16, 1)
    ts(ap("MKJ", 0, 128), ap("MKI", 0, 128), 15, A.bitwise_and)
    ts(ap("MK", 0, 128), ap("MKJ", 0, 128), 0.0, A.is_equal)
    ts(ap("NMK", 0, 16), ap("MK", 0, 16), -1.0, A.mult, 1.0, A.add)
    cp(ap("PM", 0, 1), ap("MKJ", 0, 1))
    iota(ap("DU0", 0, 16), [[16, 16]], 2048, 0)
    iota(ap("DU0", 16, 24), [[16, 8]], 128, 0)
    ts(ap("DUM", 0, 24), ap("DU0", 0, 24), ap("PM", 0, 1), A.add)
    ts(ap("LC", 0, 16), ap("ONE", 0, 16), 4096.0, A.mult)
    ts(ap("LC", 16, 24), ap("DUM", 16, 24), 128.0, A.add)
    sel(ap("SD", 0, 16), ap("SC", 0, 16), [[0, 16]], A.is_equal, 0, 0)
    act(ap("SD", 16, 24), ap("BK3", 0, 8), scale=-256.0)
    ms(ap("CK", 0, 768), 0.0)
    ms(ap("CK", 128, 384, 1, 0, 32), BIG / 32)
    ms(ap("CK", 0, 512, 1, 32, 64), 64.0)
    ms(ap("RS", 0, 384), 0.0)
    ms(ap("RS", 0, 384, 16), HUGE)
    ms(ap("D0", 0, 240), 1.0)
    ms(ap("D0", 0, 240, 5), 0.0)
    ms(ap("D1", 0, 240), 0.0)
    ms(ap("THR", 0, 48), 2 ** 25)
    ms(ap("ACT", 8, 9), -1.0 / 256)
    act(ap("D", 1792, 2048), ap("CK", 512, 768))
    for name, c0, c1, x in (("SS", 0, 1, 0), ("GP", 0, 1, 0), ("W1", 128, 256, 1), ("RW", 10240, 10496, 0), ("D", 2048, 2304, 0), ("YS", 384, 512, 0),
                            ("DH", 0, 40, 0), ("SX", 0, 256, -1), ("SX", 256, 512, -1), ("NCB", 256, 384, CC / 8), ("NCB", 384, 512, -FAR / 128), ("NIF", 0, 128, -1)):
        iota(ap(name, c0, c1), [[0, c1 - c0]], int(x), 0)
    for name, plain, sums in (("K0", 12, 8.0), ("KA", 1, 2.0)):
        iota(ap(name, 0, 8), [[0, 8]], plain, 0)
        sel(ap(name, 0, 8), ap(name, 0, 8), [[-32, 8]], A.is_ge, 0, 1, sums)
    act(ap("NIB", 0, 128), ap("IB", 0, 128), scale=-1.0)
    cp(ap("D", 0, 896), ap("NDI", 0, 896))
    cp(ap("D", 896, 1792), ap("NDI", 896, 1792))
    act(ap("RW", 4096, 6144), ap("RW", 0, 2048))
    cp(ap("RW", 8192, 10240), ap("RW", 0, 2048))
    cp(ap("R0", 0, 1), ap("RW", 0, 1))
    for c in (0, 4096, 8192):
        ms(ap("RW", c, c + 1), 300.0)
    act(ap("RSV", 0, 128), ap("RW", 2176, 2304))
    act(ap("RSV", 128, 256), ap("RW", 6272, 6400))
    mms([(ap("C", 256 + 128 * h, 384 + 128 * h), ap("XZ", 128 * h, 128 * h + 128), ap("IB", 0, 128), True, True) for h in range(2)])
    act(ap("XZ", 256, 512), ap("C", 256, 512))
    sz = send([(t, ap("XZ", 512 * t, 512 * t + 512), ap("XZ", 0, 512), "in%d" % t, SHARE[t]) for t in (1, 2, 3)], [ap("XZ", 0, 512)])
    sv = send([(t, ap("VSR", 16 * t, 16 * t + 16), ap("VSO", 16 * t, 16 * t + 16), "in%d" % t, SHARE[t]) for t in (1, 2, 3)], [ap("VSO", 0, 64)])
    for j, t in enumerate((0, 2)):
        sel(ap("SCT", 32 * j + 8, 32 * j + 24), ap("ONE", 0, 16), [[-8, 2], [-16, 8]], A.is_equal, -t, 1)
        sel(ap("SX", 256 * j, 256 * j + 256), ap("SX", 256 * j, 256 * j + 256), [[-8, 2], [-16, 8], [0, 16]], A.is_equal, -t, 1)
    for j, i in enumerate((8, 0, 10, 2)):
        for c, how in ((256 * j, A.not_equal), (256 * j + 128, A.is_equal)):
            sel(ap("DG", c, c + 128), ap("IB", 0, 128), [[0, 8], [1, 16]], how, -i, 0)
    for name, above, on in (("TRZ", -FAR, FAR), ("TRC", CC, -15 * CC)):
        iota(ap(name, 0, 128), [[0, 128]], int(above), 0)
        sel(ap(name, 0, 128), ap(name, 0, 128), [[-16, 8], [0, 16]], A.is_ge, 0, 1)
        sel(ap(name, 0, 128), ap(name, 0, 128), [[16, 8], [1, 16]], A.is_ge, 0, -1)
        if name == "TRC":
            if PBCS:
                iota(ap("MKI", 0, 128), [[1, 16], [16, 8]], 0, 0)
                cp(ap("OP", 0, 128), ap("MKI", 0, 128))
            for c in range(8, 8 + 40 * PBCS, 40):
                act(ap("PBC", 16 * c, 16 * c + 640), ind(ap("TRC", 0, 128), ap("OP", c, c + 40)))
            if PBCS < 3:
                iota(ap("PBC", 0, 128), [[0, 128]], int(CC), 0)
                sel(ap("PBC", 0, 128), ap("PBC", 0, 128), [[-16, 8], [0, 16]], A.is_ge, 0, 1)
            for i in range(1 + 5 * PBCS, 16):
                sel(ap("PBC", 128 * i, 128 * i + 128), ap("PBC", 0, 128), [[16, 8], [0, 16]], A.is_ge, i, -1)
        sel(ap(name, 0, 128), ap(name, 0, 128), [[-1, 128]], A.not_equal, 0, 1, on)
    sel(ap("NIF", 0, 128), ap("NIF", 0, 128), [[-1, 128]], A.is_equal, 0, 1)
    sel(ap("GT", 0, 128), ap("W1", 128, 256), [[1, 128]], A.is_ge, 0, -1, 1.0 / 3)
    scan(ap("WL", 0, 128), ap("GT", 0, 128), ap("W1", 128, 256), A.mult, A.mult, 1e29)
    act(ap("WL", 128, 129), ap("WL", 127, 128), scale=4.0)
    for c in (0, 256):
        cp(ap("FX", c, c + 256), ap("CK", 512, 768))
    for c in (257, 258, 401, 402):
        ts(ap("FX", c, 384 + c // 384 * 128, 32), ap("ONE", 0, 4), -64.0, A.mult)
    for j in range(2):
        nc = ap("NCB", 128 * j, 128 * j + 128, 1, 0, 32)
        iota(nc, [[1, 128]], 0, 0)
        sel(nc, nc, [[0, 128]], A.is_equal, 0, 1)
        ms(ap("NCB", 128 * j, 128 * j + 128, 1, 32, 64), (4096 + 1792 + 128 * j - FAR) / 32)


    xb = [0, 0]
    KB, CB = ("M2", "K"), ("M", "C")

    def xbank(h):
        xb[h] += 1
        return "YX"[h] + "01"[xb[h] % 2]

    sends = {}

    def arrived(kind, t):
        if t == 0:
            return {}
        if kind == "in":
            return {"waits": [("in%d" % t, 2 * (SHARE[t][1] - SHARE[t][0]))], "after": {sz: 4000.0, sv: 4000.0}}
        return {"waits": [("%s%d" % (kind, t), 8)], "after": {sends[kind, t]: 3000.0}}

    def xs(t, h):
        return ap("XZ", 512 * t + 128 * h, 512 * t + 128 * h + 128)

    def kcol(t, j=0):
        return ap("K0", j, j + 1) if t == 0 else ap("KR", 8 * t + j, 8 * t + j + 1)

    def prep(t):
        cp(ap("L2", 16 * t, 16 * t + 16), ap("VSR" if t else "VSO", 16 * t, 16 * t + 16), **arrived("in", t))

    def prep_next(t):
        if t + 1 < NV:
            prep(t + 1)

    def start_nodes(t, h):
        c = 16 * t + 8 * h
        tt(ap("AV", 128 * h, 128 * h + 128), ind(ap("VSR" if t else "VSO", c, c + 8), ap("OC", 0, 8)), ap("MK", 0, 128), A.mult, **arrived("in", t))
        mm(ap(CB[h], 200, 208), ap("AV", 128 * h, 128 * h + 128), ap("BK3", 0, 8))
        act(ap("D1", 120 * h + 80, 120 * h + 120, 5), ap(CB[h], 200, 208))

    def guards(t, h):
        o, w = 384 * h, 24 * h
        gr, lg, kind = 240 * t + 120 * h, 48 * t + w, "ga" if h == 0 else "gb"
        tt(ap("AG", 128 * h, 128 * h + 128), ind(ap("GR", gr, gr + 40), ap("O5", 0, 8)), ap("MK", 0, 128), A.mult, **arrived(kind, t))
        act(ap("GZ", w, w + 24), ap("GR", gr + 4, gr + 120, 5), F.Relu, bias=1.0, scale=-1.0, **arrived(kind, t))
        x = b = "Y0" if h == 0 else xbank(h)
        mm(ap(b, 448, 456), ap("AG", 128 * h, 128 * h + 128), ap("BKF", 0, 8))
        cp(ap("LG", lg, lg + 8), ap(b, 448, 456))
        act(ap("RG", o, o + 384), ind(ap("RW", 0, 4096), ap("LG", lg, lg + 24)), **arrived("la" if h == 0 else "lb", t))
        mms([c for k in range(3) for c in ((ap(x, 128 * k, 128 * k + 128), ap("IB", 0, 128), xs(t, h), True, False),
                                           (ap(x, 128 * k, 128 * k + 128), ap("NIB", 0, 128), ap("RG", o + 128 * k, o + 128 * k + 128), False, True))], **arrived("in", t))
        mms([(ap(b, 416 + 8 * k, 424 + 8 * k), ap("RG", o + 128 * k, o + 128 * k + 128), ap("SC", 0, 8), True, True) for k in range(3)])
        act(ap("CG", o, o + 384), ap(x, 0, 384), F.Sign, bias=0.5)
        mms([(ap(b, 384, 408), ap("RBIG", 256, 384), ap("GZ", w, w + 24), True, False)]
            + [(ap(b, 384 + 8 * k, 392 + 8 * k), ap("CG", o + 128 * k, o + 128 * k + 128), ap("BK3", 0, 8), False, k == 2) for k in range(3)])
        cnt = ap(b, 384, 408)
        ts(ap("T1", w, w + 24), cnt, kcol(t, 4), A.is_lt, NOG, A.mult, **arrived("ks", t))
        tt(ap("THR", w, w + 24), ap("T1", w, w + 24), ap(b, 416, 440), A.add)
        act(ap("D0", 120 * h + 1, 120 * h + 120, 5), ap("T1", w, w + 24), F.Sign)
        tt(ap("D1", 120 * h + 1, 120 * h + 120, 5), ap("GR", gr + 4, gr + 120, 5), ap("T1", w, w + 24), A.subtract, **arrived("ga" if h == 0 else "gb", t))

    def vlist(t, s, h):
        return ap("L2", 16 * t + 8 * h, 16 * t + 8 * h + 8) if s == 2 else ap("LV", 32 * t + 16 * h + 8 * s, 32 * t + 16 * h + 8 * s + 8)

    def cfg(t, s, h):
        return CFG[6 * t + 2 * s + h]

    def spans(t, s, h):
        n = 128 - 32 * cfg(t, s, h)[0].count("A")
        return [(0, n, "R", 2048 * h)] + [(n, 128, "RF", 1024 * h - 1024)] * (n < 128)

    def fused(t):
        return [32 * max(cfg(t, s, h)[0].count("A") for s in range(3)) for h in range(2)]

    def spread(t):
        n = fused(t)
        def copy(out, a, own, **kw):
            (cp(out, a) if own else sel(out, a, [[0, width(a)]], A.is_equal, 0, 0, **kw))
        for h in range(2):
            c = 512 * t + 128 * h + 128
            copy(ap("XQ", h * n[0], n[0] + h * n[1]), ap("XZ", c - n[h], c), t == 0 and OWN, **arrived("in", t))
        for i in range(16):
            copy(ap("XR", 2048 * t + i, 2048 * t + 16 * sum(n), 16), ap("XQ", 0, sum(n)), t == 0 and i < OWN)

    def gather(t, s, h):
        o = 128 * h
        e = ap("EU", o, o + 128)
        whole = s == 2 or (s == 0 and h == 0 and t % 2 == 0)
        if whole:
            cp(e, ind(ap("D", 0, 2048), vlist(t, s, h)))
        else:
            ts(e, ind(ap("D", 0, 2048), vlist(t, s, h)), 4096.0 * (s + 1), A.min)
        kinds, ch = cfg(t, s, h)[:2]
        for c0, c1 in CHUNKS[ch]:
            src, kind = ind(ap("RW", 0, 10240), ap("EU", o + c0 // 16, o + c1 // 16)), kinds[c0 // 512]
            if kind == "A":
                c, x = 1024 * h - 1024, 2048 * t + 16 * sum(fused(t)[:h + 1]) - 2048
                tt(ap("RF", c + c0, c + c1), src, ap("XR", x + c0, x + c1), A.subtract)
            else:
                (cp if kind == "E" else act)(ap("R", 2048 * h + c0, 2048 * h + c1), src)
        if s == 2 and JOIN:
            if h == 0:
                return
            o, e = 0, ap("EU", 0, 256)
        n = width(e)
        if s or whole:
            ts(ap("FA", o, o + n), e, 4096.0, A.is_ge)
        if s == 2:
            ts(ap("FB", o, o + n), e, 8192.0, A.is_ge)
        for k in range(s + 1):
            ts(ap("FW", 256 * k + o, 256 * k + o + n), e, -4096.0 * k - 2048.0, A.add)

    def compare(t, s, h):
        o = 128 * h
        kinds = cfg(t, s, h)[0]
        for q in range(4):
            c = 2048 * h + 512 * q
            if kinds[q] == "A":
                for c0, c1 in CHUNKS[cfg(t, s, h)[1]]:
                    if c0 == 512 * q:
                        ts(ap("CMP", c, c + c1 - c0), ap("RF", 1024 * h - 1024 + c0, 1024 * h - 1024 + c1), 0.0, A.is_le)
                continue
            x = "Y1" if t and s == 2 and h == 0 else xbank(h)
            mm(ap(x, 0, 512), ap("XZ", 512 * t + 256 + o, 512 * t + 384 + o), ap("RW", 6144 + 512 * q, 6656 + 512 * q), True, kinds[q] != "D", **arrived("in", t))
            if kinds[q] == "D":
                mm(ap(x, 0, 512), ap("NIB", 0, 128), ap("R", c, c + 512), False, True)
                act(ap("CMP", c, c + 512), ap(x, 0, 512), F.Sign, bias=0.5)
            else:
                tt(ap("CMP", c, c + 512), ap("R", c, c + 512), ap(x, 0, 512), A.is_le)

    def by_entry(t, s, h, bank, c0, c1, w):
        for p0, p1, name, base in spans(t, s, h):
            for i0 in range(0, 16, RUN):
                mms([(ap(bank, c0 + i, c1, 16, p0, p1), ap(name, base + 16 * p0 + i, base + 16 * p1, 16), w, False, False) for i in range(i0, i0 + RUN)])

    def tail(t, s, h):
        o, n, w, W = 128 * h, 128 * (s + 1), 24 * h, 8 * (s + 1)
        cut = s == 0 and h == 0 and t % 2 == 0
        K, kc = KB[h], kcol(t, cfg(t, s, h)[0].count("D"))
        C, c0 = ("Y0" if cut else CB[h]), 0
        mm(ap(K, 0, n), ap("ONE", 0, 128, 1, 0, 64), ap("CK", 0, n, 1, 0, 64), True, False)
        if s or cut:
            mm(ap(K, 0, n), ap("FA", o, o + 128), ap("RBIG", 128, 128 + n), False, False)
        if s == 2:
            mm(ap(K, 128, n), ap("FB", o, o + 128), ap("RBIG", 128, n), False, False)
        for k in range(s + 1):
            mm(ap(K, 128 * k, 128 * k + 128), ap("FW", 256 * k + o, 256 * k + o + 128), ap("IB", 0, 128), False, False)
        by_entry(t, s, h, K, 0, n, ap("SC", 0, W))
        for p0, p1 in ((0, 64), (64, 128)) if cfg(t, s, h)[3] else ((0, 128),):
            for i0 in range(0, 16, RUN):
                mms([(ap(C, c0 + i, c0 + 128, 16, p0, p1), ap("CMP", 2048 * h + 16 * p0 + i, 2048 * h + 16 * p1, 16), ap("BK3", 0, 8), True, True) for i in range(i0, i0 + RUN)])
        if cfg(t, s, h)[2]:
            act(ap("PEN", o, o + 128), ap(C, c0, c0 + 128), F.Relu, bias=kc, scale=-1.0, **arrived("ks", t))
        else:
            ts(ap("PEN", o, o + 128), ap(C, c0, c0 + 128), kc, A.is_lt, **arrived("ks", t))
        mms([(ap(K, 128 * k, 128 * k + 128), ap("RBIG", 128, 256), ap("PEN", o, o + 128), False, k == s) for k in range(s + 1)])
        scan(ap("SCN", 384 * h, 384 * h + n), ap("RS", 0, n), ap(K, 0, n), A.add, A.min)
        if s == 0 and h == 0 and t % 2:
            tt(ap("ASK", 0, 8), ap("SCN", 15, 128, 16), ap("THA", 8, 16), A.is_ge)
        mi, lo = ap("MI", w, w + W), ap("LO", w, w + W)
        tt(mi, ap("SCN", 384 * h + 15, 384 * h + n, 16), ap("THR", w, w + W), A.min)
        ts(lo, mi, 4095, A.bitwise_and)
        c = 120 * h + 4 - s
        cp(ap("D1", c, 120 * h + 40 * (s + 1), 5), lo)
        if s:
            ts(ap("D0", c, 120 * h + 40 * (s + 1), 5), lo, 0.0, A.is_equal)
        else:
            act(ap("D0", c, 120 * h + 40, 5), ap("D1", c, 120 * h + 40, 5), F.Relu, bias=1.0, scale=-1.0)
        if s:
            v = 80 * (1 - h) + 40 * (2 - s)
            scan(ap("VS", v, v + 40), ap("D0", 120 * h + 40 * s, 120 * h + 40 * s + 40), ap("D1", 120 * h + 40 * s, 120 * h + 40 * s + 40), A.mult, A.max)
            tt(ap("AX", o, o + 128), ind(ap("VS", v, v + 40), ap("O5", 0, 8)), ap("MK", 0, 128), A.mult)
            mm(ap(C, 192, 200), ap("AX", o, o + 128), ap("BK3", 0, 8))
            cp(vlist(t, s - 1, h), ap(C, 192, 200))
            if s == 1 and t + 1 < NV:
                kind, lv, lg = "la" if h == 0 else "lb", ap("LV", 32 * t + 16 * h, 32 * t + 16 * h + 16), 48 * (t + 1) + w + 8
                sends[kind, t + 1] = send([(1, ap("LG", lg, lg + 16), lv, "%s%d" % (kind, t + 1), 0)], [lv])
            tt(ap("THR", w, w + W - 8), ap("MI", w, w + W - 8), ap("LO", w, w + W - 8), A.subtract)
            if s == 2:
                act(ap("D1", 120 * h + 40, 120 * h + 80, 5), ap("VS", v + 4, v + 40, 5))

    def final_guards(t, h):
        act(ap("D1", 120 * h + 40, 120 * h + 120, 5), ap("D0", 120 * h + 40, 120 * h + 120, 5))
        scan(ap("GF", 240 * t + 120 * h, 240 * t + 120 * h + 120), ap("D0", 120 * h, 120 * h + 120), ap("D1", 120 * h, 120 * h + 120), A.mult, A.max)
        if t + 1 < NV:
            c, kind = 240 * t + 120 * h, "ga" if h == 0 else "gb"
            gf = ap("GF", c, c + 120)
            sends[kind, t + 1] = send([(1, ap("GR", c + 240, c + 360), gf, "%s%d" % (kind, t + 1), 0)], [gf])

    v2, v1, v0 = ap("D1", 80, 120, 5), ap("D1", 40, 80, 5), ap("VS", 124, 160, 5)
    av = ap("VS", 164, 200, 5)
    ea, eb, fr = ap("E2", 0, 128), ap("EB", 0, 128), ap("FR", 0, 128)

    def early3(t):
        act(ap("DH", 1, 40, 5), v2, scale=-1.0)
        tt(ap("DH", 2, 40, 5), v2, v1, A.subtract)
        act(ap("DH", 3, 40, 5), v1)
        act(eb, ind(ap("D", 0, 2048), vlist(t, 0, 0)))
        if t % 2 == 0:
            act(ap("RB", 0, 128), ind(ap("RW", 0, 2048), vlist(t, 0, 0)))
            for j in range(2):
                d = 256 * t + 256 * j
                mms([(ap("M", 128 + 128 * j, 256 + 128 * j), ap("DG", d, d + 128), ap("RB", 0, 128), True, False),
                     (ap("M", 128 + 128 * j, 256 + 128 * j), ap("DG", d + 128, d + 256), xs(t, 0), False, True)], **arrived("in", t))
            act(ap("HB", 0, 256), ap("M", 128, 384))
            act(ap("HB", 256, 384), ap("RW", 1792 + 64 * t, 1920 + 64 * t))

    def source(t):
        k = 1 - t % 2
        scan(ap("VS", 160, 200), ap("D0", 40 * k, 40 * k + 40), ap("DH", 0, 40), A.mult, A.add)
        tt(ap("AL", 0, 128), ind(ap("VS", 160, 200), ap("O5", 0, 8)), ap("MK", 0, 128), A.mult)
        mm(ap("M", 80, 88), ap("AL", 0, 128), ap("BK3", 0, 8))
        cp(ap("LA", 0, 8), ap("M", 80, 88))
        act(ea, ind(ap("D", 0, 2048), ap("LA", 0, 8)))
        tt(ap("NQ", 0, 8), av, v0, A.not_equal)
        tt(ap("Q8", 0, 8), ap("NQ", 0, 8), av, A.min)
        act(fr, ea if k else eb, F.Relu, bias=1.0, scale=-1.0)
        mm(ap("M", 32, 40), fr, ap("BK3", 0, 8))
        tt(ap("ASK", 8 - 8 * k, 16 - 8 * k), ap("Q8", 0, 8), ap("M", 32, 40), A.min)
        if k:
            mm(ap("M", 384, 512), ap("ONE", 0, 128, 1, 0, 64), ap("NCB", 64 * t, 64 * t + 128, 1, 0, 64), True, False)
            mm(ap("M", 384, 512), ap("TRZ", 0, 128), fr, False, True)
            tt(ap("E2", 128, 256), ea, ap("M", 384, 512), A.max)
        else:
            act(ap("THA", 0, 8), ap("ASK", 8, 16), bias=HUGE, scale=-HUGE)
            tt(ap("THA", 8, 16), ap("THA", 0, 8), ap("THR", 0, 8), A.add)

    def meet(t):
        ba = ap("VS", 124, 200, 5)
        ts(ap("FX", 0, 256, 16), ba, -1024.0, A.add)
        act(ap("SQ", 0, 16), ba, F.Square, bias=-128.0, scale=0.125)
        cp(ap("FX", 1, 256, 16), ap("SQ", 0, 16))
        tt(ap("FX", 2, 256, 16), ap("SQ", 0, 16), ap("FX", 1, 256, 16), A.subtract)
        for w in range(2):
            tt(ap("FX", 256 + 144 * w, 384 + 128 * w, 32), ap("FX", 16 * w, 128, 32), ap("FX", 128 + 16 * w, 256, 32), A.add)
        tt(ap("PP", 0, 8), ap("FX", 0, 128, 16), ap("FX", 128, 256, 16), A.mult)
        y = MEET[t % 2] + "1"
        for j in range(4):
            mm(ap(y, 128 * j, 128 * j + 128), ap("FX", 128 * j, 128 * j + 128), ap("IB", 0, 128))
        cp(ap("FT", 0, 512), ap(y, 0, 512))
        for b in range(4):
            y = MEET[t % 2] + "%d" % (b % 2)
            mms([(ap(y, 256 * j, 256 * j + 256), ap("FT", 256 + 128 * j, 384 + 128 * j, 1, 32 * b, 32 * b + 32), ap("FT", 0, 256, 1, 32 * b, 32 * b + 32), True, True)
                 for j in range(2)])
            for j in range(2):
                gg = 2 * b + j
                ts(ap("EQ", 256 * gg, 256 * gg + 256), ap(y, 256 * j, 256 * j + 256), ap("PP", gg, gg + 1), A.is_equal, ap("WL", 127, 128), A.mult)

    def acts(t):
        b = ACTS[t % 2]
        for g0 in range(0, 8, 2):
            mms([(ap(b, 40 + gg, 41 + gg), ap("EQ", 256 * gg + 128 * x, 256 * gg + 128 * x + 128), ap("ASK", gg, gg + 1), x == 0, x == 1)
                 for gg in (g0, g0 + 1) for x in range(2)])
        act(ap("Q8", 0, 8), ap("ASK", 0, 8), scale=ap("WL", 128, 129))
        tt(ap("ACT", 0, 8), ap("Q8", 0, 8), ap(b, 40, 48), A.is_gt)
        nl = 24 if t % 2 == 0 else 16
        tt(ap("AC", 0, 128), ind(ap("ACT", 0, 8), ap("OC", 0, 8)), ap("MK", 0, 128), A.mult)
        if t < NV - 1:
            mms([(ap(b, 72, 73), ap("ONE", 0, 128), ap("ACT", gg, gg + 1), gg == 0, gg == 8) for gg in range(9)])
        mms([(ap(b, 48, 48 + nl), ap("IB", 0, 128), ap("LC", 0, nl), True, False), (ap(b, 48, 56), ap("AL", 0, 128), ap("BK3", 0, 8), False, False),
             (ap(b, 56, 64), ap("AX", 0, 128), ap("BK3", 0, 8), False, False), (ap(b, 48, 48 + nl), ap("AC", 0, 128), ap("SD", 0, nl), False, True)])
        tt(ap("LU", 0, nl), ap("DUM", 0, nl), ap(b, 48, 48 + nl), A.min)
        if t < NV - 1:
            ts(ap("KT", 0, 1), ap(b, 72, 73), RN2, A.add, RN2, A.subtract)
            ts(ap("KT", 8, 9), ap("KT", 0, 1), ap(b, 72, 73), A.subtract, 4.5, A.subtract)
            ks = ap("KS", 8 * t, 8 * t + 8)
            act(ks, ap("KA", 0, 8), bias=16.0, scale=ap("KT", 8, 9))
            sends["ks", t + 1] = send([(1, ap("KR", 8 * t + 8, 8 * t + 16), ks, "ks%d" % (t + 1), 0)], [ks])
        cp(ap("LS", 0, nl), ap("LU", 0, nl))

    def split_rows(t):
        n = spans(t, 0, 0)[0][1]
        mm(ap("M", 128, 384), ap("ONE", 0, 128, 1, 0, 64), ap("CK", 512, 768, 1, 0, 64), True, False)
        mm(ap("M", 128, 384, 1, 0, n), ap("XZ", 512 * t, 512 * t + n), ap("SX", 128 * t, 128 * t + 256), False, False, **arrived("in", t))
        by_entry(t, 0, 0, "M", 128, 384, ap("SCT", 16 * t + 8, 16 * t + 24))
        mm(ap("M", 128, 144), ap("ONE", 0, 128, 1, 0, 64), ap("CK", 512, 528, 1, 0, 64), False, True)
        act(ap("GE", 0, 256), ap("M", 128, 384), F.Sign, bias=0.5)
        mm(ap("M", 128, 256), ap("GE", 0, 128), ap("IB", 0, 128))
        mm(ap("M", 256, 384), ap("GE", 0, 128), ap("IB", 0, 128), True, False)
        mm(ap("M", 256, 384), ap("GE", 128, 256), ap("IB", 0, 128), False, True)
        act(ap("ST", 0, 128), ap("M", 256, 384), F.Relu, bias=-1.0, scale=-1.0)
        tt(ap("YS", 256, 384), eb, ap("M", 128, 256), A.mult)
        mm(ap("M", 384, 512), ap("ONE", 0, 128), ap("NCB", 256, 384), True, False)
        mm(ap("M", 384, 512), ap("TRC", 0, 128), ap("ST", 0, 128), False, True)
        tt(ap("U", 0, 128), eb, ap("M", 384, 512), A.add)
        act(ap("U", 128, 256), ap("U", 0, 128))
        act(ap("U", 256, 512), ap("U", 0, 256))
        act(ap("W2", 0, 128), ap("YS", 256, 384), F.Relu, scale=-1.0)

    def place_rows(t):
        for b in range(4):
            y = "Y%d" % (b % 2)
            mms([(ap(y, 128 * j, 128 * j + 128), ap("PBC", 512 * b + 128 * j, 512 * b + 128 * j + 128), fr, True, True) for j in range(b == 0, 4)])
            for c0, c1 in ((128, 256), (256, 512)) if b == 0 else ((0, 512),):
                tt(ap("MM", 512 * b + c0, 512 * b + c1), ap("U", 0, c1 - c0), ap(y, c0, c1), A.max)
            if b == 3:
                tt(ap("W6", 0, 128), ap("U", 0, 128), ap(y, 384, 512), A.is_ge)
            for j in range(4):
                c, i = 512 * b + 128 * j, 4 * b + j + 129
                mm(ap("M", i, i + 113, 16), ap("MM" if c else "U", c, c + 128), ap("BKF", 0, 8))
        act(ap("SS", 1, 129), ap("M", 129, 257))
        tt(ap("GD", 0, 128), ap("SS", 0, 128), ap("M", 129, 257), A.subtract)
        ts(ap("GT", 0, 128), ap("GD", 0, 128), RND, A.add, RND, A.subtract)
        mm(ap("M", 384, 512), ap("GD", 0, 128), ap("IF", 0, 128), True, False)
        mm(ap("M", 384, 512), ap("GT", 0, 128), ap("NIF", 0, 128), False, True)
        act(ap("W1", 0, 128), ap("M", 384, 512), scale=ap("NMK", 0, 1))

    def move_down(t):
        scan(ap("GP", 1, 41), ap("D0", 0, 40), ap("D1", 0, 40), A.mult, A.max)
        act(ap("AA", 0, 128), ind(ap("GP", 0, 41), ap("O5", 0, 8)))
        mm(ap("M", 256, 384), ap("AA", 0, 128), ap("IF", 0, 128))
        tt(ap("W1", 0, 128), ea, ap("M", 256, 384), A.not_equal)
        mm(ap("M", 384, 512), ap("AA", 0, 128), ap("IF", 0, 128), True, False)
        mm(ap("M", 384, 512), ap("ONE", 0, 128), ap("NCB", 384, 512), False, False)
        mm(ap("M", 384, 512), ap("TRZ", 0, 128), fr, False, True)
        tt(ap("E2", 128, 256), eb, ap("M", 384, 512), A.max)

    def write_back(t):
        if t % 2:
            tt(ind(ap("D", 0, 2304), ap("LS", 0, 16)), ap("E2", 0, 256), ap("W1", 0, 256), A.mult)
            return
        n0, ln = 1792 + 64 * t, ap("LS", 16, 24)
        tt(ind(ap("D", 0, 2304), ap("LS", 8, 16)), ap("W2", 0, 128), ap("W6", 0, 128), A.mult)
        act(ap("D", n0, n0 + 128), ind(ap("YS", 256, 512), ln), F.Relu)
        for c in (0, 4096, 8192):
            cp(ind(ap("RW", c, c + 2304), ap("LS", 8, 16)), ap("HB", 0, 128))
            if c < 8192:
                act(ap("RW", c + n0, c + n0 + 128), ind(ap("HB", 128, 384), ln))
                r = 128 * (c // 4096)
                act(ap("RW", c + 2176, c + 2304), ap("RSV", r, r + 128))
        tt(ind(ap("D", 0, 2304), ap("LS", 0, 8)), ap("W1", 0, 128), ap("E2", 128, 256), A.add)

    prep(0)
    spread(0)
    for t in range(NV):
        if t % 2:
            act(ap("D0", 4, 40, 5), ap("ONE", 0, 8))
        if t + 1 < NV:
            spread(t + 1)
        steps = [(start_nodes, 0), (start_nodes, 1), (guards, 0), (gather, 2, 0), (compare, 2, 0), (gather, 2, 1), (compare, 2, 1), (tail, 2, 0), (guards, 1),
                 (gather, 1, 0), (compare, 1, 0), (tail, 2, 1), (gather, 1, 1), (compare, 1, 1), (prep_next,), (tail, 1, 0), (tail, 1, 1),
                 (gather, 0, 1), (gather, 0, 0), (early3,), (source,)]
        late = [(compare, 0, 1)]
        if t % 2:
            steps += late * ORDER[1] + [(move_down,), (compare, 0, 0), (meet,)] + late * (1 - ORDER[1]) + [(tail, 0, 0), (acts,), (final_guards, 0)]
        else:
            steps += late * ORDER[0] + [(split_rows,), (compare, 0, 0), (meet,), (acts,)] + late * (1 - ORDER[0]) + [(tail, 0, 0), (final_guards, 0), (place_rows,)]
        steps += [(tail, 0, 1), (final_guards, 1), (write_back,)]
        for s_ in steps:
            stage[0] += 1
            stage[1] = s_[-1] if len(s_) > 1 else 0
            if t or s_[0] is not guards:
                s_[0](t, *s_[1:])
        if t == 2:
            act(ap("R0", 1, 16), ap("RW", 4097, 4112))
            store("y", T.yr[:, 0:16], ap("R0", 0, 16), 2000.0)
            store("y", T.yr[:, 16:2048], ap("RW", 4112, 6144), 4000.0)
    store("y", T.yn[:, 0:1024], ap("D", 0, 1024), 4000.0)
    store("s", T.yn[:, 1024:2048], ap("D", 1024, 2048), 4000.0)
    for h in range(2):
        for k in range(3):
            (cp if k else act)(ap("T1", 24 * h + k, 24 * h + 24, 3), ap("GF", 724 + 120 * h + 40 * k, 760 + 120 * h + 40 * k, 5))
        mm(ap(KB[h], 0, 128, 1, 0, 24), ap("T1", 24 * h, 24 * h + 24), ap("IF", 0, 128))
        act(ap("YG", 128 * h, 128 * h + 128, 1, 0, 24), ap(KB[h], 0, 128, 1, 0, 24))
    store("y", T.yg[:, :], ap("YG", 0, 256, 1, 0, 24), 2000.0)

    n = len(ops)
    succ = [[] for _ in range(n)]
    edge = [{} for _ in range(n)]
    for k, o in enumerate(ops):
        for j, wt in o["dep"].items():
            edge[k][j] = ops[j]["lat"] + (LAT if wt else 0.0)
        for j, l in o["soft"].items():
            edge[k][j] = max(edge[k].get(j, 0.0), l)
        for j in edge[k]:
            succ[j].append(k)
    level = [0.0] * n
    for k in range(n - 1, -1, -1):
        level[k] = ops[k]["cost"] + max([ops[k]["lat"]] + [edge[j][k] + level[j] for j in succ[k]])
    cost = [o["cost"] for o in ops]
    engs = [o["eng"] for o in ops]
    tails = [o["lat"] for o in ops]
    fwd = [list(edge[k].items()) for k in range(n)]
    bwd = [[(j, edge[j][k]) for j in succ[k]] for k in range(n)]

    def place(seq, pre, first):
        busy = {e: ([], []) for e in "vspgy"}
        at = [0.0] * n
        for k in seq:
            t0 = first[k]
            for j, l in pre[k]:
                if at[j] + cost[j] + l > t0:
                    t0 = at[j] + cost[j] + l
            st, en = busy[engs[k]]
            lo, hi = 0, len(en)
            while lo < hi:
                mid = (lo + hi) // 2
                if en[mid] <= t0:
                    lo = mid + 1
                else:
                    hi = mid
            while lo < len(st) and st[lo] < t0 + cost[k]:
                t0 = max(t0, en[lo])
                lo += 1
            st.insert(lo, t0)
            en.insert(lo, t0 + cost[k])
            at[k] = t0
        return at

    def replay(seq, cs, pre):
        free = {e: 0.0 for e in "vspgy"}
        done = [0.0] * n
        for k in seq:
            t0 = free[engs[k]]
            for j, l in pre[k]:
                if done[j] + l > t0:
                    t0 = done[j] + l
            done[k] = free[engs[k]] = t0 + cs[k]
        return max(done[k] + tails[k] for k in range(n))

    if "order" not in PLAN:
        others = []
        for ga, sc, f, lat, far in OTHERS:
            cs = [(o["cost"] + o["ng"] * (ga - GATH) + o["ns"] * (sc - SCAT)) * (f if o["eng"] in "vsp" else 1.0) for o in ops]
            pre = [[(j, l * far if j in ops[k]["soft"] else l + (lat - LAT if ops[k]["dep"].get(j) else 0.0)) for j, l in fwd[k]] for k in range(n)]
            others.append((cs, pre))
        rng = np.random.default_rng(1)
        zero = [0.0] * n
        best = None
        stages = np.array([o["stage"] for o in ops])
        for rnd in range(ROUNDS):
            if rnd < len(LEADS):
                key = [-level[k] - LEADS[rnd] * ops[k]["half"] for k in range(n)]
            else:
                base = np.array(best[1])
                mid = rng.uniform(0.0, best[0])
                near = np.abs(base - mid) < rng.uniform(1000.0, WINDOW)
                st_ = rng.normal(0.0, SHAKE * rng.choice([0.0, 3.0, 10.0]), stage[0] + 1)
                key = (base + near * (rng.normal(0.0, SHAKE, n) + st_[stages])).tolist()
            for k in range(n):
                for j, l in fwd[k]:
                    if key[j] + 0.001 > key[k]:
                        key[k] = key[j] + 0.001
            seq = sorted(range(n), key=lambda k: key[k])
            for it in range(PASSES):
                at = place(seq, fwd, zero)
                end = max(at[k] + cost[k] + tails[k] for k in range(n))
                if best is None or end <= best[0] + 1500.0:
                    sq_ = sorted(range(n), key=lambda k: (at[k], k))
                    each = [replay(sq_, c_, p_) for c_, p_ in others]
                    worth = end + sum(each)
                    if best is None or worth <= best[2]:
                        best = (end, at, worth, each)
                if it == PASSES - 1:
                    break
                back = place(sorted(range(n), key=lambda k: (-at[k] - cost[k], -k)), bwd, tails)
                seq = sorted(range(n), key=lambda k: (-back[k] - cost[k], k))
        seq = sorted(range(n), key=lambda k: (best[1][k], k))
        sets = [(cost, fwd)] + [others[i] for i in KEEP]
        sets = [(cs, pre, [[(j, dict(pre[j])[k]) for j in succ[k]] for k in range(n)]) for cs, pre in sets]
        qn = ["vspgy".index(e) for e in engs]
        above = [set(edge[k]) for k in range(n)]

        def ways(seq, a, b, old, cs, pre, post):
            done, rest = list(old[1]), list(old[2])
            free, calm = [0.0] * 5, b - a + CALM
            for k in seq[max(a - CALM, 0):a]:
                free[qn[k]] = done[k]
            for k in seq[a:]:
                t0 = free[qn[k]]
                for j, l in pre[k]:
                    if done[j] + l > t0:
                        t0 = done[j] + l
                t0 += cs[k]
                free[qn[k]] = t0
                if t0 != done[k]:
                    done[k] = t0
                    if calm < CALM:
                        calm = CALM
                calm -= 1
                if calm < 0:
                    break
            free, calm = [0.0] * 5, b - a + CALM
            for k in seq[b + CALM:b:-1]:
                free[qn[k]] = rest[k]
            for k in seq[b::-1]:
                t0 = free[qn[k]]
                if tails[k] > t0:
                    t0 = tails[k]
                for j, l in post[k]:
                    if rest[j] + l > t0:
                        t0 = rest[j] + l
                t0 += cs[k]
                free[qn[k]] = t0
                if t0 != rest[k]:
                    rest[k] = t0
                    if calm < CALM:
                        calm = CALM
                calm -= 1
                if calm < 0:
                    break
            return max(rest), done, rest

        st = [ways(seq, 0, n - 1, (0, zero, zero), *m) for m in sets]
        cur = sum(x[0] for x in st)
        top = (cur, seq)
        for rnd in range(MOVES):
            heat = max(HEAT * (1.0 - rnd / MOVES), 1.0) * len(sets)
            dice = rng.random(5 * TRIES + 1).tolist()
            mi = int(dice.pop() * len(sets))
            if rnd % FRESH == 0:
                if rnd % (8 * FRESH) == 0:
                    seq = sorted(seq, key=lambda k: st[0][1][k] - cost[k])
                    st = [ways(seq, 0, n - 1, x, *m) for x, m in zip(st, sets)]
                    cur = sum(x[0] for x in st)
                    if cur < top[0]:
                        top = (cur, seq)
                (end, done, rest), cs = st[mi], sets[mi][0]
                pos, last, held = [0] * n, [-1] * 5, []
                for i, k in enumerate(seq):
                    pos[k] = i
                    j = last[qn[k]]
                    if done[k] + rest[k] - cs[k] > end - 1.0 and j >= 0 and done[j] + cs[k] > done[k] - 0.5 and j not in above[k]:
                        held.append((j, k))
                    last[qn[k]] = k
            while dice and held:
                u, v = held[int(dice.pop() * len(held))]
                e, m, back_, lim = qn[v], int(dice.pop() * REACH), dice.pop() < 0.5, cur - heat * math.log(dice.pop() + 1e-12)
                a, b = pos[u], pos[v]
                dice.pop()
                if a > b:
                    continue
                if back_:
                    while m and a > 0:
                        a -= 1
                        m -= qn[seq[a]] == e
                    w, go = seq[a:b + 1], {v}
                    for k in reversed(w):
                        if k in go:
                            go.update(above[k])
                    if u in go:
                        continue
                    w = [k for k in w if k in go] + [k for k in w if k not in go]
                else:
                    while m and b < n - 1:
                        b += 1
                        m -= qn[seq[b]] == e
                    w, go = seq[a:b + 1], {u}
                    for k in w:
                        if not go.isdisjoint(above[k]):
                            go.add(k)
                    if v in go:
                        continue
                    w = [k for k in w if k not in go] + [k for k in w if k in go]
                bef, aft = [-1] * 5, [-1] * 5
                for k in seq[max(a - 100, 0):a]:
                    bef[qn[k]] = k
                for k in reversed(seq[b + 1:b + 100]):
                    aft[qn[k]] = k
                tot = 0.0
                for (c1, dn, rs), (c_, pre, post) in zip(st, sets):
                    free = [dn[k] if k >= 0 else 0.0 for k in bef]
                    d2, far, old = {}, 0.0, 0.0
                    for k in w:
                        x = free[qn[k]]
                        for j, l in pre[k]:
                            y = (d2[j] if j in d2 else dn[j]) + l
                            if y > x:
                                x = y
                        x += c_[k]
                        d2[k] = free[qn[k]] = x
                        y = tails[k]
                        for j, l in post[k]:
                            if pos[j] > b and rs[j] + l > y:
                                y = rs[j] + l
                        if x + y > far:
                            far = x + y
                        if dn[k] + rs[k] - c_[k] > old:
                            old = dn[k] + rs[k] - c_[k]
                    for x, k in zip(free, aft):
                        if k >= 0 and x + rs[k] > far:
                            far = x + rs[k]
                    tot += far if far > c1 or old > c1 - 1.0 else c1
                if tot <= lim:
                    new = seq[:a] + w + seq[b + 1:]
                    s2 = [ways(new, a, b, x, *m_) for x, m_ in zip(st, sets)]
                    if sum(x[0] for x in s2) <= lim:
                        seq, st, cur = new, s2, sum(x[0] for x in s2)
                        for i, k in enumerate(w):
                            pos[k] = a + i
                        break
        end, done, rest = ways(top[1], 0, n - 1, (0, zero, zero), *sets[0])
        PLAN["order"], PLAN["at"], PLAN["fin"] = top[1], [done[k] - cost[k] for k in range(n)], end
        PLAN["each"] = [replay(top[1], c_, p_) for c_, p_ in others]
    order, fin = PLAN["order"], PLAN["fin"]
    for k in range(n):
        ops[k]["at"] = PLAN["at"][k]

    pos = {k: i for i, k in enumerate(order)}
    seen = {}
    need = [[] for _ in range(n)]
    marked = set()
    for k in order:
        e = ops[k]["eng"]
        best = {}
        for j, wt in ops[k]["dep"].items():
            if not wt:
                continue
            key = ops[j]["sem"] or "q" + ops[j]["eng"]
            marked.add(j)
            if key not in best or pos[j] > pos[best[key]]:
                best[key] = j
        for key, j in best.items():
            if seen.get((e, key), -1) < pos[j]:
                seen[(e, key)] = pos[j]
                need[k].append((key, j))
                marked.add(j)
    count = {"qv": 0, "qs": 0, "qp": 0, "qg": 0}
    val = {}
    queue = {"v": g.vector, "s": g.scalar, "p": g.tensor, "g": g, "y": g.sync}
    got = set()
    for k in order:
        o = ops[k]
        q = queue[o["eng"]]
        for key, j in need[k]:
            q.wait_ge(T.sem[key], val[j])
        for key, c in o["waits"]:
            if (o["eng"], key) not in got:
                got.add((o["eng"], key))
                q.wait_ge(T.sem[key], c)
        ins = o["fn"]()
        if o["sem"]:
            ins.then_inc(T.sem[o["sem"]], 16)
            val[k] = 16
        elif k in marked:
            count["q" + o["eng"]] += 1
            val[k] = count["q" + o["eng"]]
            ins.then_inc(T.sem["q" + o["eng"]], 1)
    g.wait_ge(T.sem["sent"], sent[0])
    for s in outs_:
        g.wait_ge(T.sem[s], 16)
    return {"ops": ops, "order": order, "fin": fin, "level": level, "edge": edge, "succ": succ}
